import numpy as np
import ml_dtypes


def mxq(x, axis, fmt="e4m3"):
    dtype, down = {"e4m3": (ml_dtypes.float8_e4m3fn, 7), "e5m2": (ml_dtypes.float8_e5m2, 14)}[fmt]
    v = np.moveaxis(np.asarray(x, np.float32).astype(ml_dtypes.bfloat16).astype(np.float64), axis, -1)
    blocks = v.reshape(v.shape[:-1] + (-1, 32))
    amax = np.abs(blocks).max(-1, keepdims=True)
    byte = np.maximum(np.where(amax > 0, np.frexp(amax)[1] - 1 + 127, 0) - down, 1)
    scale = np.exp2(byte - 127.0)
    codes = (blocks / scale).astype(np.float32).astype(dtype).astype(np.float64)
    return np.moveaxis((codes * scale).reshape(v.shape), -1, axis)


WIDE = False


def mx_kscale(k):
    if not WIDE:
        return np.ones(k)
    levels = np.array([10, -10, 5, -5, 0])
    if k % 512:
        return np.exp2(np.random.permutation(np.resize(levels, k // 32))).repeat(32)
    a = np.empty((k // 512, 16))
    for p in range(k // 512):
        a[p, :8] = np.random.permutation(np.resize(levels, 8))
        for g in range(8):
            far = levels[np.abs(levels - a[p, g]) >= 10]
            a[p, g + 8] = far[np.random.randint(len(far))]
    return np.exp2(a.ravel()).repeat(32)


def f64(x):
    return np.asarray(x).astype(np.float64)


def striped(idx):
    return np.tile(idx.reshape(-1, 16).T, (8, 1)).astype(np.uint16)


def unstriped(offs):
    return offs[:16].T.reshape(-1).astype(np.int64)


def pack_weight(w):
    k, n = w.shape
    w = f64(np.asarray(w, np.float32).astype(ml_dtypes.bfloat16)).reshape(k // 32, 32, n)
    amax = np.abs(w).max(1)
    byte = np.clip(np.where(amax > 0, np.frexp(amax)[1] - 1 + 127 - 7, 1), 1, 254)
    scaled = (w * np.exp2(127.0 - byte)[:, None, :]).reshape(k, n).astype(np.float32)
    words = np.ascontiguousarray(scaled.reshape(k // 512, 128, 4, n).transpose(0, 1, 3, 2)).astype(ml_dtypes.float8_e4m3fn).view(np.uint8)
    return words, np.ascontiguousarray(byte.astype(np.uint8).reshape(k // 512, 16, n))


def unpack_weight(words, scales):
    g, p, n, _ = words.shape
    vals = np.ascontiguousarray(words).view(ml_dtypes.float8_e4m3fn).astype(np.float64) * np.repeat(np.exp2(scales.astype(np.float64) - 127.0), 8, axis=1)[..., None]
    return vals.transpose(0, 1, 3, 2).reshape(g * 512, n)


E2M1 = np.array([0.0, 0.5, 1.0, 1.5, 2.0, 3.0, 4.0, 6.0, -0.0, -0.5, -1.0, -1.5, -2.0, -3.0, -4.0, -6.0])


def pack_fp4(w):
    k, n = w.shape
    w = f64(np.asarray(w, np.float32).astype(ml_dtypes.bfloat16)).reshape(k // 32, 32, n)
    amax = np.abs(w).max(1)
    mant, ex = np.frexp(amax / 6.0)
    byte = np.clip(np.where(amax > 0, np.where(mant > 0.5, ex, ex - 1) + 127, 1), 1, 254)
    scaled = (w * np.exp2(127.0 - byte)[:, None, :]).reshape(k, n).astype(np.float32)
    c = np.ascontiguousarray(scaled.reshape(k // 512, 128, 4, n).transpose(0, 1, 3, 2)).astype(ml_dtypes.float4_e2m1fn).view(np.uint8) & 0xF
    words = (c[..., 0::2] | (c[..., 1::2] << 4)).reshape(k // 512, 128, 2 * n)
    return np.ascontiguousarray(words), np.ascontiguousarray(byte.astype(np.uint8).reshape(k // 512, 16, n))


def unpack_fp4(words, scales):
    g, _, n = scales.shape
    words = np.ascontiguousarray(words).reshape(g, 128, n, 2)
    nib = np.empty((g, 128, n, 4), np.uint8)
    nib[..., 0::2] = words & 0xF
    nib[..., 1::2] = words >> 4
    vals = E2M1[nib] * np.repeat(np.exp2(scales.astype(np.float64) - 127.0), 8, axis=1)[..., None]
    return vals.transpose(0, 1, 3, 2).reshape(g * 512, n)


def relu(v):
    return np.maximum(v, 0.0)


K, T, S, V, H, N = 1024, 2048, 1024, 512, 512, 128


def setup_inputs():
    n = np.random.standard_normal
    s = mx_kscale(K)[:, None]
    u = mx_kscale(H)
    packed_xT = pack_weight(n((K, T)) * s)
    packed_w3 = pack_fp4(n((H, N)) / np.sqrt(H) / u[:, None])
    return {
        "x_words": packed_xT[0],
        "x_scales": packed_xT[1],
        "w1": (n((K, H)) / np.sqrt(2 * K) / s * u).astype(np.float32),
        "w2": (n((K, H)) / np.sqrt(2 * K) / s * u).astype(np.float32),
        "w3_words": packed_w3[0],
        "w3_scales": packed_w3[1],
        "offs": striped(np.random.permutation(T)[:S]),
        "cen": striped(np.random.permutation(S)[:V]),
        "pos1": striped(np.random.permutation(S)[:V]),
        "pos2": striped(np.random.permutation(S)[:V]),
    }


def reference(x_words, x_scales, w1, w2, w3_words, w3_scales, offs, cen, pos1, pos2):
    xq = unpack_weight(x_words, x_scales)[:, unstriped(offs)]
    y = mxq(f64(w1), 0, "e4m3").T @ xq
    yc = y[:, unstriped(cen)]
    e = mxq(f64(w2), 0, "e4m3").T @ xq
    z = np.maximum(relu(yc + e[:, unstriped(pos1)]), relu(yc + e[:, unstriped(pos2)]))
    return unpack_fp4(w3_words, w3_scales).T @ mxq(z, 0, "e4m3")

@@ -1,0 +1,268 @@
+from contextlib import ExitStack
+
+import concourse.mybir as mybir
+from concourse.masks import make_identity
+
+K, T, S, V, H, N = 1024, 2048, 1024, 512, 512, 128
+FLOPS = 2 * (2 * K * H * S + H * N * V)
+
+F32 = mybir.dt.float32
+BF16 = mybir.dt.bfloat16
+I32 = mybir.dt.int32
+U32 = mybir.dt.uint32
+U16 = mybir.dt.uint16
+U8 = mybir.dt.uint8
+FP8X4 = mybir.dt.float8_e4m3fn_x4
+FP4X4 = mybir.dt.float4_e2m1fn_x4
+RELU = mybir.ActivationFunctionType.Relu
+MAX = mybir.AluOpType.max
+MULT = mybir.AluOpType.mult
+ADD = mybir.AluOpType.add
+SUB = mybir.AluOpType.subtract
+
+P = 128
+PASSES = 2
+TILES = 4
+BANK = 512
+
+
+def tile_picked_edgecv_relu_p_kernel(
+    tc, x_words, x_scales, w1, w2, w3_words, w3_scales, offs, cen, pos1, pos2, out
+):
+    nc = tc.nc
+    with ExitStack() as ctx:
+        keep = ctx.enter_context(tc.tile_pool(name="keep", bufs=1))
+        psum = ctx.enter_context(tc.psum_pool(name="psum", bufs=1))
+
+        def sb(shape, dtype, name, tag=None):
+            return keep.tile(shape, dtype, name=name, tag=tag or name, align_bytes=64)
+
+        def bank(b, name):
+            return psum.tile([P, BANK], F32, name=name, tag="bank%d" % b)
+
+        def load_list(src, name):
+            t = keep.tile(list(src.shape), U16, name=name)
+            nc.sync.dma_start(t[:], src)
+            return t
+
+        weights = {"y": w1, "e": w2}
+        raw = {}
+
+        def load_w(m, c0, c1):
+            width = P * (c1 - c0)
+            t = sb([P, PASSES, 4, width], F32, "raw_%s%d" % (m, c0))
+            for z in range(PASSES):
+                rows = weights[m][512 * z : 512 * (z + 1), P * c0 : P * c1]
+                nc.sync.dma_start(t[:, z], rows.rearrange("(p j) c -> p j c", j=4))
+            for c in range(c0, c1):
+                raw[m, c] = t[:, :, :, P * (c - c0) : P * (c - c0 + 1)]
+
+        x_win = {}
+
+        def load_x(z):
+            t = sb([P, T], U32, "x_window%d" % z)
+            nc.sync.dma_start(t[:].bitcast(I32), x_words[z].rearrange("p c r -> p (c r)").bitcast(I32))
+            x_win[z] = t
+
+        xs_win = sb([P, T], U8, "xs_win")
+        nc.gpsimd.memset(xs_win[:].bitcast(I32), 0)
+        for q in range(4):
+            nc.gpsimd.dma_start(
+                xs_win[32 * q : 32 * q + 8, :].bitcast(I32), x_scales[:, 4 * q : 4 * q + 4, :].bitcast(I32)
+            )
+        offs_t = load_list(offs, "offs_t")
+        load_x(0)
+        load_x(1)
+        pos1_t = load_list(pos1, "pos1_t")
+        load_w("e", 0, 1)
+        cen_t = load_list(cen, "cen_t")
+        load_w("e", 1, 2)
+        pos2_t = load_list(pos2, "pos2_t")
+        load_w("y", 0, 1)
+        load_w("y", 1, 2)
+        load_w("e", 3, 4)
+        load_w("e", 2, 3)
+        load_w("y", 2, 3)
+        load_w("y", 3, 4)
+        w3w = sb([P, 2 * N], U8, "w3w")
+        nc.sync.dma_start(w3w[:], w3_words[0])
+        w3s = sb([P, N], U8, "w3s")
+        nc.gpsimd.memset(w3s[:].bitcast(I32), 0)
+        for q in range(4):
+            nc.sync.dma_start(
+                w3s[32 * q : 32 * q + 4, :].bitcast(I32), w3_scales[0, 4 * q : 4 * q + 4, :].bitcast(I32)
+            )
+        ident0 = sb([P, P], F32, "ident0")
+        make_identity(nc, ident0[:])
+        ident = sb([P, P], F32, "ident")
+        nc.scalar.activation(ident[:], ident0[:], RELU)
+
+        xg0 = sb([P, S], U32, "xg0")
+        xsg = sb([P, S], U8, "xsg")
+        xg1 = {}
+
+        def gather_x1(cuts, tag=None):
+            s0 = cuts[0]
+            xg1[s0] = sb([P, cuts[-1] - s0], U32, "xg1_%d" % s0, tag)
+            for a, b in zip(cuts, cuts[1:]):
+                nc.vector.tensor_copy(xg1[s0][:, a - s0 : b - s0], x_win[1][:].indirect(offs_t[:, a // 16 : b // 16]))
+
+        def x1_cols(s0, s1):
+            b = max(k for k in xg1 if k <= s0)
+            return xg1[b][:, s0 - b : s1 - b]
+
+        codes, planes, rows = {}, {}, {}
+
+        def quantise_w(m, c, eng="scalar", tag=None):
+            g = sb([P, PASSES, P, 4], BF16, "wb_%s%d" % (m, c), tag)
+            if eng == "gpsimd":
+                for z in range(PASSES):
+                    nc.gpsimd.tensor_scalar(
+                        g[:, z].rearrange("p (g i) j -> p g j i", i=4),
+                        raw[m, c][:, z].rearrange("p j (g i) -> p g j i", i=4),
+                        1.0, 0.0, MULT, ADD,
+                    )
+            else:
+                (nc.scalar.copy if eng == "scalar" else nc.vector.tensor_copy)(
+                    g[:].rearrange("p z (g i) j -> p z g j i", i=4),
+                    raw[m, c].rearrange("p z j (g i) -> p z g j i", i=4),
+                )
+            codes[m, c] = sb([P, PASSES * P], U32, "wq_%s%d" % (m, c))
+            planes[m, c] = sb([P, PASSES * P], U8, "ws_%s%d" % (m, c))
+            nc.vector.quantize_mx(
+                out=codes[m, c][:].bitcast(FP8X4),
+                scales=planes[m, c][:],
+                in_=g[:].rearrange("p z c j -> p (z c j)"),
+            )
+
+        def product(m, c, banks, tag=None, cuts=(0, 512, 1024)):
+            rows[m, c] = sb([P, S], F32, "rows_%s%d" % (m, c), tag)
+            for h in range(len(cuts) - 1):
+                acc = bank(banks[h], "acc_%s%d%d" % (m, c, h))
+                s0, s1 = cuts[h], cuts[h + 1]
+                for z in range(PASSES):
+                    nc.tensor.matmul_mx(
+                        out=acc[:, : s1 - s0],
+                        lhsT=codes[m, c][:, P * z : P * (z + 1)].bitcast(FP8X4),
+                        lhsT_scale=planes[m, c][:, P * z : P * (z + 1)],
+                        rhs=(x1_cols(s0, s1) if z else xg0[:, s0:s1]).bitcast(FP8X4),
+                        rhs_scale=xsg[4 * z : P, s0:s1],
+                        start=(z == 0),
+                        stop=(z == PASSES - 1),
+                    )
+                nc.scalar.copy(rows[m, c][:, s0:s1], acc[:, : s1 - s0])
+
+        zt = sb([P, TILES, H], BF16, "zt")
+        got = {}
+
+        def gather(k, c, b0=0, b1=4, tag=None):
+            m, lst = {"1": ("e", pos1_t), "2": ("e", pos2_t), "c": ("y", cen_t)}[k]
+            g = sb([P, P * (b1 - b0)], F32, "g%s_%d%d" % (k, c, b0), tag)
+            nc.vector.tensor_copy(g[:], rows[m, c][:].indirect(lst[:, 8 * b0 : 8 * b1]))
+            for b in range(b0, b1):
+                got[k, c, b] = (g, b0)
+
+        def part(k, c, b0, b1):
+            g, base = got[k, c, b0]
+            return g[:, P * (b0 - base) : P * (b1 - base)]
+
+        def largest(c, b0=0, b1=4, tag=None):
+            gm = sb([P, P * (b1 - b0)], F32, "gm_%d%d" % (c, b0), tag)
+            nc.vector.tensor_tensor(gm[:], part("1", c, b0, b1), part("2", c, b0, b1), MAX)
+            for b in range(b0, b1):
+                got["m", c, b] = (gm, b0)
+
+        def edges(c, b, b0=0, b1=4):
+            n = P * (b1 - b0)
+            acc = bank(b, "zsum%d%d" % (c, b0))
+            for i in range(b0, b1):
+                cols = slice(P * (i - b0), P * (i - b0 + 1))
+                nc.tensor.matmul(acc[:, cols], part("m", c, i, i + 1), ident[:], start=True, stop=False, is_transpose=True)
+                nc.tensor.matmul(acc[:, cols], part("c", c, i, i + 1), ident[:], start=False, stop=True, is_transpose=True)
+            nc.scalar.activation(
+                zt[:, b0:b1, P * c : P * (c + 1)], acc[:, :n].rearrange("v (b i) -> v b i", i=P), RELU
+            )
+
+        zb = {}
+
+        def turn(b0, b1, b_turn, eng="scalar"):
+            n = P * (b1 - b0)
+            turned = bank(b_turn, "turned%d" % b0)
+            for i in range(b1 - b0):
+                words = zt[:, b0 + i, :].bitcast(F32)
+                for u in range(2):
+                    nc.tensor.transpose(turned[:, n * u + P * i : n * u + P * (i + 1)], words[:, u::2], ident[:])
+            zb[b0] = sb([P, n, 4], BF16, "zb%d" % b0)
+            (nc.scalar.copy if eng == "scalar" else nc.vector.tensor_copy)(
+                zb[b0][:].bitcast(F32), turned[:, : 2 * n].rearrange("p (u v) -> p v u", u=2)
+            )
+
+        def project(b0, b1, b_out, eng="scalar"):
+            n = P * (b1 - b0)
+            zq = sb([P, n], U32, "zq%d" % b0)
+            zs = sb([P, n], U8, "zs%d" % b0)
+            nc.vector.quantize_mx(out=zq[:].bitcast(FP8X4), scales=zs[:], in_=zb[b0][:].rearrange("p v j -> p (v j)"))
+            acc = bank(b_out, "res%d" % b0)
+            nc.tensor.matmul_mx(
+                out=acc[:, :n],
+                lhsT=w3w[:].bitcast(FP4X4),
+                lhsT_scale=w3s[:],
+                rhs=zq[:].bitcast(FP8X4),
+                rhs_scale=zs[:],
+                start=True,
+                stop=True,
+            )
+            res = sb([P, n], F32, "res_sb%d" % b0)
+            (nc.scalar.copy if eng == "scalar" else nc.vector.tensor_copy)(res[:], acc[:, :n])
+            nc.sync.dma_start(out[:, P * b0 : P * b1], res[:])
+
+        nc.vector.tensor_copy(xg0[:], x_win[0][:].indirect(offs_t[:]))
+        nc.vector.tensor_copy(xsg[:], xs_win[:].indirect(offs_t[:]))
+        quantise_w("y", 0, "vector", "raw_e0")
+        quantise_w("e", 0, "scalar", None)
+        quantise_w("e", 1, "scalar", "ident0")
+        gather_x1((512, 768, 1024), None)
+        gather_x1((0, 512), "xs_win")
+        product("e", 0, (5, 4, 6), "x_window0", (0, 512, 768, 1024))
+        gather("1", 0, 0, 4, None)
+        quantise_w("y", 1, "vector", None)
+        product("e", 1, (7, 2), "raw_y1", (0, 512, 1024))
+        quantise_w("e", 2, "scalar", None)
+        product("y", 0, (5, 6), None, (0, 512, 1024))
+        gather("2", 1, 0, 4, None)
+        gather("2", 0, 0, 4, "raw_y0")
+        quantise_w("y", 2, "scalar", "wb_e0")
+        product("y", 1, (3, 4), None, (0, 512, 1024))
+        product("e", 2, (5, 2), None, (0, 512, 1024))
+        product("y", 2, (3, 2), "g2_10", (0, 512, 1024))
+        gather("1", 1, 0, 4, None)
+        quantise_w("y", 3, "scalar", "wb_e0")
+        gather("2", 2, 0, 4, None)
+        gather("c", 2, 0, 4, None)
+        gather("c", 0, 0, 4, "wb_e1")
+        gather("c", 1, 0, 4, None)
+        product("y", 3, (7, 6), "g1_10", (0, 512, 1024))
+        gather("1", 2, 0, 4, None)
+        quantise_w("e", 3, "scalar", None)
+        product("e", 3, (4, 3), "g1_00", (0, 512, 1024))
+        largest(2, 0, 4, None)
+        largest(1, 0, 4, "raw_e2")
+        gather("1", 3, 0, 4, None)
+        largest(0, 0, 4, None)
+        gather("2", 3, 0, 4, None)
+        gather("c", 3, 0, 2, "g1_20")
+        edges(0, 2, 0, 4)
+        largest(3, 0, 4, "wb_e0")
+        gather("c", 3, 2, 3, "raw_y1")
+        edges(1, 1, 0, 4)
+        gather("c", 3, 3, 4, "gc_10")
+        edges(2, 0, 0, 4)
+        edges(3, 7, 0, 2)
+        turn(0, 2, 1, "vector")
+        edges(3, 7, 3, 4)
+        project(0, 2, 1, "vector")
+        turn(3, 4, 0, "scalar")
+        edges(3, 3, 2, 3)
+        project(3, 4, 7, "scalar")
+        turn(2, 3, 6, "scalar")
+        project(2, 3, 3, "scalar")

@@ -37,8 +37,19 @@ def tile_picked_edgecv_relu_p_kernel(
         def sb(shape, dtype, name, tag=None):
             return keep.tile(shape, dtype, name=name, tag=tag or name, align_bytes=64)
 
+        banks = [psum.tile([P, BANK], F32, name="bank%d" % b) for b in range(8)]
+
         def bank(b, name):
-            return psum.tile([P, BANK], F32, name=name, tag="bank%d" % b)
+            return banks[b]
+
+        space = {}
+
+        def words(n, name, over=None):
+            if over is None:
+                space[name] = sb([P, n], F32, name)
+            else:
+                space[name] = space[over]
+            return space[name][:, :n]
 
         def load_list(src, name):
             t = keep.tile(list(src.shape), U16, name=name)
@@ -50,7 +61,7 @@ def tile_picked_edgecv_relu_p_kernel(
 
         def load_w(m, c0, c1):
             width = P * (c1 - c0)
-            t = sb([P, PASSES, 4, width], F32, "raw_%s%d" % (m, c0))
+            t = words(PASSES * 4 * width, "raw_%s%d" % (m, c0)).rearrange("p (z j c) -> p z j c", z=PASSES, j=4)
             for z in range(PASSES):
                 rows = weights[m][512 * z : 512 * (z + 1), P * c0 : P * c1]
                 nc.sync.dma_start(t[:, z], rows.rearrange("(p j) c -> p j c", j=4))
@@ -67,25 +78,25 @@ def tile_picked_edgecv_relu_p_kernel(
         xs_win = sb([P, T], U8, "xs_win")
         nc.gpsimd.memset(xs_win[:].bitcast(I32), 0)
         for q in range(4):
-            nc.gpsimd.dma_start(
+            nc.sync.dma_start(
                 xs_win[32 * q : 32 * q + 8, :].bitcast(I32), x_scales[:, 4 * q : 4 * q + 4, :].bitcast(I32)
             )
+        w3w = sb([P, 2 * N], U8, "w3w")
         offs_t = load_list(offs, "offs_t")
         load_x(0)
-        load_x(1)
         pos1_t = load_list(pos1, "pos1_t")
-        load_w("e", 0, 1)
         cen_t = load_list(cen, "cen_t")
-        load_w("e", 1, 2)
+        load_x(1)
+        load_w("e", 0, 1)
         pos2_t = load_list(pos2, "pos2_t")
+        load_w("e", 1, 2)
         load_w("y", 0, 1)
         load_w("y", 1, 2)
-        load_w("e", 3, 4)
+        nc.sync.dma_start(w3w[:], w3_words[0])
         load_w("e", 2, 3)
+        load_w("e", 3, 4)
         load_w("y", 2, 3)
         load_w("y", 3, 4)
-        w3w = sb([P, 2 * N], U8, "w3w")
-        nc.sync.dma_start(w3w[:], w3_words[0])
         w3s = sb([P, N], U8, "w3s")
         nc.gpsimd.memset(w3s[:].bitcast(I32), 0)
         for q in range(4):
@@ -98,8 +109,18 @@ def tile_picked_edgecv_relu_p_kernel(
         nc.scalar.activation(ident[:], ident0[:], RELU)
 
         xg0 = sb([P, S], U32, "xg0")
-        xsg = sb([P, S], U8, "xsg")
+        xsg = {}
         xg1 = {}
+
+        def gather_xs(cuts, tag=None):
+            s0 = cuts[0]
+            xsg[s0] = sb([P, cuts[-1] - s0], U8, "xsg_%d" % s0, tag)
+            for a, b in zip(cuts, cuts[1:]):
+                nc.vector.tensor_copy(xsg[s0][:, a - s0 : b - s0], xs_win[:].indirect(offs_t[:, a // 16 : b // 16]))
+
+        def xs_cols(z, s0, s1):
+            b = max(k for k in xsg if k <= s0)
+            return xsg[b][4 * z : P, s0 - b : s1 - b]
 
         def gather_x1(cuts, tag=None):
             s0 = cuts[0]
@@ -114,7 +135,7 @@ def tile_picked_edgecv_relu_p_kernel(
         codes, planes, rows = {}, {}, {}
 
         def quantise_w(m, c, eng="scalar", tag=None):
-            g = sb([P, PASSES, P, 4], BF16, "wb_%s%d" % (m, c), tag)
+            g = words(PASSES * P * 2, "wb_%s%d" % (m, c), tag).bitcast(BF16).rearrange("p (z c j) -> p z c j", z=PASSES, j=4)
             if eng == "gpsimd":
                 for z in range(PASSES):
                     nc.gpsimd.tensor_scalar(
@@ -124,7 +145,7 @@ def tile_picked_edgecv_relu_p_kernel(
                     )
             else:
                 (nc.scalar.copy if eng == "scalar" else nc.vector.tensor_copy)(
-                    g[:].rearrange("p z (g i) j -> p z g j i", i=4),
+                    g.rearrange("p z (g i) j -> p z g j i", i=4),
                     raw[m, c].rearrange("p z j (g i) -> p z g j i", i=4),
                 )
             codes[m, c] = sb([P, PASSES * P], U32, "wq_%s%d" % (m, c))
@@ -132,13 +153,13 @@ def tile_picked_edgecv_relu_p_kernel(
             nc.vector.quantize_mx(
                 out=codes[m, c][:].bitcast(FP8X4),
                 scales=planes[m, c][:],
-                in_=g[:].rearrange("p z c j -> p (z c j)"),
+                in_=g.rearrange("p z c j -> p (z c j)"),
             )
 
-        def product(m, c, banks, tag=None, cuts=(0, 512, 1024)):
-            rows[m, c] = sb([P, S], F32, "rows_%s%d" % (m, c), tag)
+        def product(m, c, into, tag=None, cuts=(0, 512, 1024)):
+            rows[m, c] = words(S, "rows_%s%d" % (m, c), tag)
             for h in range(len(cuts) - 1):
-                acc = bank(banks[h], "acc_%s%d%d" % (m, c, h))
+                acc = bank(into[h], "acc_%s%d%d" % (m, c, h))
                 s0, s1 = cuts[h], cuts[h + 1]
                 for z in range(PASSES):
                     nc.tensor.matmul_mx(
@@ -146,7 +167,7 @@ def tile_picked_edgecv_relu_p_kernel(
                         lhsT=codes[m, c][:, P * z : P * (z + 1)].bitcast(FP8X4),
                         lhsT_scale=planes[m, c][:, P * z : P * (z + 1)],
                         rhs=(x1_cols(s0, s1) if z else xg0[:, s0:s1]).bitcast(FP8X4),
-                        rhs_scale=xsg[4 * z : P, s0:s1],
+                        rhs_scale=xs_cols(z, s0, s1),
                         start=(z == 0),
                         stop=(z == PASSES - 1),
                     )
@@ -157,8 +178,8 @@ def tile_picked_edgecv_relu_p_kernel(
 
         def gather(k, c, b0=0, b1=4, tag=None):
             m, lst = {"1": ("e", pos1_t), "2": ("e", pos2_t), "c": ("y", cen_t)}[k]
-            g = sb([P, P * (b1 - b0)], F32, "g%s_%d%d" % (k, c, b0), tag)
-            nc.vector.tensor_copy(g[:], rows[m, c][:].indirect(lst[:, 8 * b0 : 8 * b1]))
+            g = words(P * (b1 - b0), "g%s_%d%d" % (k, c, b0), tag)
+            nc.vector.tensor_copy(g, rows[m, c].indirect(lst[:, 8 * b0 : 8 * b1]))
             for b in range(b0, b1):
                 got[k, c, b] = (g, b0)
 
@@ -167,8 +188,8 @@ def tile_picked_edgecv_relu_p_kernel(
             return g[:, P * (b0 - base) : P * (b1 - base)]
 
         def largest(c, b0=0, b1=4, tag=None):
-            gm = sb([P, P * (b1 - b0)], F32, "gm_%d%d" % (c, b0), tag)
-            nc.vector.tensor_tensor(gm[:], part("1", c, b0, b1), part("2", c, b0, b1), MAX)
+            gm = words(P * (b1 - b0), "gm_%d%d" % (c, b0), tag)
+            nc.vector.tensor_tensor(gm, part("1", c, b0, b1), part("2", c, b0, b1), MAX)
             for b in range(b0, b1):
                 got["m", c, b] = (gm, b0)
 
@@ -177,8 +198,8 @@ def tile_picked_edgecv_relu_p_kernel(
             acc = bank(b, "zsum%d%d" % (c, b0))
             for i in range(b0, b1):
                 cols = slice(P * (i - b0), P * (i - b0 + 1))
-                nc.tensor.matmul(acc[:, cols], part("m", c, i, i + 1), ident[:], start=True, stop=False, is_transpose=True)
-                nc.tensor.matmul(acc[:, cols], part("c", c, i, i + 1), ident[:], start=False, stop=True, is_transpose=True)
+                nc.tensor.matmul(acc[:, cols], part("c", c, i, i + 1), ident[:], start=True, stop=False, is_transpose=True)
+                nc.tensor.matmul(acc[:, cols], part("m", c, i, i + 1), ident[:], start=False, stop=True, is_transpose=True)
             nc.scalar.activation(
                 zt[:, b0:b1, P * c : P * (c + 1)], acc[:, :n].rearrange("v (b i) -> v b i", i=P), RELU
             )
@@ -189,9 +210,9 @@ def tile_picked_edgecv_relu_p_kernel(
             n = P * (b1 - b0)
             turned = bank(b_turn, "turned%d" % b0)
             for i in range(b1 - b0):
-                words = zt[:, b0 + i, :].bitcast(F32)
+                pairs = zt[:, b0 + i, :].bitcast(F32)
                 for u in range(2):
-                    nc.tensor.transpose(turned[:, n * u + P * i : n * u + P * (i + 1)], words[:, u::2], ident[:])
+                    nc.tensor.transpose(turned[:, n * u + P * i : n * u + P * (i + 1)], pairs[:, u::2], ident[:])
             zb[b0] = sb([P, n, 4], BF16, "zb%d" % b0)
             (nc.scalar.copy if eng == "scalar" else nc.vector.tensor_copy)(
                 zb[b0][:].bitcast(F32), turned[:, : 2 * n].rearrange("p (u v) -> p v u", u=2)
@@ -217,52 +238,52 @@ def tile_picked_edgecv_relu_p_kernel(
             nc.sync.dma_start(out[:, P * b0 : P * b1], res[:])
 
         nc.vector.tensor_copy(xg0[:], x_win[0][:].indirect(offs_t[:]))
-        nc.vector.tensor_copy(xsg[:], xs_win[:].indirect(offs_t[:]))
-        quantise_w("y", 0, "vector", "raw_e0")
+        gather_x1((0, 1024), None)
+        gather_xs((0, 512), "x_window0")
+        quantise_w("e", 1, "scalar", None)
         quantise_w("e", 0, "scalar", None)
-        quantise_w("e", 1, "scalar", "ident0")
-        gather_x1((512, 768, 1024), None)
-        gather_x1((0, 512), "xs_win")
-        product("e", 0, (5, 4, 6), "x_window0", (0, 512, 768, 1024))
-        gather("1", 0, 0, 4, None)
-        quantise_w("y", 1, "vector", None)
-        product("e", 1, (7, 2), "raw_y1", (0, 512, 1024))
+        gather_xs((512, 768, 1024), "raw_e0")
+        product("e", 0, (6, 7, 5), None, (0, 512, 768, 1024))
+        product("e", 1, (6, 5), None, (0, 512, 1024))
+        quantise_w("y", 0, "vector", "wb_e1")
+        quantise_w("y", 1, "scalar", None)
+        product("y", 0, (2, 5), "raw_y0", (0, 512, 1024))
         quantise_w("e", 2, "scalar", None)
-        product("y", 0, (5, 6), None, (0, 512, 1024))
         gather("2", 1, 0, 4, None)
-        gather("2", 0, 0, 4, "raw_y0")
-        quantise_w("y", 2, "scalar", "wb_e0")
-        product("y", 1, (3, 4), None, (0, 512, 1024))
-        product("e", 2, (5, 2), None, (0, 512, 1024))
-        product("y", 2, (3, 2), "g2_10", (0, 512, 1024))
         gather("1", 1, 0, 4, None)
-        quantise_w("y", 3, "scalar", "wb_e0")
-        gather("2", 2, 0, 4, None)
-        gather("c", 2, 0, 4, None)
-        gather("c", 0, 0, 4, "wb_e1")
-        gather("c", 1, 0, 4, None)
-        product("y", 3, (7, 6), "g1_10", (0, 512, 1024))
-        gather("1", 2, 0, 4, None)
+        product("e", 2, (5, 7), None, (0, 512, 1024))
         quantise_w("e", 3, "scalar", None)
-        product("e", 3, (4, 3), "g1_00", (0, 512, 1024))
-        largest(2, 0, 4, None)
         largest(1, 0, 4, "raw_e2")
-        gather("1", 3, 0, 4, None)
-        largest(0, 0, 4, None)
+        gather("c", 0, 0, 4, None)
+        gather("2", 0, 0, 4, None)
+        gather("1", 0, 0, 4, None)
+        product("y", 1, (2, 1), None, (0, 512, 1024))
+        quantise_w("y", 2, "vector", "wb_e2")
+        gather("1", 2, 0, 4, None)
+        gather("2", 2, 0, 4, None)
+        largest(0, 0, 4, "raw_y1")
+        edges(0, 4, 0, 4)
+        quantise_w("y", 3, "scalar", "raw_y2")
+        product("y", 2, (5, 0), None, (0, 512, 1024))
+        product("e", 3, (2, 4), "raw_e3", (0, 512, 1024))
+        product("y", 3, (5, 1), None, (0, 512, 1024))
+        gather("c", 2, 0, 4, None)
         gather("2", 3, 0, 4, None)
-        gather("c", 3, 0, 2, "g1_20")
-        edges(0, 2, 0, 4)
-        largest(3, 0, 4, "wb_e0")
-        gather("c", 3, 2, 3, "raw_y1")
-        edges(1, 1, 0, 4)
-        gather("c", 3, 3, 4, "gc_10")
-        edges(2, 0, 0, 4)
-        edges(3, 7, 0, 2)
-        turn(0, 2, 1, "vector")
-        edges(3, 7, 3, 4)
-        project(0, 2, 1, "vector")
-        turn(3, 4, 0, "scalar")
-        edges(3, 3, 2, 3)
-        project(3, 4, 7, "scalar")
-        turn(2, 3, 6, "scalar")
-        project(2, 3, 3, "scalar")
+        gather("c", 3, 2, 3, None)
+        largest(2, 0, 4, None)
+        edges(2, 6, 0, 4)
+        gather("c", 3, 3, 4, None)
+        gather("c", 3, 0, 2, "wb_y2")
+        gather("1", 3, 0, 4, "wb_y3")
+        gather("c", 1, 0, 4, None)
+        edges(1, 5, 0, 4)
+        largest(3, 0, 4, None)
+        edges(3, 6, 2, 3)
+        edges(3, 5, 0, 2)
+        turn(0, 2, 0, "scalar")
+        edges(3, 4, 3, 4)
+        turn(3, 4, 4, "vector")
+        turn(2, 3, 2, "scalar")
+        project(3, 4, 7, "vector")
+        project(2, 3, 0, "vector")
+        project(0, 2, 4, "vector")

@@ -16,14 +16,23 @@ FP8X4 = mybir.dt.float8_e4m3fn_x4
 FP4X4 = mybir.dt.float4_e2m1fn_x4
 RELU = mybir.ActivationFunctionType.Relu
 MAX = mybir.AluOpType.max
-MULT = mybir.AluOpType.mult
-ADD = mybir.AluOpType.add
-SUB = mybir.AluOpType.subtract
 
 P = 128
 PASSES = 2
-TILES = 4
 BANK = 512
+UNIT = 1024
+RAW_AT = 256
+
+UNITS = (
+    ("e", 0, 1, (0, 1)),
+    ("e", 1, 1, (0, 1)),
+    ("e", 2, 2, (0,)),
+    ("e", 2, 2, (1,)),
+    ("y", 0, 2, (0,)),
+    ("y", 0, 2, (1,)),
+    ("y", 2, 2, (0,)),
+    ("y", 2, 2, (1,)),
+)
 
 
 def tile_picked_edgecv_relu_p_kernel(
@@ -33,23 +42,10 @@ def tile_picked_edgecv_relu_p_kernel(
     with ExitStack() as ctx:
         keep = ctx.enter_context(tc.tile_pool(name="keep", bufs=1))
         psum = ctx.enter_context(tc.psum_pool(name="psum", bufs=1))
+        banks = [psum.tile([P, BANK], F32, name="bank%d" % b) for b in range(8)]
 
         def sb(shape, dtype, name, tag=None):
             return keep.tile(shape, dtype, name=name, tag=tag or name, align_bytes=64)
-
-        banks = [psum.tile([P, BANK], F32, name="bank%d" % b) for b in range(8)]
-
-        def bank(b, name):
-            return banks[b]
-
-        space = {}
-
-        def words(n, name, over=None):
-            if over is None:
-                space[name] = sb([P, n], F32, name)
-            else:
-                space[name] = space[over]
-            return space[name][:, :n]
 
         def load_list(src, name):
             t = keep.tile(list(src.shape), U16, name=name)
@@ -57,175 +53,138 @@ def tile_picked_edgecv_relu_p_kernel(
             return t
 
         weights = {"y": w1, "e": w2}
-        raw = {}
+        stage = [sb([P, 2 * UNIT], F32, "raw_%d" % i) for i in range(len(UNITS))]
+        raw, where = {}, {}
 
-        def load_w(m, c0, c1):
-            width = P * (c1 - c0)
-            t = words(PASSES * 4 * width, "raw_%s%d" % (m, c0)).rearrange("p (z j c) -> p z j c", z=PASSES, j=4)
-            for z in range(PASSES):
-                rows = weights[m][512 * z : 512 * (z + 1), P * c0 : P * c1]
-                nc.sync.dma_start(t[:, z], rows.rearrange("(p j) c -> p j c", j=4))
-            for c in range(c0, c1):
-                raw[m, c] = t[:, :, :, P * (c - c0) : P * (c - c0 + 1)]
+        def load_w(i):
+            m, c0, width, zs = UNITS[i]
+            raw[i] = stage[i][:, RAW_AT : RAW_AT + UNIT].rearrange("p (z j c) -> p z j c", z=len(zs), j=4)
+            for a, z in enumerate(zs):
+                src = weights[m][512 * z : 512 * (z + 1), P * c0 : P * (c0 + width)]
+                nc.sync.dma_start(raw[i][:, a], src.rearrange("(p j) c -> p j c", j=4))
+                for c in range(width):
+                    where[m, c0 + c, z] = (i, P * (a * width + c))
 
-        x_win = {}
+        x_win = [sb([P, T], U32, "x_window%d" % z) for z in range(PASSES)]
 
         def load_x(z):
-            t = sb([P, T], U32, "x_window%d" % z)
-            nc.sync.dma_start(t[:].bitcast(I32), x_words[z].rearrange("p c r -> p (c r)").bitcast(I32))
-            x_win[z] = t
+            nc.sync.dma_start(x_win[z][:].bitcast(I32), x_words[z].rearrange("p c r -> p (c r)").bitcast(I32))
 
         xs_win = sb([P, T], U8, "xs_win")
         nc.gpsimd.memset(xs_win[:].bitcast(I32), 0)
         for q in range(4):
-            nc.sync.dma_start(
+            nc.gpsimd.dma_start(
                 xs_win[32 * q : 32 * q + 8, :].bitcast(I32), x_scales[:, 4 * q : 4 * q + 4, :].bitcast(I32)
             )
-        w3w = sb([P, 2 * N], U8, "w3w")
         offs_t = load_list(offs, "offs_t")
         load_x(0)
-        pos1_t = load_list(pos1, "pos1_t")
-        cen_t = load_list(cen, "cen_t")
+        load_w(0)
         load_x(1)
-        load_w("e", 0, 1)
+        load_w(1)
+        load_w(2)
+        pos1_t = load_list(pos1, "pos1_t")
         pos2_t = load_list(pos2, "pos2_t")
-        load_w("e", 1, 2)
-        load_w("y", 0, 1)
-        load_w("y", 1, 2)
+        for i in range(3, len(UNITS)):
+            load_w(i)
+        cen_t = load_list(cen, "cen_t")
+        w3w = sb([P, 2 * N], U8, "w3w")
         nc.sync.dma_start(w3w[:], w3_words[0])
-        load_w("e", 2, 3)
-        load_w("e", 3, 4)
-        load_w("y", 2, 3)
-        load_w("y", 3, 4)
         w3s = sb([P, N], U8, "w3s")
         nc.gpsimd.memset(w3s[:].bitcast(I32), 0)
         for q in range(4):
             nc.sync.dma_start(
                 w3s[32 * q : 32 * q + 4, :].bitcast(I32), w3_scales[0, 4 * q : 4 * q + 4, :].bitcast(I32)
             )
-        ident0 = sb([P, P], F32, "ident0")
-        make_identity(nc, ident0[:])
         ident = sb([P, P], F32, "ident")
-        nc.scalar.activation(ident[:], ident0[:], RELU)
+        make_identity(nc, ident[:])
 
-        xg0 = sb([P, S], U32, "xg0")
-        xsg = {}
-        xg1 = {}
+        codes, planes, cast, rows = {}, {}, {}, {}
 
-        def gather_xs(cuts, tag=None):
-            s0 = cuts[0]
-            xsg[s0] = sb([P, cuts[-1] - s0], U8, "xsg_%d" % s0, tag)
-            for a, b in zip(cuts, cuts[1:]):
-                nc.vector.tensor_copy(xsg[s0][:, a - s0 : b - s0], xs_win[:].indirect(offs_t[:, a // 16 : b // 16]))
-
-        def xs_cols(z, s0, s1):
-            b = max(k for k in xsg if k <= s0)
-            return xsg[b][4 * z : P, s0 - b : s1 - b]
-
-        def gather_x1(cuts, tag=None):
-            s0 = cuts[0]
-            xg1[s0] = sb([P, cuts[-1] - s0], U32, "xg1_%d" % s0, tag)
-            for a, b in zip(cuts, cuts[1:]):
-                nc.vector.tensor_copy(xg1[s0][:, a - s0 : b - s0], x_win[1][:].indirect(offs_t[:, a // 16 : b // 16]))
-
-        def x1_cols(s0, s1):
-            b = max(k for k in xg1 if k <= s0)
-            return xg1[b][:, s0 - b : s1 - b]
-
-        codes, planes, rows = {}, {}, {}
-
-        def quantise_w(m, c, eng="scalar", tag=None):
-            g = words(PASSES * P * 2, "wb_%s%d" % (m, c), tag).bitcast(BF16).rearrange("p (z c j) -> p z c j", z=PASSES, j=4)
-            if eng == "gpsimd":
-                for z in range(PASSES):
-                    nc.gpsimd.tensor_scalar(
-                        g[:, z].rearrange("p (g i) j -> p g j i", i=4),
-                        raw[m, c][:, z].rearrange("p j (g i) -> p g j i", i=4),
-                        1.0, 0.0, MULT, ADD,
-                    )
-            else:
-                (nc.scalar.copy if eng == "scalar" else nc.vector.tensor_copy)(
-                    g.rearrange("p z (g i) j -> p z g j i", i=4),
-                    raw[m, c].rearrange("p z j (g i) -> p z g j i", i=4),
-                )
-            codes[m, c] = sb([P, PASSES * P], U32, "wq_%s%d" % (m, c))
-            planes[m, c] = sb([P, PASSES * P], U8, "ws_%s%d" % (m, c))
-            nc.vector.quantize_mx(
-                out=codes[m, c][:].bitcast(FP8X4),
-                scales=planes[m, c][:],
-                in_=g.rearrange("p z c j -> p (z c j)"),
+        def quantise_w(i, into, codes_tag=None, copy=nc.scalar.copy):
+            cast[i] = into
+            grouped = into.bitcast(BF16)
+            copy(
+                grouped.rearrange("p (z g i j) -> p z g j i", z=raw[i].shape[1], i=4, j=4),
+                raw[i].rearrange("p z j (g i) -> p z g j i", i=4),
             )
+            codes[i] = sb([P, 2 * P], U32, "wq_%d" % i, codes_tag)
+            planes[i] = sb([P, 2 * P], U8, "ws_%d" % i)
+            nc.vector.quantize_mx(out=codes[i][:].bitcast(FP8X4), scales=planes[i][:], in_=grouped)
 
-        def product(m, c, into, tag=None, cuts=(0, 512, 1024)):
-            rows[m, c] = words(S, "rows_%s%d" % (m, c), tag)
+        def product(m, c, into, via, cuts=(0, 512, 1024)):
+            rows[m, c] = into
             for h in range(len(cuts) - 1):
-                acc = bank(into[h], "acc_%s%d%d" % (m, c, h))
                 s0, s1 = cuts[h], cuts[h + 1]
+                acc = banks[via[h]][:, : s1 - s0]
                 for z in range(PASSES):
+                    i, col = where[m, c, z]
                     nc.tensor.matmul_mx(
-                        out=acc[:, : s1 - s0],
-                        lhsT=codes[m, c][:, P * z : P * (z + 1)].bitcast(FP8X4),
-                        lhsT_scale=planes[m, c][:, P * z : P * (z + 1)],
-                        rhs=(x1_cols(s0, s1) if z else xg0[:, s0:s1]).bitcast(FP8X4),
-                        rhs_scale=xs_cols(z, s0, s1),
+                        out=acc,
+                        lhsT=codes[i][:, col : col + P].bitcast(FP8X4),
+                        lhsT_scale=planes[i][:, col : col + P],
+                        rhs=xg[z][:, s0:s1].bitcast(FP8X4),
+                        rhs_scale=xsg[4 * z : P, s0:s1],
                         start=(z == 0),
                         stop=(z == PASSES - 1),
                     )
-                nc.scalar.copy(rows[m, c][:, s0:s1], acc[:, : s1 - s0])
+                nc.scalar.copy(rows[m, c][:, s0:s1], acc)
 
-        zt = sb([P, TILES, H], BF16, "zt")
-        got = {}
+        zt = sb([P, 4, 2, P, 2], BF16, "zt")
+        far, mid = {}, {}
 
-        def gather(k, c, b0=0, b1=4, tag=None):
-            m, lst = {"1": ("e", pos1_t), "2": ("e", pos2_t), "c": ("y", cen_t)}[k]
-            g = words(P * (b1 - b0), "g%s_%d%d" % (k, c, b0), tag)
-            nc.vector.tensor_copy(g, rows[m, c].indirect(lst[:, 8 * b0 : 8 * b1]))
-            for b in range(b0, b1):
-                got[k, c, b] = (g, b0)
-
-        def part(k, c, b0, b1):
-            g, base = got[k, c, b0]
-            return g[:, P * (b0 - base) : P * (b1 - base)]
-
-        def largest(c, b0=0, b1=4, tag=None):
-            gm = words(P * (b1 - b0), "gm_%d%d" % (c, b0), tag)
-            nc.vector.tensor_tensor(gm, part("1", c, b0, b1), part("2", c, b0, b1), MAX)
-            for b in range(b0, b1):
-                got["m", c, b] = (gm, b0)
-
-        def edges(c, b, b0=0, b1=4):
+        def neighbours(c, b0=0, b1=4, first=None, second=None):
             n = P * (b1 - b0)
-            acc = bank(b, "zsum%d%d" % (c, b0))
-            for i in range(b0, b1):
-                cols = slice(P * (i - b0), P * (i - b0 + 1))
-                nc.tensor.matmul(acc[:, cols], part("c", c, i, i + 1), ident[:], start=True, stop=False, is_transpose=True)
-                nc.tensor.matmul(acc[:, cols], part("m", c, i, i + 1), ident[:], start=False, stop=True, is_transpose=True)
-            nc.scalar.activation(
-                zt[:, b0:b1, P * c : P * (c + 1)], acc[:, :n].rearrange("v (b i) -> v b i", i=P), RELU
-            )
+            g1 = sb([P, n], F32, "g1_%d%d" % (c, b0))[:] if first is None else first
+            g2 = sb([P, n], F32, "g2_%d%d" % (c, b0))[:] if second is None else second
+            gm = sb([P, n], F32, "gm_%d%d" % (c, b0))
+            nc.vector.tensor_copy(g1, rows["e", c].indirect(pos1_t[:, 8 * b0 : 8 * b1]))
+            nc.vector.tensor_copy(g2, rows["e", c].indirect(pos2_t[:, 8 * b0 : 8 * b1]))
+            nc.vector.tensor_tensor(gm[:], g1, g2, MAX)
+            for b in range(b0, b1):
+                far[c, b] = gm[:, P * (b - b0) : P * (b - b0 + 1)]
+
+        def centres(c):
+            gc = sb([P, V], F32, "gc_%d" % c)
+            nc.vector.tensor_copy(gc[:], rows["y", c].indirect(cen_t[:]))
+            for b in range(4):
+                mid[c, b] = gc[:, P * b : P * (b + 1)]
+
+        def edges(c, via, b0=0, b1=4):
+            n = P * (b1 - b0)
+            acc = banks[via]
+            for b in range(b0, b1):
+                cols = slice(P * (b - b0), P * (b - b0 + 1))
+                first, second = mid[c, b], far[c, b]
+                nc.tensor.matmul(acc[:, cols], first, ident[:], start=True, stop=False, is_transpose=True)
+                nc.tensor.matmul(acc[:, cols], second, ident[:], start=False, stop=True, is_transpose=True)
+            sums = acc[:, :n].rearrange("v (b q u e) -> v b u q e", q=32, u=2, e=2)
+            if b1 - b0 == 1:
+                nc.scalar.activation(zt[:, b0, :, 32 * c : 32 * (c + 1), :], sums[:, 0], RELU)
+            else:
+                for u in range(2):
+                    nc.scalar.activation(zt[:, b0:b1, u, 32 * c : 32 * (c + 1), :], sums[:, :, u], RELU)
 
         zb = {}
 
-        def turn(b0, b1, b_turn, eng="scalar"):
+        def turn(b0, b1, via, copy):
             n = P * (b1 - b0)
-            turned = bank(b_turn, "turned%d" % b0)
-            for i in range(b1 - b0):
-                pairs = zt[:, b0 + i, :].bitcast(F32)
+            turned = banks[via]
+            for b in range(b0, b1):
                 for u in range(2):
-                    nc.tensor.transpose(turned[:, n * u + P * i : n * u + P * (i + 1)], pairs[:, u::2], ident[:])
+                    pairs = zt[:, b, u].rearrange("v q e -> v (q e)").bitcast(F32)
+                    at = n * u + P * (b - b0)
+                    nc.tensor.transpose(turned[:, at : at + P], pairs, ident[:])
             zb[b0] = sb([P, n, 4], BF16, "zb%d" % b0)
-            (nc.scalar.copy if eng == "scalar" else nc.vector.tensor_copy)(
-                zb[b0][:].bitcast(F32), turned[:, : 2 * n].rearrange("p (u v) -> p v u", u=2)
-            )
+            copy(zb[b0][:].bitcast(F32), turned[:, : 2 * n].rearrange("p (u v) -> p v u", u=2))
 
-        def project(b0, b1, b_out, eng="scalar"):
+        def project(b0, b1, via, copy):
             n = P * (b1 - b0)
             zq = sb([P, n], U32, "zq%d" % b0)
             zs = sb([P, n], U8, "zs%d" % b0)
             nc.vector.quantize_mx(out=zq[:].bitcast(FP8X4), scales=zs[:], in_=zb[b0][:].rearrange("p v j -> p (v j)"))
-            acc = bank(b_out, "res%d" % b0)
+            acc = banks[via][:, :n]
             nc.tensor.matmul_mx(
-                out=acc[:, :n],
+                out=acc,
                 lhsT=w3w[:].bitcast(FP4X4),
                 lhsT_scale=w3s[:],
                 rhs=zq[:].bitcast(FP8X4),
@@ -234,56 +193,61 @@ def tile_picked_edgecv_relu_p_kernel(
                 stop=True,
             )
             res = sb([P, n], F32, "res_sb%d" % b0)
-            (nc.scalar.copy if eng == "scalar" else nc.vector.tensor_copy)(res[:], acc[:, :n])
+            copy(res[:], acc)
             nc.sync.dma_start(out[:, P * b0 : P * b1], res[:])
 
-        nc.vector.tensor_copy(xg0[:], x_win[0][:].indirect(offs_t[:]))
-        gather_x1((0, 1024), None)
-        gather_xs((0, 512), "x_window0")
-        quantise_w("e", 1, "scalar", None)
-        quantise_w("e", 0, "scalar", None)
-        gather_xs((512, 768, 1024), "raw_e0")
-        product("e", 0, (6, 7, 5), None, (0, 512, 768, 1024))
-        product("e", 1, (6, 5), None, (0, 512, 1024))
-        quantise_w("y", 0, "vector", "wb_e1")
-        quantise_w("y", 1, "scalar", None)
-        product("y", 0, (2, 5), "raw_y0", (0, 512, 1024))
-        quantise_w("e", 2, "scalar", None)
-        gather("2", 1, 0, 4, None)
-        gather("1", 1, 0, 4, None)
-        product("e", 2, (5, 7), None, (0, 512, 1024))
-        quantise_w("e", 3, "scalar", None)
-        largest(1, 0, 4, "raw_e2")
-        gather("c", 0, 0, 4, None)
-        gather("2", 0, 0, 4, None)
-        gather("1", 0, 0, 4, None)
-        product("y", 1, (2, 1), None, (0, 512, 1024))
-        quantise_w("y", 2, "vector", "wb_e2")
-        gather("1", 2, 0, 4, None)
-        gather("2", 2, 0, 4, None)
-        largest(0, 0, 4, "raw_y1")
-        edges(0, 4, 0, 4)
-        quantise_w("y", 3, "scalar", "raw_y2")
-        product("y", 2, (5, 0), None, (0, 512, 1024))
-        product("e", 3, (2, 4), "raw_e3", (0, 512, 1024))
-        product("y", 3, (5, 1), None, (0, 512, 1024))
-        gather("c", 2, 0, 4, None)
-        gather("2", 3, 0, 4, None)
-        gather("c", 3, 2, 3, None)
-        largest(2, 0, 4, None)
-        edges(2, 6, 0, 4)
-        gather("c", 3, 3, 4, None)
-        gather("c", 3, 0, 2, "wb_y2")
-        gather("1", 3, 0, 4, "wb_y3")
-        gather("c", 1, 0, 4, None)
-        edges(1, 5, 0, 4)
-        largest(3, 0, 4, None)
-        edges(3, 6, 2, 3)
-        edges(3, 5, 0, 2)
-        turn(0, 2, 0, "scalar")
-        edges(3, 4, 3, 4)
-        turn(3, 4, 4, "vector")
-        turn(2, 3, 2, "scalar")
-        project(3, 4, 7, "vector")
-        project(2, 3, 0, "vector")
-        project(0, 2, 4, "vector")
+        def fresh(n, name):
+            return sb([P, n], F32, name)[:]
+
+        def front(i):
+            return stage[i][:, :UNIT]
+
+        def back(i):
+            return stage[i][:, UNIT:]
+
+        def half(i):
+            return stage[i][:, UNIT : UNIT + UNIT // 2]
+
+        sc, vc = nc.scalar.copy, nc.vector.tensor_copy
+        xg = [sb([P, S], U32, "xg0")]
+        nc.vector.tensor_copy(xg[0][:], x_win[0][:].indirect(offs_t[:]))
+        xsg = sb([P, S], U8, "xsg")
+        nc.vector.tensor_copy(xsg[:], xs_win[:].indirect(offs_t[:]))
+        quantise_w(0, fresh(UNIT // 2, "wb_0"), "xs_win")
+        xg.append(sb([P, S], U32, "xg1", "wb_0"))
+        for a, b in ((0, 512), (512, 768), (768, 1024)):
+            nc.vector.tensor_copy(xg[1][:, a:b], x_win[1][:].indirect(offs_t[:, a // 16 : b // 16]))
+        slot = sb([P, UNIT], F32, "slot")
+        quantise_w(1, slot[:, 256:768], "x_window1")
+        quantise_w(2, slot[:, 256:768], None, vc)
+        product("e", 0, front(1), (0, 1, 2), (0, 512, 768, 1024))
+        neighbours(0, first=front(2)[:, :512], second=slot[:, :512])
+        quantise_w(3, half(2))
+        product("e", 1, front(3), (3, 4))
+        quantise_w(4, half(3))
+        neighbours(1, second=cast[4])
+        quantise_w(5, half(4))
+        product("e", 2, front(5), (5, 6))
+        quantise_w(6, half(5))
+        neighbours(2, second=cast[6])
+        quantise_w(7, half(6))
+        product("y", 0, front(7), (7, 0))
+        centres(0)
+        product("y", 1, back(7), (1, 7))
+        centres(1)
+        product("y", 2, front(0), (3, 4))
+        centres(2)
+        product("y", 3, front(4), (5, 6))
+        centres(3)
+        product("e", 3, front(6), (3, 4))
+        edges(0, 5)
+        edges(1, 6)
+        edges(2, 3)
+        firsts = [fresh(P, "g1_3%d" % i) for i in range(2)]
+        second = fresh(P, "g2_3")
+        for b in range(4):
+            neighbours(3, b, b + 1, firsts[b % 2], second)
+            edges(3, (7, 1, 4, 0)[b], b, b + 1)
+            turn(b, b + 1, (4, 0, 2, 7)[b], (sc, sc, sc, sc)[b])
+        for b in range(4):
+            project(b, b + 1, (5, 6, 3, 1)[b], (vc, vc, vc, vc)[b])

@@ -21,7 +21,6 @@ P = 128
 PASSES = 2
 BANK = 512
 UNIT = 1024
-RAW_AT = 256
 
 UNITS = (
     ("e", 0, 1, (0, 1)),
@@ -58,7 +57,7 @@ def tile_picked_edgecv_relu_p_kernel(
 
         def load_w(i):
             m, c0, width, zs = UNITS[i]
-            raw[i] = stage[i][:, RAW_AT : RAW_AT + UNIT].rearrange("p (z j c) -> p z j c", z=len(zs), j=4)
+            raw[i] = stage[i][:].rearrange("p (z j c) -> p z j c", z=len(zs), j=4)[:, :, :, : P * width]
             for a, z in enumerate(zs):
                 src = weights[m][512 * z : 512 * (z + 1), P * c0 : P * (c0 + width)]
                 nc.sync.dma_start(raw[i][:, a], src.rearrange("(p j) c -> p j c", j=4))
@@ -73,20 +72,18 @@ def tile_picked_edgecv_relu_p_kernel(
         xs_win = sb([P, T], U8, "xs_win")
         nc.gpsimd.memset(xs_win[:].bitcast(I32), 0)
         for q in range(4):
-            nc.gpsimd.dma_start(
+            nc.sync.dma_start(
                 xs_win[32 * q : 32 * q + 8, :].bitcast(I32), x_scales[:, 4 * q : 4 * q + 4, :].bitcast(I32)
             )
         offs_t = load_list(offs, "offs_t")
         load_x(0)
-        load_w(0)
-        load_x(1)
-        load_w(1)
-        load_w(2)
         pos1_t = load_list(pos1, "pos1_t")
         pos2_t = load_list(pos2, "pos2_t")
-        for i in range(3, len(UNITS)):
-            load_w(i)
+        load_x(1)
+        load_w(0)
         cen_t = load_list(cen, "cen_t")
+        for i in range(1, len(UNITS)):
+            load_w(i)
         w3w = sb([P, 2 * N], U8, "w3w")
         nc.sync.dma_start(w3w[:], w3_words[0])
         w3s = sb([P, N], U8, "w3s")
@@ -100,16 +97,19 @@ def tile_picked_edgecv_relu_p_kernel(
 
         codes, planes, cast, rows = {}, {}, {}, {}
 
-        def quantise_w(i, into, codes_tag=None, copy=nc.scalar.copy):
+        def quantise_w(i, into, codes_tag=None, copy=nc.scalar.copy, parts=1):
             cast[i] = into
-            grouped = into.bitcast(BF16)
-            copy(
-                grouped.rearrange("p (z g i j) -> p z g j i", z=raw[i].shape[1], i=4, j=4),
-                raw[i].rearrange("p z j (g i) -> p z g j i", i=4),
-            )
             codes[i] = sb([P, 2 * P], U32, "wq_%d" % i, codes_tag)
             planes[i] = sb([P, 2 * P], U8, "ws_%d" % i)
-            nc.vector.quantize_mx(out=codes[i][:].bitcast(FP8X4), scales=planes[i][:], in_=grouped)
+            zs = raw[i].shape[1] // parts
+            for h in range(parts):
+                grouped = into.bitcast(BF16)[:, UNIT // parts * h : UNIT // parts * (h + 1)]
+                cols = slice(2 * P // parts * h, 2 * P // parts * (h + 1))
+                copy(
+                    grouped.rearrange("p (z g i j) -> p z g j i", z=zs, i=4, j=4),
+                    raw[i][:, zs * h : zs * (h + 1)].rearrange("p z j (g i) -> p z g j i", i=4),
+                )
+                nc.vector.quantize_mx(out=codes[i][:, cols].bitcast(FP8X4), scales=planes[i][:, cols], in_=grouped)
 
         def product(m, c, into, via, cuts=(0, 512, 1024)):
             rows[m, c] = into
@@ -123,7 +123,7 @@ def tile_picked_edgecv_relu_p_kernel(
                         lhsT=codes[i][:, col : col + P].bitcast(FP8X4),
                         lhsT_scale=planes[i][:, col : col + P],
                         rhs=xg[z][:, s0:s1].bitcast(FP8X4),
-                        rhs_scale=xsg[4 * z : P, s0:s1],
+                        rhs_scale=xsg[s0 // BANK][4 * z : P, s0 % BANK : s0 % BANK + s1 - s0],
                         start=(z == 0),
                         stop=(z == PASSES - 1),
                     )
@@ -132,29 +132,29 @@ def tile_picked_edgecv_relu_p_kernel(
         zt = sb([P, 4, 2, P, 2], BF16, "zt")
         far, mid = {}, {}
 
-        def neighbours(c, b0=0, b1=4, first=None, second=None):
+        def neighbours(c, b0=0, b1=4, first=None, second=None, third=None):
             n = P * (b1 - b0)
             g1 = sb([P, n], F32, "g1_%d%d" % (c, b0))[:] if first is None else first
             g2 = sb([P, n], F32, "g2_%d%d" % (c, b0))[:] if second is None else second
-            gm = sb([P, n], F32, "gm_%d%d" % (c, b0))
+            gm = sb([P, n], F32, "gm_%d%d" % (c, b0))[:] if third is None else third
             nc.vector.tensor_copy(g1, rows["e", c].indirect(pos1_t[:, 8 * b0 : 8 * b1]))
             nc.vector.tensor_copy(g2, rows["e", c].indirect(pos2_t[:, 8 * b0 : 8 * b1]))
-            nc.vector.tensor_tensor(gm[:], g1, g2, MAX)
+            nc.vector.tensor_tensor(gm, g1, g2, MAX)
             for b in range(b0, b1):
                 far[c, b] = gm[:, P * (b - b0) : P * (b - b0 + 1)]
 
-        def centres(c):
-            gc = sb([P, V], F32, "gc_%d" % c)
-            nc.vector.tensor_copy(gc[:], rows["y", c].indirect(cen_t[:]))
-            for b in range(4):
-                mid[c, b] = gc[:, P * b : P * (b + 1)]
+        def centres(c, b0=0, b1=4, into=None):
+            gc = sb([P, P * (b1 - b0)], F32, "gc_%d%d" % (c, b0))[:] if into is None else into
+            nc.vector.tensor_copy(gc, rows["y", c].indirect(cen_t[:, 8 * b0 : 8 * b1]))
+            for b in range(b0, b1):
+                mid[c, b] = gc[:, P * (b - b0) : P * (b - b0 + 1)]
 
         def edges(c, via, b0=0, b1=4):
             n = P * (b1 - b0)
             acc = banks[via]
             for b in range(b0, b1):
                 cols = slice(P * (b - b0), P * (b - b0 + 1))
-                first, second = mid[c, b], far[c, b]
+                first, second = (far[c, b], mid[c, b]) if c == 3 else (mid[c, b], far[c, b])
                 nc.tensor.matmul(acc[:, cols], first, ident[:], start=True, stop=False, is_transpose=True)
                 nc.tensor.matmul(acc[:, cols], second, ident[:], start=False, stop=True, is_transpose=True)
             sums = acc[:, :n].rearrange("v (b q u e) -> v b u q e", q=32, u=2, e=2)
@@ -209,16 +209,15 @@ def tile_picked_edgecv_relu_p_kernel(
             return stage[i][:, UNIT : UNIT + UNIT // 2]
 
         sc, vc = nc.scalar.copy, nc.vector.tensor_copy
-        xg = [sb([P, S], U32, "xg0")]
-        nc.vector.tensor_copy(xg[0][:], x_win[0][:].indirect(offs_t[:]))
-        xsg = sb([P, S], U8, "xsg")
-        nc.vector.tensor_copy(xsg[:], xs_win[:].indirect(offs_t[:]))
-        quantise_w(0, fresh(UNIT // 2, "wb_0"), "xs_win")
-        xg.append(sb([P, S], U32, "xg1", "wb_0"))
-        for a, b in ((0, 512), (512, 768), (768, 1024)):
-            nc.vector.tensor_copy(xg[1][:, a:b], x_win[1][:].indirect(offs_t[:, a // 16 : b // 16]))
+        xg = [sb([P, S], U32, "xg0"), sb([P, S], U32, "xg1")]
+        for z in range(PASSES):
+            nc.vector.tensor_copy(xg[z][:], x_win[z][:].indirect(offs_t[:]))
+        quantise_w(0, fresh(UNIT // 2, "wb_0"), "x_window1")
+        xsg = [sb([P, BANK], U8, "xsg0"), sb([P, BANK], U8, "xsg1", "wb_0")]
+        for h in range(2):
+            nc.vector.tensor_copy(xsg[h][:], xs_win[:].indirect(offs_t[:, 32 * h : 32 * (h + 1)]))
         slot = sb([P, UNIT], F32, "slot")
-        quantise_w(1, slot[:, 256:768], "x_window1")
+        quantise_w(1, slot[:, 256:768], "xs_win")
         quantise_w(2, slot[:, 256:768], None, vc)
         product("e", 0, front(1), (0, 1, 2), (0, 512, 768, 1024))
         neighbours(0, first=front(2)[:, :512], second=slot[:, :512])
@@ -232,22 +231,23 @@ def tile_picked_edgecv_relu_p_kernel(
         neighbours(2, second=cast[6])
         quantise_w(7, half(6))
         product("y", 0, front(7), (7, 0))
+        product("y", 1, back(7), (1, 2))
         centres(0)
-        product("y", 1, back(7), (1, 7))
         centres(1)
         product("y", 2, front(0), (3, 4))
         centres(2)
+        product("e", 3, front(6), (2, 3))
+        last = fresh(V, "g1_3")
+        neighbours(3, first=last)
         product("y", 3, front(4), (5, 6))
-        centres(3)
-        product("e", 3, front(6), (3, 4))
-        edges(0, 5)
-        edges(1, 6)
+        edges(0, 4)
+        edges(1, 2)
         edges(2, 3)
-        firsts = [fresh(P, "g1_3%d" % i) for i in range(2)]
-        second = fresh(P, "g2_3")
-        for b in range(4):
-            neighbours(3, b, b + 1, firsts[b % 2], second)
-            edges(3, (7, 1, 4, 0)[b], b, b + 1)
-            turn(b, b + 1, (4, 0, 2, 7)[b], (sc, sc, sc, sc)[b])
-        for b in range(4):
-            project(b, b + 1, (5, 6, 3, 1)[b], (vc, vc, vc, vc)[b])
+        pieces = ((0, 1), (1, 2), (2, 3), (3, 4))
+        for i, (b0, b1) in enumerate(pieces):
+            centres(3, b0, b1, None)
+            edges(3, (0, 7, 1, 5)[i], b0, b1)
+        for i, (b0, b1) in enumerate(pieces):
+            turn(b0, b1, (6, 4, 2, 3)[i], (sc, sc, sc, sc)[i])
+        for i, (b0, b1) in enumerate(pieces):
+            project(b0, b1, (0, 7, 1, 5)[i], (vc, vc, vc, vc)[i])

@@ -18,236 +18,246 @@ RELU = mybir.ActivationFunctionType.Relu
 MAX = mybir.AluOpType.max
 
 P = 128
-PASSES = 2
+PACK = 4
+K_PASS = P * PACK
+PASSES = K // K_PASS
+GROUPS = V // P
 BANK = 512
-UNIT = 1024
-
-UNITS = (
-    ("e", 0, 1, (0, 1)),
-    ("e", 1, 1, (0, 1)),
-    ("e", 2, 2, (0,)),
-    ("e", 2, 2, (1,)),
-    ("y", 0, 2, (0,)),
-    ("y", 0, 2, (1,)),
-    ("y", 2, 2, (0,)),
-    ("y", 2, 2, (1,)),
-)
+PER_COLUMN = 16
+HALVES = (0, BANK, S)
+FIRST_CUTS = (0, BANK, BANK + BANK // 2, S)
 
 
 def tile_picked_edgecv_relu_p_kernel(
     tc, x_words, x_scales, w1, w2, w3_words, w3_scales, offs, cen, pos1, pos2, out
 ):
     nc = tc.nc
+    on_scalar, on_vector = nc.scalar.copy, nc.vector.tensor_copy
     with ExitStack() as ctx:
         keep = ctx.enter_context(tc.tile_pool(name="keep", bufs=1))
         psum = ctx.enter_context(tc.psum_pool(name="psum", bufs=1))
         banks = [psum.tile([P, BANK], F32, name="bank%d" % b) for b in range(8)]
 
-        def sb(shape, dtype, name, tag=None):
+        def new_tile(shape, dtype, name, tag=None):
             return keep.tile(shape, dtype, name=name, tag=tag or name, align_bytes=64)
 
+        def room(width, name, over):
+            return new_tile([P, width], F32, name)[:] if over is None else over[:, :width]
+
         def load_list(src, name):
-            t = keep.tile(list(src.shape), U16, name=name)
-            nc.sync.dma_start(t[:], src)
-            return t
+            held = keep.tile(list(src.shape), U16, name=name)
+            nc.sync.dma_start(held[:], src)
+            return held
 
         weights = {"y": w1, "e": w2}
-        stage = [sb([P, 2 * UNIT], F32, "raw_%d" % i) for i in range(len(UNITS))]
-        raw, where = {}, {}
+        staged = {}
 
-        def load_w(i):
-            m, c0, width, zs = UNITS[i]
-            raw[i] = stage[i][:].rearrange("p (z j c) -> p z j c", z=len(zs), j=4)[:, :, :, : P * width]
-            for a, z in enumerate(zs):
-                src = weights[m][512 * z : 512 * (z + 1), P * c0 : P * (c0 + width)]
-                nc.sync.dma_start(raw[i][:, a], src.rearrange("(p j) c -> p j c", j=4))
-                for c in range(width):
-                    where[m, c0 + c, z] = (i, P * (a * width + c))
+        def load_w(m, c):
+            staged[m, c] = new_tile([P, PASSES * PACK * P], F32, "raw_%s%d" % (m, c))[:]
+            by_pass = staged[m, c].rearrange("p (z t i) -> p z t i", z=PASSES, t=PACK)
+            for z in range(PASSES):
+                src = weights[m][K_PASS * z : K_PASS * (z + 1), P * c : P * (c + 1)]
+                nc.sync.dma_start(by_pass[:, z], src.rearrange("(p t) i -> p t i", t=PACK))
 
-        x_win = [sb([P, T], U32, "x_window%d" % z) for z in range(PASSES)]
+        x_window = {}
 
         def load_x(z):
-            nc.sync.dma_start(x_win[z][:].bitcast(I32), x_words[z].rearrange("p c r -> p (c r)").bitcast(I32))
+            x_window[z] = new_tile([P, T], U32, "x_window%d" % z)
+            nc.sync.dma_start(x_window[z][:].bitcast(I32), x_words[z].rearrange("p c t -> p (c t)").bitcast(I32))
 
-        xs_win = sb([P, T], U8, "xs_win")
-        nc.gpsimd.memset(xs_win[:].bitcast(I32), 0)
+        scale_window = new_tile([P, T], U8, "xs_win")
+        nc.gpsimd.memset(scale_window[:].bitcast(I32), 0)
         for q in range(4):
             nc.sync.dma_start(
-                xs_win[32 * q : 32 * q + 8, :].bitcast(I32), x_scales[:, 4 * q : 4 * q + 4, :].bitcast(I32)
+                scale_window[32 * q : 32 * q + 4 * PASSES, :].bitcast(I32), x_scales[:, 4 * q : 4 * q + 4, :].bitcast(I32)
             )
+        w3_codes = new_tile([P, 2 * N], U8, "w3w")
         offs_t = load_list(offs, "offs_t")
         load_x(0)
         pos1_t = load_list(pos1, "pos1_t")
-        pos2_t = load_list(pos2, "pos2_t")
-        load_x(1)
-        load_w(0)
         cen_t = load_list(cen, "cen_t")
-        for i in range(1, len(UNITS)):
-            load_w(i)
-        w3w = sb([P, 2 * N], U8, "w3w")
-        nc.sync.dma_start(w3w[:], w3_words[0])
-        w3s = sb([P, N], U8, "w3s")
-        nc.gpsimd.memset(w3s[:].bitcast(I32), 0)
+        load_x(1)
+        load_w("e", 0)
+        pos2_t = load_list(pos2, "pos2_t")
+        load_w("e", 1)
+        load_w("y", 0)
+        load_w("y", 1)
+        nc.sync.dma_start(w3_codes[:], w3_words[0])
+        load_w("e", 2)
+        load_w("e", 3)
+        load_w("y", 2)
+        load_w("y", 3)
+        w3_plane = new_tile([P, N], U8, "w3s")
+        nc.gpsimd.memset(w3_plane[:].bitcast(I32), 0)
         for q in range(4):
             nc.sync.dma_start(
-                w3s[32 * q : 32 * q + 4, :].bitcast(I32), w3_scales[0, 4 * q : 4 * q + 4, :].bitcast(I32)
+                w3_plane[32 * q : 32 * q + 4, :].bitcast(I32), w3_scales[0, 4 * q : 4 * q + 4, :].bitcast(I32)
             )
-        ident = sb([P, P], F32, "ident")
-        make_identity(nc, ident[:])
+        ident_made = new_tile([P, P], F32, "ident0")
+        make_identity(nc, ident_made[:])
+        ident = new_tile([P, P], F32, "ident")
+        nc.scalar.activation(ident[:], ident_made[:], RELU)
 
-        codes, planes, cast, rows = {}, {}, {}, {}
+        x_picked = {0: new_tile([P, S], U32, "xg0")}
+        scales_picked = {}
+        rounded, codes, planes, rows = {}, {}, {}, {}
+        z_turned = new_tile([P, GROUPS, 2, P, 2], BF16, "zt")
+        picked = {}
+        z_ready = {}
 
-        def quantise_w(i, into, codes_tag=None, copy=nc.scalar.copy, parts=1):
-            cast[i] = into
-            codes[i] = sb([P, 2 * P], U32, "wq_%d" % i, codes_tag)
-            planes[i] = sb([P, 2 * P], U8, "ws_%d" % i)
-            zs = raw[i].shape[1] // parts
-            for h in range(parts):
-                grouped = into.bitcast(BF16)[:, UNIT // parts * h : UNIT // parts * (h + 1)]
-                cols = slice(2 * P // parts * h, 2 * P // parts * (h + 1))
-                copy(
-                    grouped.rearrange("p (z g i j) -> p z g j i", z=zs, i=4, j=4),
-                    raw[i][:, zs * h : zs * (h + 1)].rearrange("p z j (g i) -> p z g j i", i=4),
+        def entries(lst, first, last):
+            return lst[:, first // PER_COLUMN : last // PER_COLUMN]
+
+        def gather_scales(cuts, tag):
+            first = cuts[0]
+            scales_picked[first] = new_tile([P, BANK], U8, "xsg_%d" % first, tag)
+            for a, b in zip(cuts, cuts[1:]):
+                nc.vector.tensor_copy(
+                    scales_picked[first][:, a - first : b - first], scale_window[:].indirect(entries(offs_t, a, b))
                 )
-                nc.vector.quantize_mx(out=codes[i][:, cols].bitcast(FP8X4), scales=planes[i][:, cols], in_=grouped)
 
-        def product(m, c, into, via, cuts=(0, 512, 1024)):
-            rows[m, c] = into
-            for h in range(len(cuts) - 1):
-                s0, s1 = cuts[h], cuts[h + 1]
-                acc = banks[via[h]][:, : s1 - s0]
+        def quantise_w(m, c, copy, over=None):
+            rounded[m, c] = room(PASSES * PACK * P // 2, "wb_%s%d" % (m, c), over)
+            grouped = rounded[m, c].bitcast(BF16).rearrange("p (z i t) -> p z i t", z=PASSES, t=PACK)
+            copy(
+                grouped.rearrange("p z (a b) t -> p z a t b", b=4),
+                staged[m, c].rearrange("p (z t i) -> p z t i", z=PASSES, t=PACK).rearrange("p z t (a b) -> p z a t b", b=4),
+            )
+            codes[m, c] = new_tile([P, PASSES * P], U32, "wq_%s%d" % (m, c))
+            planes[m, c] = new_tile([P, PASSES * P], U8, "ws_%s%d" % (m, c))
+            nc.vector.quantize_mx(
+                out=codes[m, c][:].bitcast(FP8X4),
+                scales=planes[m, c][:],
+                in_=grouped.rearrange("p z i t -> p (z i t)"),
+            )
+
+        def product(m, c, via, over=None, cuts=HALVES):
+            rows[m, c] = room(S, "rows_%s%d" % (m, c), over)
+            for b, first, last in zip(via, cuts, cuts[1:]):
+                half = first // BANK * BANK
                 for z in range(PASSES):
-                    i, col = where[m, c, z]
                     nc.tensor.matmul_mx(
-                        out=acc,
-                        lhsT=codes[i][:, col : col + P].bitcast(FP8X4),
-                        lhsT_scale=planes[i][:, col : col + P],
-                        rhs=xg[z][:, s0:s1].bitcast(FP8X4),
-                        rhs_scale=xsg[s0 // BANK][4 * z : P, s0 % BANK : s0 % BANK + s1 - s0],
+                        out=banks[b][:, : last - first],
+                        lhsT=codes[m, c][:, P * z : P * (z + 1)].bitcast(FP8X4),
+                        lhsT_scale=planes[m, c][:, P * z : P * (z + 1)],
+                        rhs=x_picked[z][:, first:last].bitcast(FP8X4),
+                        rhs_scale=scales_picked[half][4 * z : P, first - half : last - half],
                         start=(z == 0),
                         stop=(z == PASSES - 1),
                     )
-                nc.scalar.copy(rows[m, c][:, s0:s1], acc)
+                nc.scalar.copy(rows[m, c][:, first:last], banks[b][:, : last - first])
 
-        zt = sb([P, 4, 2, P, 2], BF16, "zt")
-        far, mid = {}, {}
+        whole = {}
 
-        def neighbours(c, b0=0, b1=4, first=None, second=None, third=None):
-            n = P * (b1 - b0)
-            g1 = sb([P, n], F32, "g1_%d%d" % (c, b0))[:] if first is None else first
-            g2 = sb([P, n], F32, "g2_%d%d" % (c, b0))[:] if second is None else second
-            gm = sb([P, n], F32, "gm_%d%d" % (c, b0))[:] if third is None else third
-            nc.vector.tensor_copy(g1, rows["e", c].indirect(pos1_t[:, 8 * b0 : 8 * b1]))
-            nc.vector.tensor_copy(g2, rows["e", c].indirect(pos2_t[:, 8 * b0 : 8 * b1]))
-            nc.vector.tensor_tensor(gm, g1, g2, MAX)
-            for b in range(b0, b1):
-                far[c, b] = gm[:, P * (b - b0) : P * (b - b0 + 1)]
+        def note(kind, c, groups, values):
+            whole[kind, c] = values
+            for n, g in enumerate(groups):
+                picked[kind, c, g] = values[:, P * n : P * (n + 1)]
 
-        def centres(c, b0=0, b1=4, into=None):
-            gc = sb([P, P * (b1 - b0)], F32, "gc_%d%d" % (c, b0))[:] if into is None else into
-            nc.vector.tensor_copy(gc, rows["y", c].indirect(cen_t[:, 8 * b0 : 8 * b1]))
-            for b in range(b0, b1):
-                mid[c, b] = gc[:, P * (b - b0) : P * (b - b0 + 1)]
+        def gather(kind, c, groups=range(GROUPS), over=None):
+            m, lst = {"1": ("e", pos1_t), "2": ("e", pos2_t), "cen": ("y", cen_t)}[kind]
+            values = room(P * len(groups), "g%s_%d%d" % (kind, c, groups.start), over)
+            nc.vector.tensor_copy(values, rows[m, c].indirect(entries(lst, P * groups.start, P * groups.stop)))
+            note(kind, c, groups, values)
 
-        def edges(c, via, b0=0, b1=4):
-            n = P * (b1 - b0)
-            acc = banks[via]
-            for b in range(b0, b1):
-                cols = slice(P * (b - b0), P * (b - b0 + 1))
-                first, second = (far[c, b], mid[c, b]) if c == 3 else (mid[c, b], far[c, b])
-                nc.tensor.matmul(acc[:, cols], first, ident[:], start=True, stop=False, is_transpose=True)
-                nc.tensor.matmul(acc[:, cols], second, ident[:], start=False, stop=True, is_transpose=True)
-            sums = acc[:, :n].rearrange("v (b q u e) -> v b u q e", q=32, u=2, e=2)
-            if b1 - b0 == 1:
-                nc.scalar.activation(zt[:, b0, :, 32 * c : 32 * (c + 1), :], sums[:, 0], RELU)
+        def larger(c, over):
+            values = room(V, "gm_%d" % c, over)
+            nc.vector.tensor_tensor(values, whole["1", c], whole["2", c], MAX)
+            note("max", c, range(GROUPS), values)
+
+        def edges(c, b, groups=range(GROUPS)):
+            for n, g in enumerate(groups):
+                block = banks[b][:, P * n : P * (n + 1)]
+                nc.tensor.matmul(block, picked["cen", c, g], ident[:], start=True, stop=False, is_transpose=True)
+                nc.tensor.matmul(block, picked["max", c, g], ident[:], start=False, stop=True, is_transpose=True)
+            quarter = slice(P // PACK * c, P // PACK * (c + 1))
+            sums = banks[b][:, : P * len(groups)].rearrange("v (g r u d) -> v g u r d", r=P // PACK, u=2, d=2)
+            if len(groups) == 1:
+                nc.scalar.activation(z_turned[:, groups.start, :, quarter, :], sums[:, 0], RELU)
             else:
                 for u in range(2):
-                    nc.scalar.activation(zt[:, b0:b1, u, 32 * c : 32 * (c + 1), :], sums[:, :, u], RELU)
+                    nc.scalar.activation(z_turned[:, groups.start : groups.stop, u, quarter, :], sums[:, :, u], RELU)
 
-        zb = {}
+        def turn(g, b, copy):
+            for u in range(2):
+                pairs = z_turned[:, g, u].rearrange("v p d -> v (p d)").bitcast(F32)
+                nc.tensor.transpose(banks[b][:, P * u : P * (u + 1)], pairs, ident[:])
+            z_ready[g] = new_tile([P, P, PACK], BF16, "zb%d" % g)
+            copy(z_ready[g][:].bitcast(F32), banks[b][:, : 2 * P].rearrange("p (u v) -> p v u", u=2))
 
-        def turn(b0, b1, via, copy):
-            n = P * (b1 - b0)
-            turned = banks[via]
-            for b in range(b0, b1):
-                for u in range(2):
-                    pairs = zt[:, b, u].rearrange("v q e -> v (q e)").bitcast(F32)
-                    at = n * u + P * (b - b0)
-                    nc.tensor.transpose(turned[:, at : at + P], pairs, ident[:])
-            zb[b0] = sb([P, n, 4], BF16, "zb%d" % b0)
-            copy(zb[b0][:].bitcast(F32), turned[:, : 2 * n].rearrange("p (u v) -> p v u", u=2))
-
-        def project(b0, b1, via, copy):
-            n = P * (b1 - b0)
-            zq = sb([P, n], U32, "zq%d" % b0)
-            zs = sb([P, n], U8, "zs%d" % b0)
-            nc.vector.quantize_mx(out=zq[:].bitcast(FP8X4), scales=zs[:], in_=zb[b0][:].rearrange("p v j -> p (v j)"))
-            acc = banks[via][:, :n]
+        def project(g, b):
+            z_codes = new_tile([P, P], U32, "zq%d" % g)
+            z_plane = new_tile([P, P], U8, "zs%d" % g)
+            nc.vector.quantize_mx(
+                out=z_codes[:].bitcast(FP8X4), scales=z_plane[:], in_=z_ready[g][:].rearrange("p v t -> p (v t)")
+            )
             nc.tensor.matmul_mx(
-                out=acc,
-                lhsT=w3w[:].bitcast(FP4X4),
-                lhsT_scale=w3s[:],
-                rhs=zq[:].bitcast(FP8X4),
-                rhs_scale=zs[:],
+                out=banks[b][:, :P],
+                lhsT=w3_codes[:].bitcast(FP4X4),
+                lhsT_scale=w3_plane[:],
+                rhs=z_codes[:].bitcast(FP8X4),
+                rhs_scale=z_plane[:],
                 start=True,
                 stop=True,
             )
-            res = sb([P, n], F32, "res_sb%d" % b0)
-            copy(res[:], acc)
-            nc.sync.dma_start(out[:, P * b0 : P * b1], res[:])
+            result = new_tile([P, P], F32, "res_sb%d" % g)
+            nc.scalar.copy(result[:], banks[b][:, :P])
+            nc.sync.dma_start(out[:, P * g : P * (g + 1)], result[:])
 
-        def fresh(n, name):
-            return sb([P, n], F32, name)[:]
+        nc.vector.tensor_copy(x_picked[0][:], x_window[0][:].indirect(offs_t[:]))
+        x_picked[1] = new_tile([P, S], U32, "xg1_0")
+        nc.vector.tensor_copy(x_picked[1][:], x_window[1][:].indirect(offs_t[:]))
+        gather_scales(FIRST_CUTS[:2], "x_window0")
+        quantise_w("e", 1, on_scalar)
+        quantise_w("e", 0, on_scalar)
+        gather_scales(FIRST_CUTS[1:], "raw_e0")
 
-        def front(i):
-            return stage[i][:, :UNIT]
+        product("e", 0, (6, 7, 5), cuts=FIRST_CUTS)
+        product("e", 1, (6, 5))
+        quantise_w("y", 0, on_vector, over=rounded["e", 1])
+        quantise_w("y", 1, on_scalar)
+        product("y", 0, (2, 5), over=staged["y", 0])
+        quantise_w("e", 2, on_scalar)
+        gather("2", 1)
+        gather("1", 1)
+        product("e", 2, (5, 7))
+        quantise_w("e", 3, on_scalar)
+        larger(1, staged["e", 2])
+        gather("cen", 0)
+        gather("2", 0)
+        gather("1", 0)
+        product("y", 1, (2, 1))
+        quantise_w("y", 2, on_vector, over=rounded["e", 2])
+        gather("1", 2)
+        gather("2", 2)
+        larger(0, staged["y", 1])
+        quantise_w("y", 3, on_scalar, over=rounded["y", 2])
+        product("y", 2, (3, 0), over=staged["e", 3])
+        product("e", 3, (1, 2))
+        gather("cen", 2)
+        edges(0, 7)
+        gather("2", 3, over=rounded["y", 3])
+        gather("cen", 1)
+        gather("1", 3)
+        larger(2, staged["y", 3])
+        edges(1, 6)
+        larger(3, staged["y", 2])
+        product("y", 3, (6, 0))
 
-        def back(i):
-            return stage[i][:, UNIT:]
-
-        def half(i):
-            return stage[i][:, UNIT : UNIT + UNIT // 2]
-
-        sc, vc = nc.scalar.copy, nc.vector.tensor_copy
-        xg = [sb([P, S], U32, "xg0"), sb([P, S], U32, "xg1")]
-        for z in range(PASSES):
-            nc.vector.tensor_copy(xg[z][:], x_win[z][:].indirect(offs_t[:]))
-        quantise_w(0, fresh(UNIT // 2, "wb_0"), "x_window1")
-        xsg = [sb([P, BANK], U8, "xsg0"), sb([P, BANK], U8, "xsg1", "wb_0")]
-        for h in range(2):
-            nc.vector.tensor_copy(xsg[h][:], xs_win[:].indirect(offs_t[:, 32 * h : 32 * (h + 1)]))
-        slot = sb([P, UNIT], F32, "slot")
-        quantise_w(1, slot[:, 256:768], "xs_win")
-        quantise_w(2, slot[:, 256:768], None, vc)
-        product("e", 0, front(1), (0, 1, 2), (0, 512, 768, 1024))
-        neighbours(0, first=front(2)[:, :512], second=slot[:, :512])
-        quantise_w(3, half(2))
-        product("e", 1, front(3), (3, 4))
-        quantise_w(4, half(3))
-        neighbours(1, second=cast[4])
-        quantise_w(5, half(4))
-        product("e", 2, front(5), (5, 6))
-        quantise_w(6, half(5))
-        neighbours(2, second=cast[6])
-        quantise_w(7, half(6))
-        product("y", 0, front(7), (7, 0))
-        product("y", 1, back(7), (1, 2))
-        centres(0)
-        centres(1)
-        product("y", 2, front(0), (3, 4))
-        centres(2)
-        product("e", 3, front(6), (2, 3))
-        last = fresh(V, "g1_3")
-        neighbours(3, first=last)
-        product("y", 3, front(4), (5, 6))
-        edges(0, 4)
-        edges(1, 2)
-        edges(2, 3)
-        pieces = ((0, 1), (1, 2), (2, 3), (3, 4))
-        for i, (b0, b1) in enumerate(pieces):
-            centres(3, b0, b1, None)
-            edges(3, (0, 7, 1, 5)[i], b0, b1)
-        for i, (b0, b1) in enumerate(pieces):
-            turn(b0, b1, (6, 4, 2, 3)[i], (sc, sc, sc, sc)[i])
-        for i, (b0, b1) in enumerate(pieces):
-            project(b0, b1, (0, 7, 1, 5)[i], (vc, vc, vc, vc)[i])
+        gather("cen", 3, range(2, 3))
+        edges(2, 0)
+        edges(3, 1, range(2, 3))
+        gather("cen", 3, range(3, 4), over=rounded["e", 3])
+        gather("cen", 3, range(0, 1))
+        gather("cen", 3, range(1, 2))
+        edges(3, 7, range(3, 4))
+        turn(3, 2, on_vector)
+        edges(3, 5, range(0, 1))
+        edges(3, 6, range(1, 2))
+        turn(2, 5, on_scalar)
+        turn(0, 7, on_scalar)
+        project(2, 7)
+        project(0, 5)
+        turn(1, 4, on_scalar)
+        project(3, 0)
+        project(1, 1)

@@ -16,14 +16,18 @@ FP8X4 = mybir.dt.float8_e4m3fn_x4
 FP4X4 = mybir.dt.float4_e2m1fn_x4
 RELU = mybir.ActivationFunctionType.Relu
 MAX = mybir.AluOpType.max
+MULT = mybir.AluOpType.mult
+ADD = mybir.AluOpType.add
 
 P = 128
 PACK = 4
 K_PASS = P * PACK
 PASSES = K // K_PASS
+TILES = H // P
 GROUPS = V // P
 BANK = 512
 PER_COLUMN = 16
+LAP = 16
 HALVES = (0, BANK, S)
 FIRST_CUTS = (0, BANK, BANK + BANK // 2, S)
 
@@ -32,7 +36,6 @@ def tile_picked_edgecv_relu_p_kernel(
     tc, x_words, x_scales, w1, w2, w3_words, w3_scales, offs, cen, pos1, pos2, out
 ):
     nc = tc.nc
-    on_scalar, on_vector = nc.scalar.copy, nc.vector.tensor_copy
     with ExitStack() as ctx:
         keep = ctx.enter_context(tc.tile_pool(name="keep", bufs=1))
         psum = ctx.enter_context(tc.psum_pool(name="psum", bufs=1))
@@ -41,19 +44,27 @@ def tile_picked_edgecv_relu_p_kernel(
         def new_tile(shape, dtype, name, tag=None):
             return keep.tile(shape, dtype, name=name, tag=tag or name, align_bytes=64)
 
-        def room(width, name, over):
-            return new_tile([P, width], F32, name)[:] if over is None else over[:, :width]
-
         def load_list(src, name):
             held = keep.tile(list(src.shape), U16, name=name)
             nc.sync.dma_start(held[:], src)
             return held
 
         weights = {"y": w1, "e": w2}
-        staged = {}
+        strip = [new_tile([P, 4 * V], F32, "strip%d" % c) for c in range(TILES)]
+        e_strip = new_tile([P, TILES * V], F32, "e_strip")
+        staged, rounded, behind, beside = {}, {}, {}, {}
+        for c in range(TILES):
+            first = (V - LAP) * c
+            rounded["e", c] = e_strip[:, first : first + V]
+            behind["e", c] = e_strip[:, max(first - V + LAP, 0) : first + LAP]
+            beside["e", c] = strip[c][:, :V]
+            staged["e", c] = strip[c][:, V - LAP : V - LAP + S]
+            rounded["y", c] = strip[c][:, 2 * V : 3 * V]
+            behind["y", c] = strip[c][:, 3 * V - LAP : 4 * V - LAP]
+            staged["y", c] = new_tile([P, S], F32, "raw_y%d" % c)[:]
+            beside["y", c] = staged["y", c][:, :V]
 
         def load_w(m, c):
-            staged[m, c] = new_tile([P, PASSES * PACK * P], F32, "raw_%s%d" % (m, c))[:]
             by_pass = staged[m, c].rearrange("p (z t i) -> p z t i", z=PASSES, t=PACK)
             for z in range(PASSES):
                 src = weights[m][K_PASS * z : K_PASS * (z + 1), P * c : P * (c + 1)]
@@ -66,27 +77,26 @@ def tile_picked_edgecv_relu_p_kernel(
             nc.sync.dma_start(x_window[z][:].bitcast(I32), x_words[z].rearrange("p c t -> p (c t)").bitcast(I32))
 
         scale_window = new_tile([P, T], U8, "xs_win")
-        nc.gpsimd.memset(scale_window[:].bitcast(I32), 0)
+        nc.vector.memset(scale_window[:].bitcast(I32), 0)
+        offs_t = load_list(offs, "offs_t")
         for q in range(4):
             nc.sync.dma_start(
                 scale_window[32 * q : 32 * q + 4 * PASSES, :].bitcast(I32), x_scales[:, 4 * q : 4 * q + 4, :].bitcast(I32)
             )
-        w3_codes = new_tile([P, 2 * N], U8, "w3w")
-        offs_t = load_list(offs, "offs_t")
         load_x(0)
-        pos1_t = load_list(pos1, "pos1_t")
-        cen_t = load_list(cen, "cen_t")
-        load_x(1)
         load_w("e", 0)
+        load_x(1)
+        load_w("y", 0)
+        pos1_t = load_list(pos1, "pos1_t")
         pos2_t = load_list(pos2, "pos2_t")
         load_w("e", 1)
-        load_w("y", 0)
+        cen_t = load_list(cen, "cen_t")
         load_w("y", 1)
+        for c in range(2, TILES):
+            load_w("e", c)
+            load_w("y", c)
+        w3_codes = new_tile([P, 2 * N], U8, "w3w")
         nc.sync.dma_start(w3_codes[:], w3_words[0])
-        load_w("e", 2)
-        load_w("e", 3)
-        load_w("y", 2)
-        load_w("y", 3)
         w3_plane = new_tile([P, N], U8, "w3s")
         nc.gpsimd.memset(w3_plane[:].bitcast(I32), 0)
         for q in range(4):
@@ -98,78 +108,84 @@ def tile_picked_edgecv_relu_p_kernel(
         ident = new_tile([P, P], F32, "ident")
         nc.scalar.activation(ident[:], ident_made[:], RELU)
 
-        x_picked = {0: new_tile([P, S], U32, "xg0")}
-        scales_picked = {}
-        rounded, codes, planes, rows = {}, {}, {}, {}
-        z_turned = new_tile([P, GROUPS, 2, P, 2], BF16, "zt")
-        picked = {}
-        z_ready = {}
-
         def entries(lst, first, last):
             return lst[:, first // PER_COLUMN : last // PER_COLUMN]
 
-        def gather_scales(cuts, tag):
-            first = cuts[0]
-            scales_picked[first] = new_tile([P, BANK], U8, "xsg_%d" % first, tag)
-            for a, b in zip(cuts, cuts[1:]):
-                nc.vector.tensor_copy(
-                    scales_picked[first][:, a - first : b - first], scale_window[:].indirect(entries(offs_t, a, b))
+        scales_picked, x_picked = {}, {}
+        for half in (0, BANK):
+            scales_picked[half] = new_tile([P, BANK], U8, "xsg_%d" % half)
+            nc.vector.tensor_copy(scales_picked[half][:], scale_window[:].indirect(entries(offs_t, half, half + BANK)))
+        x_first = new_tile([P, S], U32, "xg0")
+        nc.vector.tensor_copy(x_first[:], x_window[0][:].indirect(offs_t[:]))
+        for half in (0, BANK):
+            x_picked[0, half] = x_first[:, half : half + BANK]
+
+        code_tiles = [new_tile([P, PASSES * P], U32, "codes%d" % z, tag="x_window%d" % z) for z in range(PASSES)]
+        plane_tiles = [new_tile([P, PASSES * P], U8, "plane%d" % z) for z in range(PASSES)]
+        now = {}
+        z_turned = new_tile([P, GROUPS, 2, P, 2], BF16, "zt")
+        rows, picked, z_ready = {}, {}, {}
+
+        def quantise_w(m, c):
+            dst, src = rounded[m, c].bitcast(BF16), staged[m, c]
+            slot = int(m == "e" and c > 0)
+            now["codes"], now["plane"] = code_tiles[slot], plane_tiles[slot]
+            if slot:
+                nc.gpsimd.tensor_scalar(
+                    dst.rearrange("p (z i t) -> p z i t", z=PASSES, t=PACK),
+                    src.rearrange("p (z t i) -> p z i t", z=PASSES, t=PACK),
+                    1.0,
+                    0.0,
+                    MULT,
+                    ADD,
                 )
-
-        def quantise_w(m, c, copy, over=None):
-            rounded[m, c] = room(PASSES * PACK * P // 2, "wb_%s%d" % (m, c), over)
-            grouped = rounded[m, c].bitcast(BF16).rearrange("p (z i t) -> p z i t", z=PASSES, t=PACK)
-            copy(
-                grouped.rearrange("p z (a b) t -> p z a t b", b=4),
-                staged[m, c].rearrange("p (z t i) -> p z t i", z=PASSES, t=PACK).rearrange("p z t (a b) -> p z a t b", b=4),
-            )
-            codes[m, c] = new_tile([P, PASSES * P], U32, "wq_%s%d" % (m, c))
-            planes[m, c] = new_tile([P, PASSES * P], U8, "ws_%s%d" % (m, c))
-            nc.vector.quantize_mx(
-                out=codes[m, c][:].bitcast(FP8X4),
-                scales=planes[m, c][:],
-                in_=grouped.rearrange("p z i t -> p (z i t)"),
-            )
-
-        def product(m, c, via, over=None, cuts=HALVES):
-            rows[m, c] = room(S, "rows_%s%d" % (m, c), over)
-            for b, first, last in zip(via, cuts, cuts[1:]):
-                half = first // BANK * BANK
-                for z in range(PASSES):
-                    nc.tensor.matmul_mx(
-                        out=banks[b][:, : last - first],
-                        lhsT=codes[m, c][:, P * z : P * (z + 1)].bitcast(FP8X4),
-                        lhsT_scale=planes[m, c][:, P * z : P * (z + 1)],
-                        rhs=x_picked[z][:, first:last].bitcast(FP8X4),
-                        rhs_scale=scales_picked[half][4 * z : P, first - half : last - half],
-                        start=(z == 0),
-                        stop=(z == PASSES - 1),
+            else:
+                parts = PASSES if (m, c) == ("e", 0) else 1
+                width = PASSES * K_PASS // parts
+                for n in range(parts):
+                    nc.scalar.copy(
+                        dst[:, width * n : width * (n + 1)].rearrange("p (z a b t) -> p z a t b", a=P // 4, b=4, t=PACK),
+                        src[:, width * n : width * (n + 1)].rearrange("p (z t a b) -> p z a t b", a=P // 4, b=4, t=PACK),
                     )
+            nc.vector.quantize_mx(out=now["codes"][:].bitcast(FP8X4), scales=now["plane"][:], in_=dst)
+
+        def multiply(z, b, first, last):
+            half = first // BANK * BANK
+            nc.tensor.matmul_mx(
+                out=banks[b][:, : last - first],
+                lhsT=now["codes"][:, P * z : P * (z + 1)].bitcast(FP8X4),
+                lhsT_scale=now["plane"][:, P * z : P * (z + 1)],
+                rhs=x_picked[z, half][:, first - half : last - half].bitcast(FP8X4),
+                rhs_scale=scales_picked[half][4 * z : P, first - half : last - half],
+                start=(z == 0),
+                stop=(z == PASSES - 1),
+            )
+
+        def product(m, c):
+            rows[m, c] = new_tile([P, S], F32, "rows_%s%d" % (m, c))
+            via = {"e": (0, 1), "y": (2, 3)}[m]
+            for b, first, last in zip(via, HALVES, HALVES[1:]):
+                for z in range(PASSES):
+                    multiply(z, b, first, last)
                 nc.scalar.copy(rows[m, c][:, first:last], banks[b][:, : last - first])
-
-        whole = {}
-
-        def note(kind, c, groups, values):
-            whole[kind, c] = values
-            for n, g in enumerate(groups):
-                picked[kind, c, g] = values[:, P * n : P * (n + 1)]
 
         def gather(kind, c, groups=range(GROUPS), over=None):
             m, lst = {"1": ("e", pos1_t), "2": ("e", pos2_t), "cen": ("y", cen_t)}[kind]
-            values = room(P * len(groups), "g%s_%d%d" % (kind, c, groups.start), over)
-            nc.vector.tensor_copy(values, rows[m, c].indirect(entries(lst, P * groups.start, P * groups.stop)))
-            note(kind, c, groups, values)
+            values = over
+            if over is None:
+                values = new_tile([P, P * len(groups)], F32, "g%s_%d%d" % (kind, c, groups.start))[:]
+            nc.vector.tensor_copy(values, rows[m, c][:].indirect(entries(lst, P * groups.start, P * groups.stop)))
+            picked[kind, c, groups.start] = values
 
-        def larger(c, over):
-            values = room(V, "gm_%d" % c, over)
-            nc.vector.tensor_tensor(values, whole["1", c], whole["2", c], MAX)
-            note("max", c, range(GROUPS), values)
+        def larger(c):
+            picked["max", c] = beside["y", c + 1] if c + 1 < TILES else new_tile([P, V], F32, "gm_last")[:]
+            nc.vector.tensor_tensor(picked["max", c], picked["1", c, 0], picked["2", c, 0], MAX)
 
         def edges(c, b, groups=range(GROUPS)):
             for n, g in enumerate(groups):
                 block = banks[b][:, P * n : P * (n + 1)]
-                nc.tensor.matmul(block, picked["cen", c, g], ident[:], start=True, stop=False, is_transpose=True)
-                nc.tensor.matmul(block, picked["max", c, g], ident[:], start=False, stop=True, is_transpose=True)
+                nc.tensor.matmul(block, picked["max", c][:, P * g : P * (g + 1)], ident[:], start=True, stop=False, is_transpose=True)
+                nc.tensor.matmul(block, picked["cen", c, groups.start][:, P * n : P * (n + 1)], ident[:], start=False, stop=True, is_transpose=True)
             quarter = slice(P // PACK * c, P // PACK * (c + 1))
             sums = banks[b][:, : P * len(groups)].rearrange("v (g r u d) -> v g u r d", r=P // PACK, u=2, d=2)
             if len(groups) == 1:
@@ -204,60 +220,39 @@ def tile_picked_edgecv_relu_p_kernel(
             nc.scalar.copy(result[:], banks[b][:, :P])
             nc.sync.dma_start(out[:, P * g : P * (g + 1)], result[:])
 
-        nc.vector.tensor_copy(x_picked[0][:], x_window[0][:].indirect(offs_t[:]))
-        x_picked[1] = new_tile([P, S], U32, "xg1_0")
-        nc.vector.tensor_copy(x_picked[1][:], x_window[1][:].indirect(offs_t[:]))
-        gather_scales(FIRST_CUTS[:2], "x_window0")
-        quantise_w("e", 1, on_scalar)
-        quantise_w("e", 0, on_scalar)
-        gather_scales(FIRST_CUTS[1:], "raw_e0")
+        quantise_w("e", 0)
+        rows["e", 0] = new_tile([P, S], F32, "rows_e0")
+        pieces = list(zip((0, 1, 4), FIRST_CUTS, FIRST_CUTS[1:]))
+        for half in (0, BANK):
+            x_picked[1, half] = new_tile([P, BANK], U32, "xg1_%d" % half)
+        for b, first, last in pieces:
+            multiply(0, b, first, last)
+        for b, first, last in pieces:
+            half = first // BANK * BANK
+            nc.vector.tensor_copy(
+                x_picked[1, half][:, first - half : last - half], x_window[1][:].indirect(entries(offs_t, first, last))
+            )
+            multiply(1, b, first, last)
+            nc.scalar.copy(rows["e", 0][:, first:last], banks[b][:, : last - first])
 
-        product("e", 0, (6, 7, 5), cuts=FIRST_CUTS)
-        product("e", 1, (6, 5))
-        quantise_w("y", 0, on_vector, over=rounded["e", 1])
-        quantise_w("y", 1, on_scalar)
-        product("y", 0, (2, 5), over=staged["y", 0])
-        quantise_w("e", 2, on_scalar)
-        gather("2", 1)
-        gather("1", 1)
-        product("e", 2, (5, 7))
-        quantise_w("e", 3, on_scalar)
-        larger(1, staged["e", 2])
-        gather("cen", 0)
-        gather("2", 0)
-        gather("1", 0)
-        product("y", 1, (2, 1))
-        quantise_w("y", 2, on_vector, over=rounded["e", 2])
-        gather("1", 2)
-        gather("2", 2)
-        larger(0, staged["y", 1])
-        quantise_w("y", 3, on_scalar, over=rounded["y", 2])
-        product("y", 2, (3, 0), over=staged["e", 3])
-        product("e", 3, (1, 2))
-        gather("cen", 2)
-        edges(0, 7)
-        gather("2", 3, over=rounded["y", 3])
-        gather("cen", 1)
-        gather("1", 3)
-        larger(2, staged["y", 3])
-        edges(1, 6)
-        larger(3, staged["y", 2])
-        product("y", 3, (6, 0))
-
-        gather("cen", 3, range(2, 3))
-        edges(2, 0)
-        edges(3, 1, range(2, 3))
-        gather("cen", 3, range(3, 4), over=rounded["e", 3])
-        gather("cen", 3, range(0, 1))
-        gather("cen", 3, range(1, 2))
-        edges(3, 7, range(3, 4))
-        turn(3, 2, on_vector)
-        edges(3, 5, range(0, 1))
-        edges(3, 6, range(1, 2))
-        turn(2, 5, on_scalar)
-        turn(0, 7, on_scalar)
-        project(2, 7)
-        project(0, 5)
-        turn(1, 4, on_scalar)
-        project(3, 0)
-        project(1, 1)
+        quantise_w("y", 0)
+        product("y", 0)
+        for c in range(TILES - 1):
+            gather("1", c, over=behind["y", c])
+            quantise_w("e", c + 1)
+            product("e", c + 1)
+            gather("2", c, over=beside["e", c + 1])
+            gather("cen", c, over=behind["e", c + 1])
+            quantise_w("y", c + 1)
+            product("y", c + 1)
+            larger(c)
+            edges(c, 1)
+        gather("1", TILES - 1, over=behind["y", TILES - 1])
+        gather("2", TILES - 1)
+        larger(TILES - 1)
+        for g in range(GROUPS):
+            gather("cen", TILES - 1, range(g, g + 1))
+            edges(TILES - 1, 4 + g, range(g, g + 1))
+        for g in range(GROUPS):
+            turn(g, g, nc.vector.tensor_copy if g == 2 else nc.scalar.copy)
+            project(g, 4 + g)

@@ -50,19 +50,14 @@ def tile_picked_edgecv_relu_p_kernel(
             return held
 
         weights = {"y": w1, "e": w2}
-        strip = [new_tile([P, 4 * V], F32, "strip%d" % c) for c in range(TILES)]
-        e_strip = new_tile([P, TILES * V], F32, "e_strip")
-        staged, rounded, behind, beside = {}, {}, {}, {}
+        staged = {(m, c): new_tile([P, S], F32, "raw_%s%d" % (m, c))[:] for c in range(TILES) for m in "ey"}
+        strip = new_tile([P, (TILES + 1) * V], F32, "strip")
+        rounded, after_y = {}, {}
         for c in range(TILES):
-            first = (V - LAP) * c
-            rounded["e", c] = e_strip[:, first : first + V]
-            behind["e", c] = e_strip[:, max(first - V + LAP, 0) : first + LAP]
-            beside["e", c] = strip[c][:, :V]
-            staged["e", c] = strip[c][:, V - LAP : V - LAP + S]
-            rounded["y", c] = strip[c][:, 2 * V : 3 * V]
-            behind["y", c] = strip[c][:, 3 * V - LAP : 4 * V - LAP]
-            staged["y", c] = new_tile([P, S], F32, "raw_y%d" % c)[:]
-            beside["y", c] = staged["y", c][:, :V]
+            base = (TILES - 1 - c) * V
+            rounded["y", c] = strip[:, base : base + V]
+            rounded["e", c] = strip[:, base + LAP : base + LAP + V]
+            after_y[c] = strip[:, base + V - LAP : base + 2 * V - LAP]
 
         def load_w(m, c):
             by_pass = staged[m, c].rearrange("p (z t i) -> p z t i", z=PASSES, t=PACK)
@@ -78,23 +73,21 @@ def tile_picked_edgecv_relu_p_kernel(
 
         scale_window = new_tile([P, T], U8, "xs_win")
         nc.vector.memset(scale_window[:].bitcast(I32), 0)
-        offs_t = load_list(offs, "offs_t")
         for q in range(4):
             nc.sync.dma_start(
                 scale_window[32 * q : 32 * q + 4 * PASSES, :].bitcast(I32), x_scales[:, 4 * q : 4 * q + 4, :].bitcast(I32)
             )
+        offs_t = load_list(offs, "offs_t")
+        pos1_t = load_list(pos1, "pos1_t")
+        pos2_t = load_list(pos2, "pos2_t")
         load_x(0)
         load_w("e", 0)
         load_x(1)
-        load_w("y", 0)
-        pos1_t = load_list(pos1, "pos1_t")
-        pos2_t = load_list(pos2, "pos2_t")
-        load_w("e", 1)
         cen_t = load_list(cen, "cen_t")
-        load_w("y", 1)
-        for c in range(2, TILES):
-            load_w("e", c)
-            load_w("y", c)
+        load_w("y", 0)
+        for c in range(1, TILES):
+            for m in "ey":
+                load_w(m, c)
         w3_codes = new_tile([P, 2 * N], U8, "w3w")
         nc.sync.dma_start(w3_codes[:], w3_words[0])
         w3_plane = new_tile([P, N], U8, "w3s")
@@ -124,13 +117,13 @@ def tile_picked_edgecv_relu_p_kernel(
         plane_tiles = [new_tile([P, PASSES * P], U8, "plane%d" % z) for z in range(PASSES)]
         now = {}
         z_turned = new_tile([P, GROUPS, 2, P, 2], BF16, "zt")
-        rows, picked, z_ready = {}, {}, {}
+        rows, picked, spans, z_ready = {}, {}, {}, {}
 
         def quantise_w(m, c):
             dst, src = rounded[m, c].bitcast(BF16), staged[m, c]
-            slot = int(m == "e" and c > 0)
+            slot = int(m == "y")
             now["codes"], now["plane"] = code_tiles[slot], plane_tiles[slot]
-            if slot:
+            if m == "y":
                 nc.gpsimd.tensor_scalar(
                     dst.rearrange("p (z i t) -> p z i t", z=PASSES, t=PACK),
                     src.rearrange("p (z t i) -> p z i t", z=PASSES, t=PACK),
@@ -163,29 +156,37 @@ def tile_picked_edgecv_relu_p_kernel(
 
         def product(m, c):
             rows[m, c] = new_tile([P, S], F32, "rows_%s%d" % (m, c))
-            via = {"e": (0, 1), "y": (2, 3)}[m]
+            via = (0, 1) if m == "e" else (2, 3)
             for b, first, last in zip(via, HALVES, HALVES[1:]):
                 for z in range(PASSES):
                     multiply(z, b, first, last)
                 nc.scalar.copy(rows[m, c][:, first:last], banks[b][:, : last - first])
 
+        def note(kind, c, groups, values):
+            for n, g in enumerate(groups):
+                picked[kind, c, g] = values[:, P * n : P * (n + 1)]
+            spans[kind, c, groups.start, groups.stop] = values
+
+        def room(name, groups, over):
+            return new_tile([P, P * len(groups)], F32, name)[:] if over is None else over
+
         def gather(kind, c, groups=range(GROUPS), over=None):
             m, lst = {"1": ("e", pos1_t), "2": ("e", pos2_t), "cen": ("y", cen_t)}[kind]
-            values = over
-            if over is None:
-                values = new_tile([P, P * len(groups)], F32, "g%s_%d%d" % (kind, c, groups.start))[:]
+            values = room("g%s_%d%d" % (kind, c, groups.start), groups, over)
             nc.vector.tensor_copy(values, rows[m, c][:].indirect(entries(lst, P * groups.start, P * groups.stop)))
-            picked[kind, c, groups.start] = values
+            note(kind, c, groups, values)
 
-        def larger(c):
-            picked["max", c] = beside["y", c + 1] if c + 1 < TILES else new_tile([P, V], F32, "gm_last")[:]
-            nc.vector.tensor_tensor(picked["max", c], picked["1", c, 0], picked["2", c, 0], MAX)
+        def larger(c, groups=range(GROUPS), over=None):
+            values = room("gm_%d%d" % (c, groups.start), groups, over)
+            first = spans["1", c, 0, GROUPS][:, P * groups.start : P * groups.stop]
+            nc.vector.tensor_tensor(values, first, spans["2", c, groups.start, groups.stop], MAX)
+            note("max", c, groups, values)
 
         def edges(c, b, groups=range(GROUPS)):
             for n, g in enumerate(groups):
                 block = banks[b][:, P * n : P * (n + 1)]
-                nc.tensor.matmul(block, picked["max", c][:, P * g : P * (g + 1)], ident[:], start=True, stop=False, is_transpose=True)
-                nc.tensor.matmul(block, picked["cen", c, groups.start][:, P * n : P * (n + 1)], ident[:], start=False, stop=True, is_transpose=True)
+                nc.tensor.matmul(block, picked["max", c, g], ident[:], start=True, stop=False, is_transpose=True)
+                nc.tensor.matmul(block, picked["cen", c, g], ident[:], start=False, stop=True, is_transpose=True)
             quarter = slice(P // PACK * c, P // PACK * (c + 1))
             sums = banks[b][:, : P * len(groups)].rearrange("v (g r u d) -> v g u r d", r=P // PACK, u=2, d=2)
             if len(groups) == 1:
@@ -194,21 +195,24 @@ def tile_picked_edgecv_relu_p_kernel(
                 for u in range(2):
                     nc.scalar.activation(z_turned[:, groups.start : groups.stop, u, quarter, :], sums[:, :, u], RELU)
 
-        def turn(g, b, copy):
-            for u in range(2):
-                pairs = z_turned[:, g, u].rearrange("v p d -> v (p d)").bitcast(F32)
-                nc.tensor.transpose(banks[b][:, P * u : P * (u + 1)], pairs, ident[:])
-            z_ready[g] = new_tile([P, P, PACK], BF16, "zb%d" % g)
-            copy(z_ready[g][:].bitcast(F32), banks[b][:, : 2 * P].rearrange("p (u v) -> p v u", u=2))
-
-        def project(g, b):
-            z_codes = new_tile([P, P], U32, "zq%d" % g)
-            z_plane = new_tile([P, P], U8, "zs%d" % g)
-            nc.vector.quantize_mx(
-                out=z_codes[:].bitcast(FP8X4), scales=z_plane[:], in_=z_ready[g][:].rearrange("p v t -> p (v t)")
+        def turn(groups, b, copy):
+            for n, g in enumerate(groups):
+                for u in range(2):
+                    pairs = z_turned[:, g, u].rearrange("v p d -> v (p d)").bitcast(F32)
+                    nc.tensor.transpose(banks[b][:, P * (2 * n + u) : P * (2 * n + u + 1)], pairs, ident[:])
+            z_ready[groups.start] = new_tile([P, len(groups) * K_PASS], BF16, "zb%d" % groups.start)
+            copy(
+                z_ready[groups.start][:].bitcast(F32).rearrange("p (g v u) -> p g v u", v=P, u=2),
+                banks[b][:, : 2 * P * len(groups)].rearrange("p (g u v) -> p g v u", v=P, u=2),
             )
+
+        def project(groups, b, copy=nc.scalar.copy):
+            width = P * len(groups)
+            z_codes = new_tile([P, width], U32, "zq%d" % groups.start)
+            z_plane = new_tile([P, width], U8, "zs%d" % groups.start)
+            nc.vector.quantize_mx(out=z_codes[:].bitcast(FP8X4), scales=z_plane[:], in_=z_ready[groups.start][:])
             nc.tensor.matmul_mx(
-                out=banks[b][:, :P],
+                out=banks[b][:, :width],
                 lhsT=w3_codes[:].bitcast(FP4X4),
                 lhsT_scale=w3_plane[:],
                 rhs=z_codes[:].bitcast(FP8X4),
@@ -216,9 +220,9 @@ def tile_picked_edgecv_relu_p_kernel(
                 start=True,
                 stop=True,
             )
-            result = new_tile([P, P], F32, "res_sb%d" % g)
-            nc.scalar.copy(result[:], banks[b][:, :P])
-            nc.sync.dma_start(out[:, P * g : P * (g + 1)], result[:])
+            result = new_tile([P, width], F32, "res_sb%d" % groups.start)
+            copy(result[:], banks[b][:, :width])
+            nc.sync.dma_start(out[:, P * groups.start : P * groups.stop], result[:])
 
         quantise_w("e", 0)
         rows["e", 0] = new_tile([P, S], F32, "rows_e0")
@@ -237,22 +241,35 @@ def tile_picked_edgecv_relu_p_kernel(
 
         quantise_w("y", 0)
         product("y", 0)
-        for c in range(TILES - 1):
-            gather("1", c, over=behind["y", c])
+        last = TILES - 1
+        for c in range(last):
+            gather("1", c, over=after_y[c])
             quantise_w("e", c + 1)
             product("e", c + 1)
-            gather("2", c, over=beside["e", c + 1])
-            gather("cen", c, over=behind["e", c + 1])
+            gather("2", c, over=staged["e", c + 1][:, :V])
+            gather("cen", c)
             quantise_w("y", c + 1)
             product("y", c + 1)
-            larger(c)
-            edges(c, 1)
-        gather("1", TILES - 1, over=behind["y", TILES - 1])
-        gather("2", TILES - 1)
-        larger(TILES - 1)
-        for g in range(GROUPS):
-            gather("cen", TILES - 1, range(g, g + 1))
-            edges(TILES - 1, 4 + g, range(g, g + 1))
-        for g in range(GROUPS):
-            turn(g, g, nc.vector.tensor_copy if g == 2 else nc.scalar.copy)
-            project(g, 4 + g)
+            larger(c, over=staged["y", c + 1][:, :V])
+            edges(c, 4)
+        gather("1", last, over=after_y[last])
+        gather("2", last, range(0, 2))
+        larger(last, range(0, 2))
+        gather("cen", last, range(0, 1))
+        edges(last, 5, range(0, 1))
+        gather("cen", last, range(1, 2))
+        edges(last, 6, range(1, 2))
+        gather("2", last, range(2, 4), over=None)
+        larger(last, range(2, 4))
+        turn(range(0, 1), 1, nc.vector.tensor_copy)
+        turn(range(1, 2), 2, nc.vector.tensor_copy)
+        gather("cen", last, range(2, 3))
+        edges(last, 7, range(2, 3))
+        gather("cen", last, range(3, 4))
+        edges(last, 0, range(3, 4))
+        project(range(0, 1), 5, nc.scalar.copy)
+        project(range(1, 2), 6, nc.scalar.copy)
+        turn(range(2, 3), 3, nc.scalar.copy)
+        project(range(2, 3), 7, nc.scalar.copy)
+        turn(range(3, 4), 4, nc.scalar.copy)
+        project(range(3, 4), 0, nc.scalar.copy)

@@ -38,11 +38,15 @@ def tile_picked_edgecv_relu_p_kernel(
     nc = tc.nc
     with ExitStack() as ctx:
         keep = ctx.enter_context(tc.tile_pool(name="keep", bufs=1))
+        reused = ctx.enter_context(tc.tile_pool(name="reused", bufs=1))
         psum = ctx.enter_context(tc.psum_pool(name="psum", bufs=1))
         banks = [psum.tile([P, BANK], F32, name="bank%d" % b) for b in range(8)]
 
         def new_tile(shape, dtype, name, tag=None):
             return keep.tile(shape, dtype, name=name, tag=tag or name, align_bytes=64)
+
+        def placed(shape, dtype, name, offset):
+            return reused.tile(shape, dtype, name=name, align_bytes=64, offset=offset)
 
         def load_list(src, name):
             held = keep.tile(list(src.shape), U16, name=name)
@@ -51,13 +55,14 @@ def tile_picked_edgecv_relu_p_kernel(
 
         weights = {"y": w1, "e": w2}
         staged = {(m, c): new_tile([P, S], F32, "raw_%s%d" % (m, c))[:] for c in range(TILES) for m in "ey"}
-        strip = new_tile([P, (TILES + 1) * V], F32, "strip")
-        rounded, after_y = {}, {}
+        lead = [("e", 1), ("e", 2), ("y", 2), ("y", 3)]
+        middle = [("y", 0), ("y", 1), ("e", 3)]
+        buffers = [new_tile([P, V], F32, "rounding")[:]] + [staged[w][:, V:] for w in middle]
+        rounded = {("e", 0): buffers[0]}
         for c in range(TILES):
-            base = (TILES - 1 - c) * V
-            rounded["y", c] = strip[:, base : base + V]
-            rounded["e", c] = strip[:, base + LAP : base + LAP + V]
-            after_y[c] = strip[:, base + V - LAP : base + 2 * V - LAP]
+            rounded[lead[c]] = buffers[c]
+        for c in range(TILES - 1):
+            rounded[middle[c]] = buffers[c]
 
         def load_w(m, c):
             by_pass = staged[m, c].rearrange("p (z t i) -> p z t i", z=PASSES, t=PACK)
@@ -68,26 +73,28 @@ def tile_picked_edgecv_relu_p_kernel(
         x_window = {}
 
         def load_x(z):
-            x_window[z] = new_tile([P, T], U32, "x_window%d" % z)
+            x_window[z] = placed([P, T], U32, "x_window%d" % z, 4 * T * z)
             nc.sync.dma_start(x_window[z][:].bitcast(I32), x_words[z].rearrange("p c t -> p (c t)").bitcast(I32))
 
+        offs_t = load_list(offs, "offs_t")
+        load_x(0)
         scale_window = new_tile([P, T], U8, "xs_win")
         nc.vector.memset(scale_window[:].bitcast(I32), 0)
         for q in range(4):
             nc.sync.dma_start(
                 scale_window[32 * q : 32 * q + 4 * PASSES, :].bitcast(I32), x_scales[:, 4 * q : 4 * q + 4, :].bitcast(I32)
             )
-        offs_t = load_list(offs, "offs_t")
-        pos1_t = load_list(pos1, "pos1_t")
-        pos2_t = load_list(pos2, "pos2_t")
-        load_x(0)
         load_w("e", 0)
         load_x(1)
+        load_w(*lead[0])
+        pos1_t = load_list(pos1, "pos1_t")
+        pos2_t = load_list(pos2, "pos2_t")
+        load_w(*middle[0])
         cen_t = load_list(cen, "cen_t")
-        load_w("y", 0)
         for c in range(1, TILES):
-            for m in "ey":
-                load_w(m, c)
+            load_w(*lead[c])
+            if c < TILES - 1:
+                load_w(*middle[c])
         w3_codes = new_tile([P, 2 * N], U8, "w3w")
         nc.sync.dma_start(w3_codes[:], w3_words[0])
         w3_plane = new_tile([P, N], U8, "w3s")
@@ -104,41 +111,42 @@ def tile_picked_edgecv_relu_p_kernel(
         def entries(lst, first, last):
             return lst[:, first // PER_COLUMN : last // PER_COLUMN]
 
-        scales_picked, x_picked = {}, {}
-        for half in (0, BANK):
-            scales_picked[half] = new_tile([P, BANK], U8, "xsg_%d" % half)
-            nc.vector.tensor_copy(scales_picked[half][:], scale_window[:].indirect(entries(offs_t, half, half + BANK)))
+        x_picked = {}
         x_first = new_tile([P, S], U32, "xg0")
         nc.vector.tensor_copy(x_first[:], x_window[0][:].indirect(offs_t[:]))
+        scales_picked = placed([P, S], U8, "xsg", 0)
+        nc.vector.tensor_copy(scales_picked[:], scale_window[:].indirect(offs_t[:]))
         for half in (0, BANK):
             x_picked[0, half] = x_first[:, half : half + BANK]
 
-        code_tiles = [new_tile([P, PASSES * P], U32, "codes%d" % z, tag="x_window%d" % z) for z in range(PASSES)]
-        plane_tiles = [new_tile([P, PASSES * P], U8, "plane%d" % z) for z in range(PASSES)]
         now = {}
         z_turned = new_tile([P, GROUPS, 2, P, 2], BF16, "zt")
         rows, picked, spans, z_ready = {}, {}, {}, {}
 
         def quantise_w(m, c):
             dst, src = rounded[m, c].bitcast(BF16), staged[m, c]
-            slot = int(m == "y")
-            now["codes"], now["plane"] = code_tiles[slot], plane_tiles[slot]
-            if m == "y":
-                nc.gpsimd.tensor_scalar(
-                    dst.rearrange("p (z i t) -> p z i t", z=PASSES, t=PACK),
-                    src.rearrange("p (z t i) -> p z i t", z=PASSES, t=PACK),
-                    1.0,
-                    0.0,
-                    MULT,
-                    ADD,
-                )
+            if m == "e" and c < PASSES:
+                now["codes"] = placed([P, PASSES * P], U32, "codes_e%d" % c, S + 4 * T * c)
             else:
-                parts = PASSES if (m, c) == ("e", 0) else 1
-                width = PASSES * K_PASS // parts
-                for n in range(parts):
+                now["codes"] = new_tile([P, PASSES * P], U32, "codes_%s%d" % (m, c))
+            now["plane"] = new_tile([P, PASSES * P], U8, "plane_%s%d" % (m, c))
+            parts = PASSES if m == "e" and c < PASSES else 1
+            width = PASSES * K_PASS // parts
+            for n in range(parts):
+                to, frm = dst[:, width * n : width * (n + 1)], src[:, width * n : width * (n + 1)]
+                if (m, c) in middle or (m, c, n) == ("e", 1, 1):
+                    nc.gpsimd.tensor_scalar(
+                        to.rearrange("p (z i t) -> p z i t", i=P, t=PACK),
+                        frm.rearrange("p (z t i) -> p z i t", i=P, t=PACK),
+                        1.0,
+                        0.0,
+                        MULT,
+                        ADD,
+                    )
+                else:
                     nc.scalar.copy(
-                        dst[:, width * n : width * (n + 1)].rearrange("p (z a b t) -> p z a t b", a=P // 4, b=4, t=PACK),
-                        src[:, width * n : width * (n + 1)].rearrange("p (z t a b) -> p z a t b", a=P // 4, b=4, t=PACK),
+                        to.rearrange("p (z a b t) -> p z a t b", a=P // 4, b=4, t=PACK),
+                        frm.rearrange("p (z t a b) -> p z a t b", a=P // 4, b=4, t=PACK),
                     )
             nc.vector.quantize_mx(out=now["codes"][:].bitcast(FP8X4), scales=now["plane"][:], in_=dst)
 
@@ -149,14 +157,14 @@ def tile_picked_edgecv_relu_p_kernel(
                 lhsT=now["codes"][:, P * z : P * (z + 1)].bitcast(FP8X4),
                 lhsT_scale=now["plane"][:, P * z : P * (z + 1)],
                 rhs=x_picked[z, half][:, first - half : last - half].bitcast(FP8X4),
-                rhs_scale=scales_picked[half][4 * z : P, first - half : last - half],
+                rhs_scale=scales_picked[4 * z : P, first:last],
                 start=(z == 0),
                 stop=(z == PASSES - 1),
             )
 
         def product(m, c):
             rows[m, c] = new_tile([P, S], F32, "rows_%s%d" % (m, c))
-            via = (0, 1) if m == "e" else (2, 3)
+            via = (0, 1) if (m, c) in lead else (2, 3)
             for b, first, last in zip(via, HALVES, HALVES[1:]):
                 for z in range(PASSES):
                     multiply(z, b, first, last)
@@ -185,8 +193,9 @@ def tile_picked_edgecv_relu_p_kernel(
         def edges(c, b, groups=range(GROUPS)):
             for n, g in enumerate(groups):
                 block = banks[b][:, P * n : P * (n + 1)]
-                nc.tensor.matmul(block, picked["max", c, g], ident[:], start=True, stop=False, is_transpose=True)
-                nc.tensor.matmul(block, picked["cen", c, g], ident[:], start=False, stop=True, is_transpose=True)
+                early, late = ("max", "cen") if len(groups) == 1 else ("cen", "max")
+                nc.tensor.matmul(block, picked[early, c, g], ident[:], start=True, stop=False, is_transpose=True)
+                nc.tensor.matmul(block, picked[late, c, g], ident[:], start=False, stop=True, is_transpose=True)
             quarter = slice(P // PACK * c, P // PACK * (c + 1))
             sums = banks[b][:, : P * len(groups)].rearrange("v (g r u d) -> v g u r d", r=P // PACK, u=2, d=2)
             if len(groups) == 1:
@@ -228,7 +237,7 @@ def tile_picked_edgecv_relu_p_kernel(
         rows["e", 0] = new_tile([P, S], F32, "rows_e0")
         pieces = list(zip((0, 1, 4), FIRST_CUTS, FIRST_CUTS[1:]))
         for half in (0, BANK):
-            x_picked[1, half] = new_tile([P, BANK], U32, "xg1_%d" % half)
+            x_picked[1, half] = placed([P, BANK], U32, "xg1_%d" % half, 2 * S + 4 * half)
         for b, first, last in pieces:
             multiply(0, b, first, last)
         for b, first, last in pieces:
@@ -239,37 +248,43 @@ def tile_picked_edgecv_relu_p_kernel(
             multiply(1, b, first, last)
             nc.scalar.copy(rows["e", 0][:, first:last], banks[b][:, : last - first])
 
-        quantise_w("y", 0)
-        product("y", 0)
         last = TILES - 1
+        halves = (range(0, 2), range(2, 4))
         for c in range(last):
-            gather("1", c, over=after_y[c])
-            quantise_w("e", c + 1)
-            product("e", c + 1)
-            gather("2", c, over=staged["e", c + 1][:, :V])
-            gather("cen", c)
-            quantise_w("y", c + 1)
-            product("y", c + 1)
-            larger(c, over=staged["y", c + 1][:, :V])
-            edges(c, 4)
-        gather("1", last, over=after_y[last])
-        gather("2", last, range(0, 2))
-        larger(last, range(0, 2))
+            quantise_w(*lead[c])
+            product(*lead[c])
+            if c >= 2:
+                edges(c - 2, 7)
+            gather("1", c, over=staged[lead[c]][:, :V])
+            gather("2", c, over=staged[lead[c]][:, V:])
+            quantise_w(*middle[c])
+            product(*middle[c])
+            larger(c, over=staged[middle[c]][:, :V])
+            if c >= 1:
+                gather("cen", c - 1, over=buffers[c])
+        quantise_w(*lead[last])
+        product(*lead[last])
+        edges(last - 2, 4)
+        gather("cen", last - 1, over=staged[lead[last]][:, :V])
+        edges(last - 1, 2)
+        gather("1", last, over=staged[lead[last]][:, V:])
+        for n, groups in enumerate(halves):
+            gather("2", last, groups, over=buffers[last][:, V // 2 * n : V // 2 * (n + 1)])
+        for groups in halves:
+            larger(last, groups)
         gather("cen", last, range(0, 1))
         edges(last, 5, range(0, 1))
         gather("cen", last, range(1, 2))
         edges(last, 6, range(1, 2))
-        gather("2", last, range(2, 4), over=None)
-        larger(last, range(2, 4))
-        turn(range(0, 1), 1, nc.vector.tensor_copy)
-        turn(range(1, 2), 2, nc.vector.tensor_copy)
         gather("cen", last, range(2, 3))
         edges(last, 7, range(2, 3))
         gather("cen", last, range(3, 4))
         edges(last, 0, range(3, 4))
+        turn(range(0, 1), 1, nc.vector.tensor_copy)
+        turn(range(1, 2), 2, nc.vector.tensor_copy)
+        turn(range(2, 3), 3, nc.scalar.copy)
+        turn(range(3, 4), 4, nc.scalar.copy)
         project(range(0, 1), 5, nc.scalar.copy)
         project(range(1, 2), 6, nc.scalar.copy)
-        turn(range(2, 3), 3, nc.scalar.copy)
         project(range(2, 3), 7, nc.scalar.copy)
-        turn(range(3, 4), 4, nc.scalar.copy)
         project(range(3, 4), 0, nc.scalar.copy)

@@ -18,6 +18,7 @@ RELU = mybir.ActivationFunctionType.Relu
 MAX = mybir.AluOpType.max
 MULT = mybir.AluOpType.mult
 ADD = mybir.AluOpType.add
+SUBTRACT = mybir.AluOpType.subtract
 
 P = 128
 PACK = 4
@@ -190,12 +191,28 @@ def tile_picked_edgecv_relu_p_kernel(
             nc.vector.tensor_tensor(values, first, spans["2", c, groups.start, groups.stop], MAX)
             note("max", c, groups, values)
 
+        def difference(c, groups, over):
+            looked_up = rows["e", c][:].indirect(entries(pos2_t, P * groups.start, P * groups.stop))
+            first = spans["1", c, groups.start, groups.stop]
+            nc.vector.tensor_tensor(over, looked_up, first, SUBTRACT)
+            note("diff", c, groups, over)
+
+        def excess(c, groups, engine):
+            values = room("gx_%d%d" % (c, groups.start), groups, None)
+            if engine == "s":
+                nc.scalar.activation(values, spans["diff", c, groups.start, groups.stop], RELU)
+            else:
+                nc.vector.tensor_scalar(values, spans["diff", c, groups.start, groups.stop], 0.0, 0.0, MAX, ADD)
+            note("excess", c, groups, values)
+
         def edges(c, b, groups=range(GROUPS)):
             for n, g in enumerate(groups):
                 block = banks[b][:, P * n : P * (n + 1)]
-                early, late = ("max", "cen") if len(groups) == 1 else ("cen", "max")
-                nc.tensor.matmul(block, picked[early, c, g], ident[:], start=True, stop=False, is_transpose=True)
-                nc.tensor.matmul(block, picked[late, c, g], ident[:], start=False, stop=True, is_transpose=True)
+                kinds = ("1", "excess", "cen") if len(groups) == 1 else ("cen", "max")
+                for kind in kinds:
+                    nc.tensor.matmul(
+                        block, picked[kind, c, g], ident[:], start=kind == kinds[0], stop=kind == kinds[-1], is_transpose=True
+                    )
             quarter = slice(P // PACK * c, P // PACK * (c + 1))
             sums = banks[b][:, : P * len(groups)].rearrange("v (g r u d) -> v g u r d", r=P // PACK, u=2, d=2)
             if len(groups) == 1:
@@ -267,11 +284,12 @@ def tile_picked_edgecv_relu_p_kernel(
         edges(last - 2, 4)
         gather("cen", last - 1, over=staged[lead[last]][:, :V])
         edges(last - 1, 2)
-        gather("1", last, over=staged[lead[last]][:, V:])
         for n, groups in enumerate(halves):
-            gather("2", last, groups, over=buffers[last][:, V // 2 * n : V // 2 * (n + 1)])
-        for groups in halves:
-            larger(last, groups)
+            gather("1", last, groups, over=staged[lead[last]][:, V + V // 2 * n : V + V // 2 * (n + 1)])
+        for n, groups in enumerate(halves):
+            difference(last, groups, over=buffers[last][:, V // 2 * n : V // 2 * (n + 1)])
+        for groups, engine in zip(halves, "ss"):
+            excess(last, groups, engine)
         gather("cen", last, range(0, 1))
         edges(last, 5, range(0, 1))
         gather("cen", last, range(1, 2))

@@ -250,6 +250,18 @@ def tile_picked_edgecv_relu_p_kernel(
             copy(result[:], banks[b][:, :width])
             nc.sync.dma_start(out[:, P * groups.start : P * groups.stop], result[:])
 
+        def keep_warm(b, passes):
+            for n in range(passes):
+                nc.tensor.matmul_mx(
+                    out=banks[b][:],
+                    lhsT=now["codes"][:, :P].bitcast(FP8X4),
+                    lhsT_scale=now["plane"][:, :P],
+                    rhs=x_picked[0, 0].bitcast(FP8X4),
+                    rhs_scale=scales_picked[:, :BANK],
+                    start=True,
+                    stop=True,
+                )
+
         quantise_w("e", 0)
         rows["e", 0] = new_tile([P, S], F32, "rows_e0")
         pieces = list(zip((0, 1, 4), FIRST_CUTS, FIRST_CUTS[1:]))
@@ -284,6 +296,7 @@ def tile_picked_edgecv_relu_p_kernel(
         edges(last - 2, 4)
         gather("cen", last - 1, over=staged[lead[last]][:, :V])
         edges(last - 1, 2)
+        keep_warm(1, 4)
         for n, groups in enumerate(halves):
             gather("1", last, groups, over=staged[lead[last]][:, V + V // 2 * n : V + V // 2 * (n + 1)])
         for n, groups in enumerate(halves):
@@ -291,18 +304,18 @@ def tile_picked_edgecv_relu_p_kernel(
         for groups, engine in zip(halves, "ss"):
             excess(last, groups, engine)
         gather("cen", last, range(0, 1))
-        edges(last, 5, range(0, 1))
+        edges(last, 1, range(0, 1))
         gather("cen", last, range(1, 2))
-        edges(last, 6, range(1, 2))
+        edges(last, 5, range(1, 2))
         gather("cen", last, range(2, 3))
-        edges(last, 7, range(2, 3))
+        edges(last, 6, range(2, 3))
         gather("cen", last, range(3, 4))
-        edges(last, 0, range(3, 4))
-        turn(range(0, 1), 1, nc.vector.tensor_copy)
+        edges(last, 7, range(3, 4))
+        turn(range(0, 1), 0, nc.vector.tensor_copy)
         turn(range(1, 2), 2, nc.vector.tensor_copy)
         turn(range(2, 3), 3, nc.scalar.copy)
         turn(range(3, 4), 4, nc.scalar.copy)
-        project(range(0, 1), 5, nc.scalar.copy)
-        project(range(1, 2), 6, nc.scalar.copy)
-        project(range(2, 3), 7, nc.scalar.copy)
-        project(range(3, 4), 0, nc.scalar.copy)
+        project(range(0, 1), 1, nc.scalar.copy)
+        project(range(1, 2), 5, nc.scalar.copy)
+        project(range(2, 3), 6, nc.scalar.copy)
+        project(range(3, 4), 7, nc.scalar.copy)

@@ -1,7 +1,6 @@
 from contextlib import ExitStack
 
 import concourse.mybir as mybir
-from concourse.masks import make_identity
 
 K, T, S, V, H, N = 1024, 2048, 1024, 512, 512, 128
 FLOPS = 2 * (2 * K * H * S + H * N * V)
@@ -18,19 +17,19 @@ RELU = mybir.ActivationFunctionType.Relu
 MAX = mybir.AluOpType.max
 MULT = mybir.AluOpType.mult
 ADD = mybir.AluOpType.add
-SUBTRACT = mybir.AluOpType.subtract
 
 P = 128
 PACK = 4
+QUAD = 32
 K_PASS = P * PACK
 PASSES = K // K_PASS
 TILES = H // P
-GROUPS = V // P
 BANK = 512
 PER_COLUMN = 16
-LAP = 16
+HALF = V // 2
 HALVES = (0, BANK, S)
 FIRST_CUTS = (0, BANK, BANK + BANK // 2, S)
+PIECES = ((0, 256), (256, 384), (384, 512))
 
 
 def tile_picked_edgecv_relu_p_kernel(
@@ -43,8 +42,8 @@ def tile_picked_edgecv_relu_p_kernel(
         psum = ctx.enter_context(tc.psum_pool(name="psum", bufs=1))
         banks = [psum.tile([P, BANK], F32, name="bank%d" % b) for b in range(8)]
 
-        def new_tile(shape, dtype, name, tag=None):
-            return keep.tile(shape, dtype, name=name, tag=tag or name, align_bytes=64)
+        def new_tile(shape, dtype, name):
+            return keep.tile(shape, dtype, name=name, align_bytes=64)
 
         def placed(shape, dtype, name, offset):
             return reused.tile(shape, dtype, name=name, align_bytes=64, offset=offset)
@@ -54,22 +53,29 @@ def tile_picked_edgecv_relu_p_kernel(
             nc.sync.dma_start(held[:], src)
             return held
 
-        weights = {"y": w1, "e": w2}
-        staged = {(m, c): new_tile([P, S], F32, "raw_%s%d" % (m, c))[:] for c in range(TILES) for m in "ey"}
-        lead = [("e", 1), ("e", 2), ("y", 2), ("y", 3)]
-        middle = [("y", 0), ("y", 1), ("e", 3)]
-        buffers = [new_tile([P, V], F32, "rounding")[:]] + [staged[w][:, V:] for w in middle]
-        rounded = {("e", 0): buffers[0]}
-        for c in range(TILES):
-            rounded[lead[c]] = buffers[c]
-        for c in range(TILES - 1):
-            rounded[middle[c]] = buffers[c]
+        def entries(lst, first, last):
+            return lst[:, first // PER_COLUMN : last // PER_COLUMN]
 
-        def load_w(m, c):
-            by_pass = staged[m, c].rearrange("p (z t i) -> p z t i", z=PASSES, t=PACK)
+        STRIP = 4 * T * PASSES
+        FOLD = STRIP + 8 * T
+        RAW = FOLD + 8 * HALF * 2 * PACK
+        raw_e = [placed([P, PASSES * K_PASS], F32, "raw_e%d" % c, RAW + 6144 * c + 1024)[:] for c in range(TILES)]
+        ROWS = RAW + 6144 * TILES
+        raw_y = {(z, n): new_tile([P, PACK * H // 2], F32, "raw_y%d%d" % (z, n))[:] for z, n in ((0, 0), (0, 1), (1, 0))}
+        raw_y[1, 1] = placed([P, PACK * H // 2], F32, "raw_y11", ROWS)[:]
+
+        def behind_rounding(c, n):
+            return placed([P, V], F32, "behind%d%d" % (c, n), RAW + 6144 * c + 2048 * n)[:]
+
+        def load_e(c):
+            by_pass = raw_e[c].rearrange("p (z j i) -> p z j i", z=PASSES, j=PACK)
             for z in range(PASSES):
-                src = weights[m][K_PASS * z : K_PASS * (z + 1), P * c : P * (c + 1)]
-                nc.sync.dma_start(by_pass[:, z], src.rearrange("(p t) i -> p t i", t=PACK))
+                src = w2[K_PASS * z : K_PASS * (z + 1), P * c : P * (c + 1)]
+                nc.sync.dma_start(by_pass[:, z], src.rearrange("(p j) i -> p j i", j=PACK))
+
+        def load_y(z, n):
+            src = w1[K_PASS * z : K_PASS * (z + 1), H // 2 * n : H // 2 * (n + 1)]
+            nc.sync.dma_start(raw_y[z, n].rearrange("p (j i) -> p j i", j=PACK), src.rearrange("(p j) i -> p j i", j=PACK))
 
         x_window = {}
 
@@ -83,34 +89,33 @@ def tile_picked_edgecv_relu_p_kernel(
         nc.vector.memset(scale_window[:].bitcast(I32), 0)
         for q in range(4):
             nc.sync.dma_start(
-                scale_window[32 * q : 32 * q + 4 * PASSES, :].bitcast(I32), x_scales[:, 4 * q : 4 * q + 4, :].bitcast(I32)
+                scale_window[QUAD * q : QUAD * q + 4 * PASSES, :].bitcast(I32),
+                x_scales[:, 4 * q : 4 * q + 4, :].bitcast(I32),
             )
-        load_w("e", 0)
+        load_e(0)
         load_x(1)
-        load_w(*lead[0])
+        load_e(1)
         pos1_t = load_list(pos1, "pos1_t")
         pos2_t = load_list(pos2, "pos2_t")
-        load_w(*middle[0])
+        load_e(2)
+        load_y(0, 0)
+        load_e(3)
+        load_y(0, 1)
+        load_y(1, 0)
+        load_y(1, 1)
         cen_t = load_list(cen, "cen_t")
-        for c in range(1, TILES):
-            load_w(*lead[c])
-            if c < TILES - 1:
-                load_w(*middle[c])
         w3_codes = new_tile([P, 2 * N], U8, "w3w")
         nc.sync.dma_start(w3_codes[:], w3_words[0])
         w3_plane = new_tile([P, N], U8, "w3s")
         nc.gpsimd.memset(w3_plane[:].bitcast(I32), 0)
         for q in range(4):
             nc.sync.dma_start(
-                w3_plane[32 * q : 32 * q + 4, :].bitcast(I32), w3_scales[0, 4 * q : 4 * q + 4, :].bitcast(I32)
+                w3_plane[QUAD * q : QUAD * q + 4, :].bitcast(I32), w3_scales[0, 4 * q : 4 * q + 4, :].bitcast(I32)
             )
-        ident_made = new_tile([P, P], F32, "ident0")
-        make_identity(nc, ident_made[:])
-        ident = new_tile([P, P], F32, "ident")
-        nc.scalar.activation(ident[:], ident_made[:], RELU)
-
-        def entries(lst, first, last):
-            return lst[:, first // PER_COLUMN : last // PER_COLUMN]
+        below = new_tile([P, 8], F32, "below")
+        nc.gpsimd.memset(below[:], 0.0)
+        zero = new_tile([P, 8], F32, "zero")
+        nc.scalar.activation(zero[:], below[:], RELU)
 
         x_picked = {}
         x_first = new_tile([P, S], U32, "xg0")
@@ -120,202 +125,194 @@ def tile_picked_edgecv_relu_p_kernel(
         for half in (0, BANK):
             x_picked[0, half] = x_first[:, half : half + BANK]
 
-        now = {}
-        z_turned = new_tile([P, GROUPS, 2, P, 2], BF16, "zt")
-        rows, picked, spans, z_ready = {}, {}, {}, {}
+        rounding = new_tile([P, PASSES * K_PASS], BF16, "rounding")[:]
+        codes, plane, rows = {}, {}, {}
 
-        def quantise_w(m, c):
-            dst, src = rounded[m, c].bitcast(BF16), staged[m, c]
-            if m == "e" and c < PASSES:
-                now["codes"] = placed([P, PASSES * P], U32, "codes_e%d" % c, S + 4 * T * c)
+        def cast_e(dst, src, engine):
+            if engine == "g":
+                nc.gpsimd.tensor_scalar(
+                    dst.rearrange("p (z i j) -> p z i j", i=P, j=PACK),
+                    src.rearrange("p (z j i) -> p z i j", i=P, j=PACK),
+                    1.0,
+                    0.0,
+                    MULT,
+                    ADD,
+                )
             else:
-                now["codes"] = new_tile([P, PASSES * P], U32, "codes_%s%d" % (m, c))
-            now["plane"] = new_tile([P, PASSES * P], U8, "plane_%s%d" % (m, c))
-            parts = PASSES if m == "e" and c < PASSES else 1
-            width = PASSES * K_PASS // parts
-            for n in range(parts):
-                to, frm = dst[:, width * n : width * (n + 1)], src[:, width * n : width * (n + 1)]
-                if (m, c) in middle or (m, c, n) == ("e", 1, 1):
-                    nc.gpsimd.tensor_scalar(
-                        to.rearrange("p (z i t) -> p z i t", i=P, t=PACK),
-                        frm.rearrange("p (z t i) -> p z i t", i=P, t=PACK),
-                        1.0,
-                        0.0,
-                        MULT,
-                        ADD,
-                    )
-                else:
-                    nc.scalar.copy(
-                        to.rearrange("p (z a b t) -> p z a t b", a=P // 4, b=4, t=PACK),
-                        frm.rearrange("p (z t a b) -> p z a t b", a=P // 4, b=4, t=PACK),
-                    )
-            nc.vector.quantize_mx(out=now["codes"][:].bitcast(FP8X4), scales=now["plane"][:], in_=dst)
+                nc.scalar.copy(
+                    dst.rearrange("p (z a b j) -> p z a j b", a=P // 4, b=4, j=PACK),
+                    src.rearrange("p (z j a b) -> p z a j b", a=P // 4, b=4, j=PACK),
+                )
 
-        def multiply(z, b, first, last):
+        def quantise(words, src, name, scales=None):
+            if scales is None:
+                scales = new_tile([P, words.shape[1]], U8, "plane_" + name)
+            nc.vector.quantize_mx(out=words.bitcast(FP8X4), scales=scales[:], in_=src)
+            return scales[:]
+
+        def quantise_e(c, words, src):
+            scales = quantise(words, src, "e%d" % c)
+            for z in range(PASSES):
+                codes["e", c, z] = words[:, P * z : P * (z + 1)]
+                plane["e", c, z] = scales[:, P * z : P * (z + 1)]
+
+        def quantise_y(z, slots, src, held=None):
+            if held is None:
+                held = new_tile([P, P * len(slots)], U32, "codes_y%d%d" % (z, slots.start))
+            words = held[:]
+            scales = quantise(words, src, "y%d%d" % (z, slots.start))
+            for n, t in enumerate(slots):
+                codes["y", t, z] = words[:, P * n : P * (n + 1)]
+                plane["y", t, z] = scales[:, P * n : P * (n + 1)]
+
+        def multiply(m, c, z, b, first, last):
             half = first // BANK * BANK
             nc.tensor.matmul_mx(
                 out=banks[b][:, : last - first],
-                lhsT=now["codes"][:, P * z : P * (z + 1)].bitcast(FP8X4),
-                lhsT_scale=now["plane"][:, P * z : P * (z + 1)],
+                lhsT=codes[m, c, z].bitcast(FP8X4),
+                lhsT_scale=plane[m, c, z],
                 rhs=x_picked[z, half][:, first - half : last - half].bitcast(FP8X4),
                 rhs_scale=scales_picked[4 * z : P, first:last],
                 start=(z == 0),
                 stop=(z == PASSES - 1),
             )
 
-        def product(m, c):
-            rows[m, c] = new_tile([P, S], F32, "rows_%s%d" % (m, c))
-            via = (0, 1) if (m, c) in lead else (2, 3)
+        def product(m, c, via):
+            if (m, c) == ("e", 3):
+                rows[m, c] = placed([P, S], F32, "rows_e3", ROWS)
+            else:
+                rows[m, c] = new_tile([P, S], F32, "rows_%s%d" % (m, c))
             for b, first, last in zip(via, HALVES, HALVES[1:]):
                 for z in range(PASSES):
-                    multiply(z, b, first, last)
+                    multiply(m, c, z, b, first, last)
                 nc.scalar.copy(rows[m, c][:, first:last], banks[b][:, : last - first])
 
-        def note(kind, c, groups, values):
-            for n, g in enumerate(groups):
-                picked[kind, c, g] = values[:, P * n : P * (n + 1)]
-            spans[kind, c, groups.start, groups.stop] = values
+        def gather(values, c, lst, first, last):
+            nc.vector.tensor_copy(values, rows["e", c][:].indirect(entries(lst, first, last)))
 
-        def room(name, groups, over):
-            return new_tile([P, P * len(groups)], F32, name)[:] if over is None else over
+        folded = [placed([P, V], F32, "folded%d" % t, FOLD + 4 * V * t) for t in range(PACK)]
 
-        def gather(kind, c, groups=range(GROUPS), over=None):
-            m, lst = {"1": ("e", pos1_t), "2": ("e", pos2_t), "cen": ("y", cen_t)}[kind]
-            values = room("g%s_%d%d" % (kind, c, groups.start), groups, over)
-            nc.vector.tensor_copy(values, rows[m, c][:].indirect(entries(lst, P * groups.start, P * groups.stop)))
-            note(kind, c, groups, values)
+        def larger(values, one, two, c, first, last):
+            nc.vector.tensor_tensor(values, one, two, MAX)
+            for t in range(PACK):
+                nc.sync.dma_start(folded[t][QUAD * c : QUAD * (c + 1), first:last], values[t:P:PACK, :])
 
-        def larger(c, groups=range(GROUPS), over=None):
-            values = room("gm_%d%d" % (c, groups.start), groups, over)
-            first = spans["1", c, 0, GROUPS][:, P * groups.start : P * groups.stop]
-            nc.vector.tensor_tensor(values, first, spans["2", c, groups.start, groups.stop], MAX)
-            note("max", c, groups, values)
-
-        def difference(c, groups, over):
-            looked_up = rows["e", c][:].indirect(entries(pos2_t, P * groups.start, P * groups.stop))
-            first = spans["1", c, groups.start, groups.stop]
-            nc.vector.tensor_tensor(over, looked_up, first, SUBTRACT)
-            note("diff", c, groups, over)
-
-        def excess(c, groups, engine):
-            values = room("gx_%d%d" % (c, groups.start), groups, None)
-            if engine == "s":
-                nc.scalar.activation(values, spans["diff", c, groups.start, groups.stop], RELU)
-            else:
-                nc.vector.tensor_scalar(values, spans["diff", c, groups.start, groups.stop], 0.0, 0.0, MAX, ADD)
-            note("excess", c, groups, values)
-
-        def edges(c, b, groups=range(GROUPS)):
-            for n, g in enumerate(groups):
-                block = banks[b][:, P * n : P * (n + 1)]
-                kinds = ("1", "excess", "cen") if len(groups) == 1 else ("cen", "max")
-                for kind in kinds:
-                    nc.tensor.matmul(
-                        block, picked[kind, c, g], ident[:], start=kind == kinds[0], stop=kind == kinds[-1], is_transpose=True
-                    )
-            quarter = slice(P // PACK * c, P // PACK * (c + 1))
-            sums = banks[b][:, : P * len(groups)].rearrange("v (g r u d) -> v g u r d", r=P // PACK, u=2, d=2)
-            if len(groups) == 1:
-                nc.scalar.activation(z_turned[:, groups.start, :, quarter, :], sums[:, 0], RELU)
-            else:
-                for u in range(2):
-                    nc.scalar.activation(z_turned[:, groups.start : groups.stop, u, quarter, :], sums[:, :, u], RELU)
-
-        def turn(groups, b, copy):
-            for n, g in enumerate(groups):
-                for u in range(2):
-                    pairs = z_turned[:, g, u].rearrange("v p d -> v (p d)").bitcast(F32)
-                    nc.tensor.transpose(banks[b][:, P * (2 * n + u) : P * (2 * n + u + 1)], pairs, ident[:])
-            z_ready[groups.start] = new_tile([P, len(groups) * K_PASS], BF16, "zb%d" % groups.start)
-            copy(
-                z_ready[groups.start][:].bitcast(F32).rearrange("p (g v u) -> p g v u", v=P, u=2),
-                banks[b][:, : 2 * P * len(groups)].rearrange("p (g u v) -> p g v u", v=P, u=2),
-            )
-
-        def project(groups, b, copy=nc.scalar.copy):
-            width = P * len(groups)
-            z_codes = new_tile([P, width], U32, "zq%d" % groups.start)
-            z_plane = new_tile([P, width], U8, "zs%d" % groups.start)
-            nc.vector.quantize_mx(out=z_codes[:].bitcast(FP8X4), scales=z_plane[:], in_=z_ready[groups.start][:])
-            nc.tensor.matmul_mx(
-                out=banks[b][:, :width],
-                lhsT=w3_codes[:].bitcast(FP4X4),
-                lhsT_scale=w3_plane[:],
-                rhs=z_codes[:].bitcast(FP8X4),
-                rhs_scale=z_plane[:],
-                start=True,
-                stop=True,
-            )
-            result = new_tile([P, width], F32, "res_sb%d" % groups.start)
-            copy(result[:], banks[b][:, :width])
-            nc.sync.dma_start(out[:, P * groups.start : P * groups.stop], result[:])
-
-        def keep_warm(b, passes):
-            for n in range(passes):
-                nc.tensor.matmul_mx(
-                    out=banks[b][:],
-                    lhsT=now["codes"][:, :P].bitcast(FP8X4),
-                    lhsT_scale=now["plane"][:, :P],
-                    rhs=x_picked[0, 0].bitcast(FP8X4),
-                    rhs_scale=scales_picked[:, :BANK],
-                    start=True,
-                    stop=True,
-                )
-
-        quantise_w("e", 0)
+        for z in range(PASSES):
+            cast_e(rounding[:, K_PASS * z : K_PASS * (z + 1)], raw_e[0][:, K_PASS * z : K_PASS * (z + 1)], "s")
+        quantise_e(0, placed([P, PASSES * P], U32, "codes_e0", S)[:], rounding)
         rows["e", 0] = new_tile([P, S], F32, "rows_e0")
         pieces = list(zip((0, 1, 4), FIRST_CUTS, FIRST_CUTS[1:]))
         for half in (0, BANK):
             x_picked[1, half] = placed([P, BANK], U32, "xg1_%d" % half, 2 * S + 4 * half)
         for b, first, last in pieces:
-            multiply(0, b, first, last)
+            multiply("e", 0, 0, b, first, last)
         for b, first, last in pieces:
             half = first // BANK * BANK
             nc.vector.tensor_copy(
                 x_picked[1, half][:, first - half : last - half], x_window[1][:].indirect(entries(offs_t, first, last))
             )
-            multiply(1, b, first, last)
+            multiply("e", 0, 1, b, first, last)
             nc.scalar.copy(rows["e", 0][:, first:last], banks[b][:, : last - first])
 
-        last = TILES - 1
-        halves = (range(0, 2), range(2, 4))
-        for c in range(last):
-            quantise_w(*lead[c])
-            product(*lead[c])
-            if c >= 2:
-                edges(c - 2, 7)
-            gather("1", c, over=staged[lead[c]][:, :V])
-            gather("2", c, over=staged[lead[c]][:, V:])
-            quantise_w(*middle[c])
-            product(*middle[c])
-            larger(c, over=staged[middle[c]][:, :V])
-            if c >= 1:
-                gather("cen", c - 1, over=buffers[c])
-        quantise_w(*lead[last])
-        product(*lead[last])
-        edges(last - 2, 4)
-        gather("cen", last - 1, over=staged[lead[last]][:, :V])
-        edges(last - 1, 2)
-        keep_warm(1, 4)
-        for n, groups in enumerate(halves):
-            gather("1", last, groups, over=staged[lead[last]][:, V + V // 2 * n : V + V // 2 * (n + 1)])
-        for n, groups in enumerate(halves):
-            difference(last, groups, over=buffers[last][:, V // 2 * n : V // 2 * (n + 1)])
-        for groups, engine in zip(halves, "ss"):
-            excess(last, groups, engine)
-        gather("cen", last, range(0, 1))
-        edges(last, 1, range(0, 1))
-        gather("cen", last, range(1, 2))
-        edges(last, 5, range(1, 2))
-        gather("cen", last, range(2, 3))
-        edges(last, 6, range(2, 3))
-        gather("cen", last, range(3, 4))
-        edges(last, 7, range(3, 4))
-        turn(range(0, 1), 0, nc.vector.tensor_copy)
-        turn(range(1, 2), 2, nc.vector.tensor_copy)
-        turn(range(2, 3), 3, nc.scalar.copy)
-        turn(range(3, 4), 4, nc.scalar.copy)
-        project(range(0, 1), 1, nc.scalar.copy)
-        project(range(1, 2), 5, nc.scalar.copy)
-        project(range(2, 3), 6, nc.scalar.copy)
-        project(range(3, 4), 7, nc.scalar.copy)
+        def round_e(c):
+            for z in range(PASSES):
+                part = slice(K_PASS * z, K_PASS * (z + 1))
+                cast_e(rounding[:, part], raw_e[c][:, part], "g")
+
+        def round_y(dst, z, n):
+            dealt = dst.rearrange("p (t m j) -> p m j t", t=PACK, j=PACK)
+            nc.scalar.copy(
+                dealt[:, P // 2 * n : P // 2 * (n + 1)], raw_y[z, n].rearrange("p (j m t) -> p m j t", j=PACK, t=PACK)
+            )
+
+        round_b = new_tile([P, PACK * H], BF16, "round_b")[:]
+        one, two = {}, {}
+        for c in range(3):
+            round_e(c + 1)
+            quantise_e(c + 1, placed([P, PASSES * P], U32, "codes_e%d" % (c + 1), 4 * T * (c + 1))[:], rounding)
+            if c > 0:
+                larger(behind_rounding(c + 1, 2), one[c - 1], two[c - 1], c - 1, 0, V)
+            if c == 2:
+                round_y(round_b, 1, 0)
+                round_y(round_b, 1, 1)
+            product("e", c + 1, (2, 3) if c % 2 == 0 else (0, 1))
+            if c == 0:
+                round_a = placed([P, PACK * H], BF16, "round_a", 4 * T)[:]
+            if c < 2:
+                round_y(round_a, 0, c)
+            one[c], two[c] = behind_rounding(c + 1, 0), behind_rounding(c + 1, 1)
+            gather(one[c], c, pos1_t, 0, V)
+            gather(two[c], c, pos2_t, 0, V)
+
+        quantise_y(0, range(0, 4), round_a)
+        larger(raw_y[0, 1][:, :V], one[2], two[2], 2, 0, V)
+        quantise_y(1, range(0, 2), round_b[:, : 2 * K_PASS])
+        product("y", 0, (4, 5))
+        product("y", 1, (6, 7))
+        LAST = ROWS + 4 * S
+        last_one = placed([P, HALF], F32, "last_one", LAST)[:]
+        last_two = placed([P, HALF], F32, "last_two", LAST + 2048)[:]
+        gather(last_one, 3, pos1_t, 0, HALF)
+        gather(last_two, 3, pos2_t, 0, HALF)
+        larger(new_tile([P, HALF], F32, "most30")[:], last_one, last_two, 3, 0, HALF)
+        end_one = placed([P, HALF], F32, "end_one", LAST)[:]
+        end_two = placed([P, HALF], F32, "end_two", LAST + 1536)[:]
+        quantise_y(1, range(2, 4), round_b[:, 2 * K_PASS :], placed([P, 2 * P], U32, "codes_y12", LAST + 2560))
+        gather(end_one, 3, pos1_t, HALF, V)
+        gather(end_two, 3, pos2_t, HALF, V)
+        product("y", 2, (4, 5))
+        product("y", 3, (6, 7))
+        larger(placed([P, HALF], F32, "most31", LAST + 6144)[:], end_one, end_two, 3, HALF, V)
+
+        z_ready, sums = {}, {}
+
+        def relu_on_scalar(first, width, part):
+            nc.scalar.activation(
+                z_ready[first][:].rearrange("p (a b t) -> p a t b", b=4, t=PACK)[:, part],
+                sums[first][:].rearrange("p (t a b) -> p a t b", b=4, t=PACK)[:, part],
+                RELU,
+                bias=zero[:, :1],
+            )
+
+        for first, last in PIECES:
+            width = last - first
+            if last < V:
+                sums[first] = new_tile([P, PACK * width], F32, "sums%d" % first)
+            else:
+                sums[first] = placed([P, PACK * width], F32, "sums%d" % first, LAST + 6144 - 1536)
+            for t in range(PACK):
+                nc.vector.tensor_tensor(
+                    sums[first][:, width * t : width * (t + 1)],
+                    rows["y", t][:].indirect(entries(cen_t, first, last)),
+                    folded[t][:, first:last],
+                    ADD,
+                )
+            z_ready[first] = new_tile([P, PACK * width], BF16, "z%d" % first)
+            relu_on_scalar(first, width, slice(0, width // 4 if last < V else width // 8))
+        for b, (first, last) in enumerate(PIECES):
+            width = last - first
+            if b == 1:
+                end = PIECES[-1][0]
+                nc.vector.tensor_scalar(
+                    z_ready[end][:].rearrange("p (v t) -> p v t", t=PACK)[:, P // 2 :],
+                    sums[end][:].rearrange("p (t v) -> p v t", t=PACK)[:, P // 2 :],
+                    0.0,
+                    0.0,
+                    MAX,
+                    ADD,
+                )
+            z_codes = new_tile([P, width], U32, "zq%d" % first)[:]
+            held = placed([P, width], U8, "plane_z%d" % first, LAST + 6144 + 512 + first) if last < V else None
+            z_plane = quantise(z_codes, z_ready[first][:], "z%d" % first, held)
+            nc.tensor.matmul_mx(
+                out=banks[b][:, :width],
+                lhsT=w3_codes[:].bitcast(FP4X4),
+                lhsT_scale=w3_plane[:],
+                rhs=z_codes.bitcast(FP8X4),
+                rhs_scale=z_plane,
+                start=True,
+                stop=True,
+            )
+            result = new_tile([P, width], F32, "result%d" % first)
+            nc.scalar.copy(result[:], banks[b][:, :width])
+            nc.sync.dma_start(out[:, first:last], result[:])

@@ -59,13 +59,12 @@ def tile_picked_edgecv_relu_p_kernel(
         STRIP = 4 * T * PASSES
         FOLD = STRIP + 8 * T
         RAW = FOLD + 8 * HALF * 2 * PACK
-        raw_e = [placed([P, PASSES * K_PASS], F32, "raw_e%d" % c, RAW + 6144 * c + 1024)[:] for c in range(TILES)]
-        ROWS = RAW + 6144 * TILES
-        raw_y = {(z, n): new_tile([P, PACK * H // 2], F32, "raw_y%d%d" % (z, n))[:] for z, n in ((0, 0), (0, 1), (1, 0))}
-        raw_y[1, 1] = placed([P, PACK * H // 2], F32, "raw_y11", ROWS)[:]
+        raw_e = [placed([P, PASSES * K_PASS], F32, "raw_e%d" % c, RAW + 7168 * c + 1024)[:] for c in range(TILES)]
+        ROWS = RAW + 7168 * TILES
+        raw_y = [placed([P, PACK * H], F32, "raw_y%d" % z, ROWS + 8 * S * z)[:] for z in range(PASSES)]
 
         def behind_rounding(c, n):
-            return placed([P, V], F32, "behind%d%d" % (c, n), RAW + 6144 * c + 2048 * n)[:]
+            return placed([P, V], F32, "behind%d%d" % (c, n), RAW + 7168 * c + (0, 2048, 4608)[n])[:]
 
         def load_e(c):
             by_pass = raw_e[c].rearrange("p (z j i) -> p z j i", z=PASSES, j=PACK)
@@ -73,9 +72,9 @@ def tile_picked_edgecv_relu_p_kernel(
                 src = w2[K_PASS * z : K_PASS * (z + 1), P * c : P * (c + 1)]
                 nc.sync.dma_start(by_pass[:, z], src.rearrange("(p j) i -> p j i", j=PACK))
 
-        def load_y(z, n):
-            src = w1[K_PASS * z : K_PASS * (z + 1), H // 2 * n : H // 2 * (n + 1)]
-            nc.sync.dma_start(raw_y[z, n].rearrange("p (j i) -> p j i", j=PACK), src.rearrange("(p j) i -> p j i", j=PACK))
+        def load_y(z):
+            src = w1[K_PASS * z : K_PASS * (z + 1), :]
+            nc.sync.dma_start(raw_y[z], src.rearrange("(p j) i -> p (j i)", j=PACK))
 
         x_window = {}
 
@@ -98,11 +97,9 @@ def tile_picked_edgecv_relu_p_kernel(
         pos1_t = load_list(pos1, "pos1_t")
         pos2_t = load_list(pos2, "pos2_t")
         load_e(2)
-        load_y(0, 0)
+        load_y(0)
         load_e(3)
-        load_y(0, 1)
-        load_y(1, 0)
-        load_y(1, 1)
+        load_y(1)
         cen_t = load_list(cen, "cen_t")
         w3_codes = new_tile([P, 2 * N], U8, "w3w")
         nc.sync.dma_start(w3_codes[:], w3_words[0])
@@ -156,11 +153,11 @@ def tile_picked_edgecv_relu_p_kernel(
                 codes["e", c, z] = words[:, P * z : P * (z + 1)]
                 plane["e", c, z] = scales[:, P * z : P * (z + 1)]
 
-        def quantise_y(z, slots, src, held=None):
+        def quantise_y(z, slots, src, held=None, held_plane=None):
             if held is None:
                 held = new_tile([P, P * len(slots)], U32, "codes_y%d%d" % (z, slots.start))
             words = held[:]
-            scales = quantise(words, src, "y%d%d" % (z, slots.start))
+            scales = quantise(words, src, "y%d%d" % (z, slots.start), held_plane)
             for n, t in enumerate(slots):
                 codes["y", t, z] = words[:, P * n : P * (n + 1)]
                 plane["y", t, z] = scales[:, P * n : P * (n + 1)]
@@ -178,8 +175,8 @@ def tile_picked_edgecv_relu_p_kernel(
             )
 
         def product(m, c, via):
-            if (m, c) == ("e", 3):
-                rows[m, c] = placed([P, S], F32, "rows_e3", ROWS)
+            if m == "e" and c >= 2:
+                rows[m, c] = placed([P, S], F32, "rows_e%d" % c, ROWS + 8 * S * (c - 2))
             else:
                 rows[m, c] = new_tile([P, S], F32, "rows_%s%d" % (m, c))
             for b, first, last in zip(via, HALVES, HALVES[1:]):
@@ -221,9 +218,8 @@ def tile_picked_edgecv_relu_p_kernel(
 
         def round_y(dst, z, n):
             dealt = dst.rearrange("p (t m j) -> p m j t", t=PACK, j=PACK)
-            nc.scalar.copy(
-                dealt[:, P // 2 * n : P // 2 * (n + 1)], raw_y[z, n].rearrange("p (j m t) -> p m j t", j=PACK, t=PACK)
-            )
+            half = slice(P // 2 * n, P // 2 * (n + 1))
+            nc.scalar.copy(dealt[:, half], raw_y[z].rearrange("p (j m t) -> p m j t", j=PACK, t=PACK)[:, half])
 
         round_b = new_tile([P, PACK * H], BF16, "round_b")[:]
         one, two = {}, {}
@@ -233,36 +229,37 @@ def tile_picked_edgecv_relu_p_kernel(
             if c > 0:
                 larger(behind_rounding(c + 1, 2), one[c - 1], two[c - 1], c - 1, 0, V)
             if c == 2:
+                quantise_y(0, range(0, 4), round_a, None, placed([P, H], U8, "plane_y0", RAW + 7168 * 3 + 4096))
                 round_y(round_b, 1, 0)
                 round_y(round_b, 1, 1)
             product("e", c + 1, (2, 3) if c % 2 == 0 else (0, 1))
             if c == 0:
                 round_a = placed([P, PACK * H], BF16, "round_a", 4 * T)[:]
-            if c < 2:
-                round_y(round_a, 0, c)
+                round_y(round_a, 0, 0)
+                round_y(round_a, 0, 1)
             one[c], two[c] = behind_rounding(c + 1, 0), behind_rounding(c + 1, 1)
             gather(one[c], c, pos1_t, 0, V)
             gather(two[c], c, pos2_t, 0, V)
 
-        quantise_y(0, range(0, 4), round_a)
-        larger(raw_y[0, 1][:, :V], one[2], two[2], 2, 0, V)
+        LAST = ROWS + 16 * S
         quantise_y(1, range(0, 2), round_b[:, : 2 * K_PASS])
         product("y", 0, (4, 5))
         product("y", 1, (6, 7))
-        LAST = ROWS + 4 * S
-        last_one = placed([P, HALF], F32, "last_one", LAST)[:]
-        last_two = placed([P, HALF], F32, "last_two", LAST + 2048)[:]
+        larger(placed([P, HALF], F32, "most20", ROWS + 12 * S)[:], one[2][:, :HALF], two[2][:, :HALF], 2, 0, HALF)
+        last_one = placed([P, HALF], F32, "last_one", LAST + 1024)[:]
+        last_two = placed([P, HALF], F32, "last_two", LAST + 4096)[:]
         gather(last_one, 3, pos1_t, 0, HALF)
         gather(last_two, 3, pos2_t, 0, HALF)
         larger(new_tile([P, HALF], F32, "most30")[:], last_one, last_two, 3, 0, HALF)
-        end_one = placed([P, HALF], F32, "end_one", LAST)[:]
-        end_two = placed([P, HALF], F32, "end_two", LAST + 1536)[:]
-        quantise_y(1, range(2, 4), round_b[:, 2 * K_PASS :], placed([P, 2 * P], U32, "codes_y12", LAST + 2560))
+        quantise_y(1, range(2, 4), round_b[:, 2 * K_PASS :], placed([P, 2 * P], U32, "codes_y12", LAST + 512))
+        end_one = placed([P, HALF], F32, "end_one", LAST + 1536)[:]
+        end_two = placed([P, HALF], F32, "end_two", LAST + 3584)[:]
         gather(end_one, 3, pos1_t, HALF, V)
         gather(end_two, 3, pos2_t, HALF, V)
         product("y", 2, (4, 5))
         product("y", 3, (6, 7))
-        larger(placed([P, HALF], F32, "most31", LAST + 6144)[:], end_one, end_two, 3, HALF, V)
+        larger(placed([P, HALF], F32, "most21", LAST + 4608)[:], one[2][:, HALF:], two[2][:, HALF:], 2, HALF, V)
+        larger(placed([P, HALF], F32, "most31", LAST + 8192)[:], end_one, end_two, 3, HALF, V)
 
         z_ready, sums = {}, {}
 
@@ -279,7 +276,7 @@ def tile_picked_edgecv_relu_p_kernel(
             if last < V:
                 sums[first] = new_tile([P, PACK * width], F32, "sums%d" % first)
             else:
-                sums[first] = placed([P, PACK * width], F32, "sums%d" % first, LAST + 6144 - 1536)
+                sums[first] = placed([P, PACK * width], F32, "sums%d" % first, LAST + 8192 - 1536)
             for t in range(PACK):
                 nc.vector.tensor_tensor(
                     sums[first][:, width * t : width * (t + 1)],
@@ -302,7 +299,7 @@ def tile_picked_edgecv_relu_p_kernel(
                     ADD,
                 )
             z_codes = new_tile([P, width], U32, "zq%d" % first)[:]
-            held = placed([P, width], U8, "plane_z%d" % first, LAST + 6144 + 512 + first) if last < V else None
+            held = placed([P, width], U8, "plane_z%d" % first, LAST + 8192 + 512 + first) if last < V else None
             z_plane = quantise(z_codes, z_ready[first][:], "z%d" % first, held)
             nc.tensor.matmul_mx(
                 out=banks[b][:, :width],

@@ -61,20 +61,19 @@ def tile_picked_edgecv_relu_p_kernel(
         RAW = FOLD + 8 * HALF * 2 * PACK
         raw_e = [placed([P, PASSES * K_PASS], F32, "raw_e%d" % c, RAW + 7168 * c + 1024)[:] for c in range(TILES)]
         ROWS = RAW + 7168 * TILES
-        raw_y = [placed([P, PACK * H], F32, "raw_y%d" % z, ROWS + 8 * S * z)[:] for z in range(PASSES)]
+        raw_first = placed([P, PACK * H], F32, "raw_first", ROWS)[:]
+        raw_last = placed([P, PACK * H], F32, "raw_last", ROWS + 8 * S)[:]
+        ROUND = ROWS + 18 * S
 
         def behind_rounding(c, n):
             return placed([P, V], F32, "behind%d%d" % (c, n), RAW + 7168 * c + (0, 2048, 4608)[n])[:]
 
-        def load_e(c):
+        def load_e(c, passes=range(PASSES)):
             by_pass = raw_e[c].rearrange("p (z j i) -> p z j i", z=PASSES, j=PACK)
-            for z in range(PASSES):
+            for z in passes:
                 src = w2[K_PASS * z : K_PASS * (z + 1), P * c : P * (c + 1)]
                 nc.sync.dma_start(by_pass[:, z], src.rearrange("(p j) i -> p j i", j=PACK))
 
-        def load_y(z):
-            src = w1[K_PASS * z : K_PASS * (z + 1), :]
-            nc.sync.dma_start(raw_y[z], src.rearrange("(p j) i -> p (j i)", j=PACK))
 
         x_window = {}
 
@@ -91,15 +90,16 @@ def tile_picked_edgecv_relu_p_kernel(
                 scale_window[QUAD * q : QUAD * q + 4 * PASSES, :].bitcast(I32),
                 x_scales[:, 4 * q : 4 * q + 4, :].bitcast(I32),
             )
-        load_e(0)
+        load_e(0, range(0, 1))
         load_x(1)
+        load_e(0, range(1, 2))
         load_e(1)
         pos1_t = load_list(pos1, "pos1_t")
         pos2_t = load_list(pos2, "pos2_t")
         load_e(2)
-        load_y(0)
+        nc.sync.dma_start(raw_first, w1[:K_PASS, :].rearrange("(p j) i -> p (j i)", j=PACK))
         load_e(3)
-        load_y(1)
+        nc.sync.dma_start(raw_last, w1[K_PASS:, :].rearrange("(p j) i -> p (j i)", j=PACK))
         cen_t = load_list(cen, "cen_t")
         w3_codes = new_tile([P, 2 * N], U8, "w3w")
         nc.sync.dma_start(w3_codes[:], w3_words[0])
@@ -116,8 +116,8 @@ def tile_picked_edgecv_relu_p_kernel(
 
         x_picked = {}
         x_first = new_tile([P, S], U32, "xg0")
+        scales_picked = new_tile([P, S], U8, "xsg")
         nc.vector.tensor_copy(x_first[:], x_window[0][:].indirect(offs_t[:]))
-        scales_picked = placed([P, S], U8, "xsg", 0)
         nc.vector.tensor_copy(scales_picked[:], scale_window[:].indirect(offs_t[:]))
         for half in (0, BANK):
             x_picked[0, half] = x_first[:, half : half + BANK]
@@ -148,7 +148,7 @@ def tile_picked_edgecv_relu_p_kernel(
             return scales[:]
 
         def quantise_e(c, words, src):
-            scales = quantise(words, src, "e%d" % c)
+            scales = quantise(words, src, "e%d" % c, placed([P, PASSES * P], U8, "plane_e1", ROUND) if c == 1 else None)
             for z in range(PASSES):
                 codes["e", c, z] = words[:, P * z : P * (z + 1)]
                 plane["e", c, z] = scales[:, P * z : P * (z + 1)]
@@ -176,7 +176,7 @@ def tile_picked_edgecv_relu_p_kernel(
 
         def product(m, c, via):
             if m == "e" and c >= 2:
-                rows[m, c] = placed([P, S], F32, "rows_e%d" % c, ROWS + 8 * S * (c - 2))
+                rows[m, c] = placed([P, S], F32, "rows_e%d" % c, ROWS if c == 2 else ROUND - 2048)
             else:
                 rows[m, c] = new_tile([P, S], F32, "rows_%s%d" % (m, c))
             for b, first, last in zip(via, HALVES, HALVES[1:]):
@@ -194,20 +194,29 @@ def tile_picked_edgecv_relu_p_kernel(
             for t in range(PACK):
                 nc.sync.dma_start(folded[t][QUAD * c : QUAD * (c + 1), first:last], values[t:P:PACK, :])
 
-        for z in range(PASSES):
-            cast_e(rounding[:, K_PASS * z : K_PASS * (z + 1)], raw_e[0][:, K_PASS * z : K_PASS * (z + 1)], "s")
-        quantise_e(0, placed([P, PASSES * P], U32, "codes_e0", S)[:], rounding)
+        first_rounding = new_tile([P, PASSES * K_PASS], BF16, "first_rounding")[:]
+
+        def quantise_first(z, words):
+            part = slice(K_PASS * z, K_PASS * (z + 1))
+            cast_e(first_rounding[:, part], raw_e[0][:, part], "s")
+            codes["e", 0, z] = words
+            plane["e", 0, z] = quantise(words, first_rounding[:, part], "e0%d" % z)
+
+        quantise_first(0, new_tile([P, P], U32, "codes_e00")[:])
         rows["e", 0] = new_tile([P, S], F32, "rows_e0")
         pieces = list(zip((0, 1, 4), FIRST_CUTS, FIRST_CUTS[1:]))
-        for half in (0, BANK):
-            x_picked[1, half] = placed([P, BANK], U32, "xg1_%d" % half, 2 * S + 4 * half)
         for b, first, last in pieces:
             multiply("e", 0, 0, b, first, last)
+        x_picked[1, 0] = new_tile([P, BANK], U32, "xg1_0")[:]
         for b, first, last in pieces:
             half = first // BANK * BANK
+            if first == BANK:
+                quantise_first(1, new_tile([P, P], U32, "codes_e01")[:])
+                x_picked[1, BANK] = placed([P, BANK], U32, "xg1_512", RAW + 4096)[:]
             nc.vector.tensor_copy(
                 x_picked[1, half][:, first - half : last - half], x_window[1][:].indirect(entries(offs_t, first, last))
             )
+        for b, first, last in pieces:
             multiply("e", 0, 1, b, first, last)
             nc.scalar.copy(rows["e", 0][:, first:last], banks[b][:, : last - first])
 
@@ -216,12 +225,13 @@ def tile_picked_edgecv_relu_p_kernel(
                 part = slice(K_PASS * z, K_PASS * (z + 1))
                 cast_e(rounding[:, part], raw_e[c][:, part], "g")
 
-        def round_y(dst, z, n):
-            dealt = dst.rearrange("p (t m j) -> p m j t", t=PACK, j=PACK)
-            half = slice(P // 2 * n, P // 2 * (n + 1))
-            nc.scalar.copy(dealt[:, half], raw_y[z].rearrange("p (j m t) -> p m j t", j=PACK, t=PACK)[:, half])
+        def dealt(dst):
+            return dst.rearrange("p (t m j) -> p m j t", t=PACK, j=PACK)
 
-        round_b = new_tile([P, PACK * H], BF16, "round_b")[:]
+        def by_line(src):
+            return src.rearrange("p (j m t) -> p m j t", j=PACK, t=PACK)
+
+        round_b = new_tile([P, 2 * K_PASS], BF16, "round_b")[:]
         one, two = {}, {}
         for c in range(3):
             round_e(c + 1)
@@ -230,36 +240,49 @@ def tile_picked_edgecv_relu_p_kernel(
                 larger(behind_rounding(c + 1, 2), one[c - 1], two[c - 1], c - 1, 0, V)
             if c == 2:
                 quantise_y(0, range(0, 4), round_a, None, placed([P, H], U8, "plane_y0", RAW + 7168 * 3 + 4096))
-                round_y(round_b, 1, 0)
-                round_y(round_b, 1, 1)
+                nc.scalar.copy(round_b.rearrange("p (t m j) -> p m j t", t=2, j=PACK), by_line(raw_last)[:, :, :, :2])
             product("e", c + 1, (2, 3) if c % 2 == 0 else (0, 1))
             if c == 0:
-                round_a = placed([P, PACK * H], BF16, "round_a", 4 * T)[:]
-                round_y(round_a, 0, 0)
-                round_y(round_a, 0, 1)
+                round_a = placed([P, PACK * H], BF16, "round_a", ROUND)[:]
+                for half in (slice(0, P // 2), slice(P // 2, P)):
+                    nc.scalar.copy(dealt(round_a)[:, half], by_line(raw_first)[:, half])
             one[c], two[c] = behind_rounding(c + 1, 0), behind_rounding(c + 1, 1)
             gather(one[c], c, pos1_t, 0, V)
             gather(two[c], c, pos2_t, 0, V)
 
-        LAST = ROWS + 16 * S
-        quantise_y(1, range(0, 2), round_b[:, : 2 * K_PASS])
+        round_c = placed([P, 2 * K_PASS], BF16, "round_c", ROUND + 2048)[:]
+        nc.scalar.copy(round_c.rearrange("p (t m j) -> p m j t", t=2, j=PACK), by_line(raw_last)[:, :, :, 2:])
+
+        LAST = ROWS + 24 * S
+        quantise_y(1, range(0, 2), round_b)
         product("y", 0, (4, 5))
         product("y", 1, (6, 7))
-        larger(placed([P, HALF], F32, "most20", ROWS + 12 * S)[:], one[2][:, :HALF], two[2][:, :HALF], 2, 0, HALF)
-        last_one = placed([P, HALF], F32, "last_one", LAST + 1024)[:]
-        last_two = placed([P, HALF], F32, "last_two", LAST + 4096)[:]
+
+        def behind_last(n):
+            return placed([P, HALF], F32, "behind_last%d" % n, ROWS + 8 * S + 4 * HALF * n)[:]
+
+        last_one = new_tile([P, HALF], F32, "last_one")[:]
+        last_two = new_tile([P, HALF], F32, "last_two")[:]
         gather(last_one, 3, pos1_t, 0, HALF)
         gather(last_two, 3, pos2_t, 0, HALF)
-        larger(new_tile([P, HALF], F32, "most30")[:], last_one, last_two, 3, 0, HALF)
-        quantise_y(1, range(2, 4), round_b[:, 2 * K_PASS :], placed([P, 2 * P], U32, "codes_y12", LAST + 512))
-        end_one = placed([P, HALF], F32, "end_one", LAST + 1536)[:]
-        end_two = placed([P, HALF], F32, "end_two", LAST + 3584)[:]
+        most = {2: behind_last(0), 3: behind_last(1)}
+        nc.vector.tensor_tensor(most[2], one[2][:, :HALF], two[2][:, :HALF], MAX)
+        nc.vector.tensor_tensor(most[3], last_one, last_two, MAX)
+        for t in range(PACK):
+            for c in (2, 3):
+                nc.sync.dma_start(folded[t][QUAD * c : QUAD * (c + 1), :HALF], most[c][t:P:PACK, :])
+        quantise_y(1, range(2, 4), round_c)
+        end_one, end_two = behind_last(2), behind_last(3)
         gather(end_one, 3, pos1_t, HALF, V)
         gather(end_two, 3, pos2_t, HALF, V)
         product("y", 2, (4, 5))
         product("y", 3, (6, 7))
-        larger(placed([P, HALF], F32, "most21", LAST + 4608)[:], one[2][:, HALF:], two[2][:, HALF:], 2, HALF, V)
-        larger(placed([P, HALF], F32, "most31", LAST + 8192)[:], end_one, end_two, 3, HALF, V)
+        most = {2: behind_last(4), 3: placed([P, HALF], F32, "most31", LAST + 8192)[:]}
+        nc.vector.tensor_tensor(most[2], one[2][:, HALF:], two[2][:, HALF:], MAX)
+        nc.vector.tensor_tensor(most[3], end_one, end_two, MAX)
+        for t in range(PACK):
+            for c in (2, 3):
+                nc.sync.dma_start(folded[t][QUAD * c : QUAD * (c + 1), HALF:], most[c][t:P:PACK, :])
 
         z_ready, sums = {}, {}
 

@@ -17,6 +17,7 @@ RELU = mybir.ActivationFunctionType.Relu
 MAX = mybir.AluOpType.max
 MULT = mybir.AluOpType.mult
 ADD = mybir.AluOpType.add
+SUBTRACT = mybir.AluOpType.subtract
 
 P = 128
 PACK = 4
@@ -63,7 +64,7 @@ def tile_picked_edgecv_relu_p_kernel(
         ROWS = RAW + 7168 * TILES
         raw_first = placed([P, PACK * H], F32, "raw_first", ROWS)[:]
         raw_last = placed([P, PACK * H], F32, "raw_last", ROWS + 8 * S)[:]
-        ROUND = ROWS + 18 * S
+        ROUND = ROWS + 19 * S
 
         def behind_rounding(c, n):
             return placed([P, V], F32, "behind%d%d" % (c, n), RAW + 7168 * c + (0, 2048, 4608)[n])[:]
@@ -148,7 +149,7 @@ def tile_picked_edgecv_relu_p_kernel(
             return scales[:]
 
         def quantise_e(c, words, src):
-            scales = quantise(words, src, "e%d" % c, placed([P, PASSES * P], U8, "plane_e1", ROUND) if c == 1 else None)
+            scales = quantise(words, src, "e%d" % c)
             for z in range(PASSES):
                 codes["e", c, z] = words[:, P * z : P * (z + 1)]
                 plane["e", c, z] = scales[:, P * z : P * (z + 1)]
@@ -176,7 +177,9 @@ def tile_picked_edgecv_relu_p_kernel(
 
         def product(m, c, via):
             if m == "e" and c >= 2:
-                rows[m, c] = placed([P, S], F32, "rows_e%d" % c, ROWS if c == 2 else ROUND - 2048)
+                rows[m, c] = placed([P, S], F32, "rows_e%d" % c, ROWS if c == 2 else ROUND - 3072)
+            elif (m, c) == ("e", 1):
+                rows[m, c] = placed([P, S], F32, "rows_e1", RAW + 7168 * 2 - 2048)
             else:
                 rows[m, c] = new_tile([P, S], F32, "rows_%s%d" % (m, c))
             for b, first, last in zip(via, HALVES, HALVES[1:]):
@@ -191,6 +194,9 @@ def tile_picked_edgecv_relu_p_kernel(
 
         def larger(values, one, two, c, first, last):
             nc.vector.tensor_tensor(values, one, two, MAX)
+            fold(values, c, first, last)
+
+        def fold(values, c, first, last):
             for t in range(PACK):
                 nc.sync.dma_start(folded[t][QUAD * c : QUAD * (c + 1), first:last], values[t:P:PACK, :])
 
@@ -223,7 +229,7 @@ def tile_picked_edgecv_relu_p_kernel(
         def round_e(c):
             for z in range(PASSES):
                 part = slice(K_PASS * z, K_PASS * (z + 1))
-                cast_e(rounding[:, part], raw_e[c][:, part], "g")
+                cast_e(rounding[:, part], raw_e[c][:, part], "s" if (c, z) == (2, 0) else "g")
 
         def dealt(dst):
             return dst.rearrange("p (t m j) -> p m j t", t=PACK, j=PACK)
@@ -235,25 +241,42 @@ def tile_picked_edgecv_relu_p_kernel(
         one, two = {}, {}
         for c in range(3):
             round_e(c + 1)
-            quantise_e(c + 1, placed([P, PASSES * P], U32, "codes_e%d" % (c + 1), 4 * T * (c + 1))[:], rounding)
-            if c > 0:
+            if c == 0:
+                for z in range(PASSES):
+                    codes["e", 1, z] = placed([P, P], U32, "codes_e1%d" % z, 4 * T + 4 * P * z)[:]
+                    held = placed([P, P], U8, "plane_e1%d" % z, ROUND + P * z)
+                    plane["e", 1, z] = quantise(codes["e", 1, z], rounding[:, K_PASS * z : K_PASS * (z + 1)], "", held)
+            else:
+                quantise_e(c + 1, new_tile([P, PASSES * P], U32, "codes_e%d" % (c + 1))[:], rounding)
+            if c == 1:
+                difference = behind_rounding(c + 1, 2)
+                nc.vector.tensor_tensor(difference, rows["e", 0][:].indirect(pos2_t[:]), one[0], SUBTRACT)
+            if c == 2:
                 larger(behind_rounding(c + 1, 2), one[c - 1], two[c - 1], c - 1, 0, V)
             if c == 2:
                 quantise_y(0, range(0, 4), round_a, None, placed([P, H], U8, "plane_y0", RAW + 7168 * 3 + 4096))
                 nc.scalar.copy(round_b.rearrange("p (t m j) -> p m j t", t=2, j=PACK), by_line(raw_last)[:, :, :, :2])
             product("e", c + 1, (2, 3) if c % 2 == 0 else (0, 1))
+            if c == 1:
+                excess = placed([P, V], F32, "excess", ROWS + 4 * S)[:]
+                nc.scalar.activation(excess, difference, RELU, bias=zero[:, :1])
             if c == 0:
                 round_a = placed([P, PACK * H], BF16, "round_a", ROUND)[:]
                 for half in (slice(0, P // 2), slice(P // 2, P)):
                     nc.scalar.copy(dealt(round_a)[:, half], by_line(raw_first)[:, half])
-            one[c], two[c] = behind_rounding(c + 1, 0), behind_rounding(c + 1, 1)
+            one[c] = new_tile([P, V], F32, "one1")[:] if c == 1 else behind_rounding(c + 1, 0)
             gather(one[c], c, pos1_t, 0, V)
-            gather(two[c], c, pos2_t, 0, V)
+            if c > 0:
+                two[c] = behind_rounding(c + 1, 1)
+                gather(two[c], c, pos2_t, 0, V)
+        most_first = placed([P, V], F32, "most_first", ROUND + 1024)[:]
+        nc.gpsimd.tensor_tensor(most_first, one[0], excess, ADD)
+        fold(most_first, 0, 0, V)
 
-        round_c = placed([P, 2 * K_PASS], BF16, "round_c", ROUND + 2048)[:]
+        round_c = placed([P, 2 * K_PASS], BF16, "round_c", ROUND + 3072)[:]
         nc.scalar.copy(round_c.rearrange("p (t m j) -> p m j t", t=2, j=PACK), by_line(raw_last)[:, :, :, 2:])
 
-        LAST = ROWS + 24 * S
+        LAST = ROWS + 25 * S
         quantise_y(1, range(0, 2), round_b)
         product("y", 0, (4, 5))
         product("y", 1, (6, 7))

@@ -82,15 +82,12 @@ def tile_picked_edgecv_relu_p_kernel(
             x_window[z] = placed([P, T], U32, "x_window%d" % z, 4 * T * z)
             nc.sync.dma_start(x_window[z][:].bitcast(I32), x_words[z].rearrange("p c t -> p (c t)").bitcast(I32))
 
+        scale_window = new_tile([P, T], U8, "xs_win")
+        nc.sync.dma_start(scale_window[:QUAD, :].bitcast(I32), x_scales.rearrange("z q c -> (z q) c").bitcast(I32))
+        nc.vector.memset(scale_window[QUAD : 2 * QUAD, :].bitcast(I32), 0)
+        nc.vector.memset(scale_window[2 * QUAD :, :].bitcast(I32), 0)
         offs_t = load_list(offs, "offs_t")
         load_x(0)
-        scale_window = new_tile([P, T], U8, "xs_win")
-        nc.vector.memset(scale_window[:].bitcast(I32), 0)
-        for q in range(4):
-            nc.sync.dma_start(
-                scale_window[QUAD * q : QUAD * q + 4 * PASSES, :].bitcast(I32),
-                x_scales[:, 4 * q : 4 * q + 4, :].bitcast(I32),
-            )
         load_e(0, range(0, 1))
         load_x(1)
         load_e(0, range(1, 2))
@@ -117,9 +114,18 @@ def tile_picked_edgecv_relu_p_kernel(
 
         x_picked = {}
         x_first = new_tile([P, S], U32, "xg0")
+        scale_rows = new_tile([P, S], U8, "xsr")
         scales_picked = new_tile([P, S], U8, "xsg")
+        nc.gpsimd.memset(scales_picked[:].bitcast(I32), 0)
+        nc.vector.tensor_copy(scale_rows[:], scale_window[:].indirect(offs_t[:]))
+        for z in range(PASSES):
+            for q in range(4):
+                row = 16 * z + 4 * q
+                nc.scalar.dma_start(
+                    scales_picked[QUAD * q + 4 * z : QUAD * q + 4 * z + 4, :].bitcast(I32),
+                    scale_rows[row : row + 4, :].bitcast(I32),
+                )
         nc.vector.tensor_copy(x_first[:], x_window[0][:].indirect(offs_t[:]))
-        nc.vector.tensor_copy(scales_picked[:], scale_window[:].indirect(offs_t[:]))
         for half in (0, BANK):
             x_picked[0, half] = x_first[:, half : half + BANK]
 

@@ -115,14 +115,15 @@ def tile_picked_edgecv_relu_p_kernel(
         x_picked = {}
         x_first = new_tile([P, S], U32, "xg0")
         scale_rows = new_tile([P, S], U8, "xsr")
-        scales_picked = new_tile([P, S], U8, "xsg")
-        nc.gpsimd.memset(scales_picked[:].bitcast(I32), 0)
+        scales_picked = [new_tile([P, S], U8, "xsg%d" % z) for z in range(PASSES)]
+        for z in range(PASSES):
+            nc.gpsimd.memset(scales_picked[z][:].bitcast(I32), 0)
         nc.vector.tensor_copy(scale_rows[:], scale_window[:].indirect(offs_t[:]))
         for z in range(PASSES):
             for q in range(4):
                 row = 16 * z + 4 * q
                 nc.scalar.dma_start(
-                    scales_picked[QUAD * q + 4 * z : QUAD * q + 4 * z + 4, :].bitcast(I32),
+                    scales_picked[z][QUAD * q : QUAD * q + 4, :].bitcast(I32),
                     scale_rows[row : row + 4, :].bitcast(I32),
                 )
         nc.vector.tensor_copy(x_first[:], x_window[0][:].indirect(offs_t[:]))
@@ -176,7 +177,7 @@ def tile_picked_edgecv_relu_p_kernel(
                 lhsT=codes[m, c, z].bitcast(FP8X4),
                 lhsT_scale=plane[m, c, z],
                 rhs=x_picked[z, half][:, first - half : last - half].bitcast(FP8X4),
-                rhs_scale=scales_picked[4 * z : P, first:last],
+                rhs_scale=scales_picked[z][:, first:last],
                 start=(z == 0),
                 stop=(z == PASSES - 1),
             )
@@ -196,15 +197,14 @@ def tile_picked_edgecv_relu_p_kernel(
         def gather(values, c, lst, first, last):
             nc.vector.tensor_copy(values, rows["e", c][:].indirect(entries(lst, first, last)))
 
-        folded = [placed([P, V], F32, "folded%d" % t, FOLD + 4 * V * t) for t in range(PACK)]
+        folded = placed([P, PACK, V], F32, "folded", FOLD)
 
         def larger(values, one, two, c, first, last):
             nc.vector.tensor_tensor(values, one, two, MAX)
             fold(values, c, first, last)
 
         def fold(values, c, first, last):
-            for t in range(PACK):
-                nc.sync.dma_start(folded[t][QUAD * c : QUAD * (c + 1), first:last], values[t:P:PACK, :])
+            nc.sync.dma_start(folded[QUAD * c : QUAD * (c + 1), :, first:last], values)
 
         first_rounding = new_tile([P, PASSES * K_PASS], BF16, "first_rounding")[:]
 
@@ -297,9 +297,8 @@ def tile_picked_edgecv_relu_p_kernel(
         most = {2: behind_last(0), 3: behind_last(1)}
         nc.vector.tensor_tensor(most[2], one[2][:, :HALF], two[2][:, :HALF], MAX)
         nc.vector.tensor_tensor(most[3], last_one, last_two, MAX)
-        for t in range(PACK):
-            for c in (2, 3):
-                nc.sync.dma_start(folded[t][QUAD * c : QUAD * (c + 1), :HALF], most[c][t:P:PACK, :])
+        for c in (2, 3):
+            fold(most[c], c, 0, HALF)
         quantise_y(1, range(2, 4), round_c)
         end_one, end_two = behind_last(2), behind_last(3)
         gather(end_one, 3, pos1_t, HALF, V)
@@ -309,9 +308,8 @@ def tile_picked_edgecv_relu_p_kernel(
         most = {2: behind_last(4), 3: placed([P, HALF], F32, "most31", LAST + 8192)[:]}
         nc.vector.tensor_tensor(most[2], one[2][:, HALF:], two[2][:, HALF:], MAX)
         nc.vector.tensor_tensor(most[3], end_one, end_two, MAX)
-        for t in range(PACK):
-            for c in (2, 3):
-                nc.sync.dma_start(folded[t][QUAD * c : QUAD * (c + 1), HALF:], most[c][t:P:PACK, :])
+        for c in (2, 3):
+            fold(most[c], c, HALF, V)
 
         z_ready, sums = {}, {}
 
@@ -333,7 +331,7 @@ def tile_picked_edgecv_relu_p_kernel(
                 nc.vector.tensor_tensor(
                     sums[first][:, width * t : width * (t + 1)],
                     rows["y", t][:].indirect(entries(cen_t, first, last)),
-                    folded[t][:, first:last],
+                    folded[:, t, first:last],
                     ADD,
                 )
             z_ready[first] = new_tile([P, PACK * width], BF16, "z%d" % first)

@@ -30,6 +30,7 @@ PER_COLUMN = 16
 HALF = V // 2
 HALVES = (0, BANK, S)
 FIRST_CUTS = (0, BANK, BANK + BANK // 2, S)
+BLOCK = (0, 2, 1, 3)
 PIECES = ((0, 256), (256, 384), (384, 512))
 
 
@@ -72,7 +73,7 @@ def tile_picked_edgecv_relu_p_kernel(
         def load_e(c, passes=range(PASSES)):
             by_pass = raw_e[c].rearrange("p (z j i) -> p z j i", z=PASSES, j=PACK)
             for z in passes:
-                src = w2[K_PASS * z : K_PASS * (z + 1), P * c : P * (c + 1)]
+                src = w2[K_PASS * z : K_PASS * (z + 1), P * BLOCK[c] : P * (BLOCK[c] + 1)]
                 nc.sync.dma_start(by_pass[:, z], src.rearrange("(p j) i -> p j i", j=PACK))
 
 
@@ -83,7 +84,9 @@ def tile_picked_edgecv_relu_p_kernel(
             nc.sync.dma_start(x_window[z][:].bitcast(I32), x_words[z].rearrange("p c t -> p (c t)").bitcast(I32))
 
         scale_window = new_tile([P, T], U8, "xs_win")
-        nc.sync.dma_start(scale_window[:QUAD, :].bitcast(I32), x_scales.rearrange("z q c -> (z q) c").bitcast(I32))
+        by_row = x_scales.rearrange("z (q r) c -> r q z c", r=4)
+        for r in range(4):
+            nc.sync.dma_start(scale_window[r:QUAD:4, :].bitcast(I32), by_row[r].bitcast(I32))
         nc.vector.memset(scale_window[QUAD : 2 * QUAD, :].bitcast(I32), 0)
         nc.vector.memset(scale_window[2 * QUAD :, :].bitcast(I32), 0)
         offs_t = load_list(offs, "offs_t")
@@ -91,8 +94,17 @@ def tile_picked_edgecv_relu_p_kernel(
         load_e(0, range(0, 1))
         load_x(1)
         load_e(0, range(1, 2))
-        load_e(1)
+        scale_rows = new_tile([P, S], U8, "xsr")
+        scales_picked = new_tile([P, S], U8, "xsg")
+        nc.gpsimd.memset(scales_picked[:].bitcast(I32), 0)
+        nc.vector.tensor_copy(scale_rows[:], scale_window[:].indirect(offs_t[:]))
+        for q in range(4):
+            nc.sync.dma_start(
+                scales_picked[QUAD * q : QUAD * q + 8, :].bitcast(I32),
+                scale_rows[8 * q : 8 * q + 8, :].bitcast(I32),
+            )
         pos1_t = load_list(pos1, "pos1_t")
+        load_e(1)
         pos2_t = load_list(pos2, "pos2_t")
         load_e(2)
         nc.sync.dma_start(raw_first, w1[:K_PASS, :].rearrange("(p j) i -> p (j i)", j=PACK))
@@ -114,18 +126,6 @@ def tile_picked_edgecv_relu_p_kernel(
 
         x_picked = {}
         x_first = new_tile([P, S], U32, "xg0")
-        scale_rows = new_tile([P, S], U8, "xsr")
-        scales_picked = [new_tile([P, S], U8, "xsg%d" % z) for z in range(PASSES)]
-        for z in range(PASSES):
-            nc.gpsimd.memset(scales_picked[z][:].bitcast(I32), 0)
-        nc.vector.tensor_copy(scale_rows[:], scale_window[:].indirect(offs_t[:]))
-        for z in range(PASSES):
-            for q in range(4):
-                row = 16 * z + 4 * q
-                nc.scalar.dma_start(
-                    scales_picked[z][QUAD * q : QUAD * q + 4, :].bitcast(I32),
-                    scale_rows[row : row + 4, :].bitcast(I32),
-                )
         nc.vector.tensor_copy(x_first[:], x_window[0][:].indirect(offs_t[:]))
         for half in (0, BANK):
             x_picked[0, half] = x_first[:, half : half + BANK]
@@ -177,7 +177,7 @@ def tile_picked_edgecv_relu_p_kernel(
                 lhsT=codes[m, c, z].bitcast(FP8X4),
                 lhsT_scale=plane[m, c, z],
                 rhs=x_picked[z, half][:, first - half : last - half].bitcast(FP8X4),
-                rhs_scale=scales_picked[z][:, first:last],
+                rhs_scale=scales_picked[4 * z : P, first:last],
                 start=(z == 0),
                 stop=(z == PASSES - 1),
             )
@@ -197,14 +197,15 @@ def tile_picked_edgecv_relu_p_kernel(
         def gather(values, c, lst, first, last):
             nc.vector.tensor_copy(values, rows["e", c][:].indirect(entries(lst, first, last)))
 
-        folded = placed([P, PACK, V], F32, "folded", FOLD)
+        folded = [placed([P, V], F32, "folded%d" % t, FOLD + 4 * V * t) for t in range(PACK)]
 
         def larger(values, one, two, c, first, last):
             nc.vector.tensor_tensor(values, one, two, MAX)
             fold(values, c, first, last)
 
         def fold(values, c, first, last):
-            nc.sync.dma_start(folded[QUAD * c : QUAD * (c + 1), :, first:last], values)
+            for t in range(PACK):
+                nc.sync.dma_start(folded[t][QUAD * BLOCK[c] : QUAD * (BLOCK[c] + 1), first:last], values[t:P:PACK, :])
 
         first_rounding = new_tile([P, PASSES * K_PASS], BF16, "first_rounding")[:]
 
@@ -297,8 +298,9 @@ def tile_picked_edgecv_relu_p_kernel(
         most = {2: behind_last(0), 3: behind_last(1)}
         nc.vector.tensor_tensor(most[2], one[2][:, :HALF], two[2][:, :HALF], MAX)
         nc.vector.tensor_tensor(most[3], last_one, last_two, MAX)
-        for c in (2, 3):
-            fold(most[c], c, 0, HALF)
+        for t in range(PACK):
+            for c in (2, 3):
+                nc.sync.dma_start(folded[t][QUAD * BLOCK[c] : QUAD * (BLOCK[c] + 1), :HALF], most[c][t:P:PACK, :])
         quantise_y(1, range(2, 4), round_c)
         end_one, end_two = behind_last(2), behind_last(3)
         gather(end_one, 3, pos1_t, HALF, V)
@@ -308,8 +310,9 @@ def tile_picked_edgecv_relu_p_kernel(
         most = {2: behind_last(4), 3: placed([P, HALF], F32, "most31", LAST + 8192)[:]}
         nc.vector.tensor_tensor(most[2], one[2][:, HALF:], two[2][:, HALF:], MAX)
         nc.vector.tensor_tensor(most[3], end_one, end_two, MAX)
-        for c in (2, 3):
-            fold(most[c], c, HALF, V)
+        for t in range(PACK):
+            for c in (2, 3):
+                nc.sync.dma_start(folded[t][QUAD * BLOCK[c] : QUAD * (BLOCK[c] + 1), HALF:], most[c][t:P:PACK, :])
 
         z_ready, sums = {}, {}
 
@@ -331,7 +334,7 @@ def tile_picked_edgecv_relu_p_kernel(
                 nc.vector.tensor_tensor(
                     sums[first][:, width * t : width * (t + 1)],
                     rows["y", t][:].indirect(entries(cen_t, first, last)),
-                    folded[:, t, first:last],
+                    folded[t][:, first:last],
                     ADD,
                 )
             z_ready[first] = new_tile([P, PACK * width], BF16, "z%d" % first)

@@ -14,24 +14,21 @@ U8 = mybir.dt.uint8
 FP8X4 = mybir.dt.float8_e4m3fn_x4
 FP4X4 = mybir.dt.float4_e2m1fn_x4
 RELU = mybir.ActivationFunctionType.Relu
+COPY = mybir.ActivationFunctionType.Copy
 MAX = mybir.AluOpType.max
 MULT = mybir.AluOpType.mult
 ADD = mybir.AluOpType.add
-SUBTRACT = mybir.AluOpType.subtract
 
 P = 128
 PACK = 4
 QUAD = 32
 K_PASS = P * PACK
 PASSES = K // K_PASS
-TILES = H // P
 BANK = 512
 PER_COLUMN = 16
-HALF = V // 2
-HALVES = (0, BANK, S)
-FIRST_CUTS = (0, BANK, BANK + BANK // 2, S)
-BLOCK = (0, 2, 1, 3)
-PIECES = ((0, 256), (256, 384), (384, 512))
+QUARTER = V // 4
+RAW_Y = (0, 8192)
+LAST = 16384
 
 
 def tile_picked_edgecv_relu_p_kernel(
@@ -58,30 +55,19 @@ def tile_picked_edgecv_relu_p_kernel(
         def entries(lst, first, last):
             return lst[:, first // PER_COLUMN : last // PER_COLUMN]
 
-        STRIP = 4 * T * PASSES
-        FOLD = STRIP + 8 * T
-        RAW = FOLD + 8 * HALF * 2 * PACK
-        raw_e = [placed([P, PASSES * K_PASS], F32, "raw_e%d" % c, RAW + 7168 * c + 1024)[:] for c in range(TILES)]
-        ROWS = RAW + 7168 * TILES
-        raw_first = placed([P, PACK * H], F32, "raw_first", ROWS)[:]
-        raw_last = placed([P, PACK * H], F32, "raw_last", ROWS + 8 * S)[:]
-        ROUND = ROWS + 19 * S
-
-        def behind_rounding(c, n):
-            return placed([P, V], F32, "behind%d%d" % (c, n), RAW + 7168 * c + (0, 2048, 4608)[n])[:]
-
-        def load_e(c, passes=range(PASSES)):
-            by_pass = raw_e[c].rearrange("p (z j i) -> p z j i", z=PASSES, j=PACK)
-            for z in passes:
-                src = w2[K_PASS * z : K_PASS * (z + 1), P * BLOCK[c] : P * (BLOCK[c] + 1)]
-                nc.sync.dma_start(by_pass[:, z], src.rearrange("(p j) i -> p j i", j=PACK))
-
-
-        x_window = {}
-
         def load_x(z):
-            x_window[z] = placed([P, T], U32, "x_window%d" % z, 4 * T * z)
-            nc.sync.dma_start(x_window[z][:].bitcast(I32), x_words[z].rearrange("p c t -> p (c t)").bitcast(I32))
+            held = new_tile([P, T], U32, "x_window%d" % z)
+            nc.sync.dma_start(held[:].bitcast(I32), x_words[z].rearrange("p c t -> p (c t)").bitcast(I32))
+            return held
+
+        def load_w(w, z, first, last, name, offset=None):
+            if offset is None:
+                held = new_tile([P, PACK * (last - first)], F32, name)[:]
+            else:
+                held = placed([P, PACK * (last - first)], F32, name, offset)[:]
+            src = w[K_PASS * z : K_PASS * (z + 1), first:last].rearrange("(p j) i -> p j i", j=PACK)
+            nc.sync.dma_start(held.rearrange("p (j i) -> p j i", j=PACK), src)
+            return held.rearrange("p (j m t) -> p m j t", j=PACK, t=PACK)
 
         scale_window = new_tile([P, T], U8, "xs_win")
         by_row = x_scales.rearrange("z (q r) c -> r q z c", r=4)
@@ -90,10 +76,9 @@ def tile_picked_edgecv_relu_p_kernel(
         nc.vector.memset(scale_window[QUAD : 2 * QUAD, :].bitcast(I32), 0)
         nc.vector.memset(scale_window[2 * QUAD :, :].bitcast(I32), 0)
         offs_t = load_list(offs, "offs_t")
-        load_x(0)
-        load_e(0, range(0, 1))
-        load_x(1)
-        load_e(0, range(1, 2))
+        x_window = [load_x(0)]
+        raw_e = {(0, 0): load_w(w2, 0, 0, H // 2, "raw_e00")}
+        x_window.append(load_x(1))
         scale_rows = new_tile([P, S], U8, "xsr")
         scales_picked = new_tile([P, S], U8, "xsg")
         nc.gpsimd.memset(scales_picked[:].bitcast(I32), 0)
@@ -103,13 +88,12 @@ def tile_picked_edgecv_relu_p_kernel(
                 scales_picked[QUAD * q : QUAD * q + 8, :].bitcast(I32),
                 scale_rows[8 * q : 8 * q + 8, :].bitcast(I32),
             )
+        raw_e[0, 1] = load_w(w2, 1, 0, H // 2, "raw_e01")
+        raw_e[1, 0] = load_w(w2, 0, H // 2, H, "raw_e10")
         pos1_t = load_list(pos1, "pos1_t")
-        load_e(1)
+        raw_e[1, 1] = load_w(w2, 1, H // 2, H, "raw_e11")
         pos2_t = load_list(pos2, "pos2_t")
-        load_e(2)
-        nc.sync.dma_start(raw_first, w1[:K_PASS, :].rearrange("(p j) i -> p (j i)", j=PACK))
-        load_e(3)
-        nc.sync.dma_start(raw_last, w1[K_PASS:, :].rearrange("(p j) i -> p (j i)", j=PACK))
+        raw_y = [load_w(w1, z, 0, H, "raw_y%d" % z, RAW_Y[z]) for z in range(PASSES)]
         cen_t = load_list(cen, "cen_t")
         w3_codes = new_tile([P, 2 * N], U8, "w3w")
         nc.sync.dma_start(w3_codes[:], w3_words[0])
@@ -124,30 +108,16 @@ def tile_picked_edgecv_relu_p_kernel(
         zero = new_tile([P, 8], F32, "zero")
         nc.scalar.activation(zero[:], below[:], RELU)
 
-        x_picked = {}
-        x_first = new_tile([P, S], U32, "xg0")
-        nc.vector.tensor_copy(x_first[:], x_window[0][:].indirect(offs_t[:]))
-        for half in (0, BANK):
-            x_picked[0, half] = x_first[:, half : half + BANK]
-
-        rounding = new_tile([P, PASSES * K_PASS], BF16, "rounding")[:]
         codes, plane, rows = {}, {}, {}
 
-        def cast_e(dst, src, engine):
-            if engine == "g":
-                nc.gpsimd.tensor_scalar(
-                    dst.rearrange("p (z i j) -> p z i j", i=P, j=PACK),
-                    src.rearrange("p (z j i) -> p z i j", i=P, j=PACK),
-                    1.0,
-                    0.0,
-                    MULT,
-                    ADD,
-                )
+        def round_w(dealt, raw, on_vector):
+            if on_vector:
+                nc.vector.tensor_copy(dealt, raw)
             else:
-                nc.scalar.copy(
-                    dst.rearrange("p (z a b j) -> p z a j b", a=P // 4, b=4, j=PACK),
-                    src.rearrange("p (z j a b) -> p z a j b", a=P // 4, b=4, j=PACK),
-                )
+                nc.scalar.copy(dealt, raw)
+
+        def deal(held, slots):
+            return held.rearrange("p (t m j) -> p m j t", t=slots, j=PACK)
 
         def quantise(words, src, name, scales=None):
             if scales is None:
@@ -155,205 +125,167 @@ def tile_picked_edgecv_relu_p_kernel(
             nc.vector.quantize_mx(out=words.bitcast(FP8X4), scales=scales[:], in_=src)
             return scales[:]
 
-        def quantise_e(c, words, src):
-            scales = quantise(words, src, "e%d" % c)
-            for z in range(PASSES):
-                codes["e", c, z] = words[:, P * z : P * (z + 1)]
-                plane["e", c, z] = scales[:, P * z : P * (z + 1)]
+        def quantise_w(m, z, tiles, src, offset=None):
+            name = "%s%d%d" % (m, z, tiles[0])
+            if offset is None:
+                words = new_tile([P, P * len(tiles)], U32, "codes_" + name)[:]
+            else:
+                words = placed([P, P * len(tiles)], U32, "codes_" + name, offset)[:]
+            scales = quantise(words, src, name)
+            for n, t in enumerate(tiles):
+                codes[m, t, z] = words[:, P * n : P * (n + 1)]
+                plane[m, t, z] = scales[:, P * n : P * (n + 1)]
 
-        def quantise_y(z, slots, src, held=None, held_plane=None):
-            if held is None:
-                held = new_tile([P, P * len(slots)], U32, "codes_y%d%d" % (z, slots.start))
-            words = held[:]
-            scales = quantise(words, src, "y%d%d" % (z, slots.start), held_plane)
-            for n, t in enumerate(slots):
-                codes["y", t, z] = words[:, P * n : P * (n + 1)]
-                plane["y", t, z] = scales[:, P * n : P * (n + 1)]
+        x_picked = {}
 
-        def multiply(m, c, z, b, first, last):
-            half = first // BANK * BANK
+        def multiply(m, t, z, h):
             nc.tensor.matmul_mx(
-                out=banks[b][:, : last - first],
-                lhsT=codes[m, c, z].bitcast(FP8X4),
-                lhsT_scale=plane[m, c, z],
-                rhs=x_picked[z, half][:, first - half : last - half].bitcast(FP8X4),
-                rhs_scale=scales_picked[4 * z : P, first:last],
+                out=banks[2 * t + h][:],
+                lhsT=codes[m, t, z].bitcast(FP8X4),
+                lhsT_scale=plane[m, t, z],
+                rhs=x_picked[z, h].bitcast(FP8X4),
+                rhs_scale=scales_picked[4 * z : P, BANK * h : BANK * (h + 1)],
                 start=(z == 0),
                 stop=(z == PASSES - 1),
             )
 
-        def product(m, c, via):
-            if m == "e" and c >= 2:
-                rows[m, c] = placed([P, S], F32, "rows_e%d" % c, ROWS if c == 2 else ROUND - 3072)
-            elif (m, c) == ("e", 1):
-                rows[m, c] = placed([P, S], F32, "rows_e1", RAW + 7168 * 2 - 2048)
+        def empty(m, t, on_vector=False):
+            if on_vector:
+                rows[m, t] = placed([P, S], F32, "rows_%s%d" % (m, t), RAW_Y[0] + 2048)
             else:
-                rows[m, c] = new_tile([P, S], F32, "rows_%s%d" % (m, c))
-            for b, first, last in zip(via, HALVES, HALVES[1:]):
-                for z in range(PASSES):
-                    multiply(m, c, z, b, first, last)
-                nc.scalar.copy(rows[m, c][:, first:last], banks[b][:, : last - first])
+                rows[m, t] = new_tile([P, S], F32, "rows_%s%d" % (m, t))
+            for h in range(2):
+                dst = rows[m, t][:, BANK * h : BANK * (h + 1)]
+                if on_vector:
+                    nc.vector.tensor_copy(dst, banks[2 * t + h][:])
+                else:
+                    nc.scalar.copy(dst, banks[2 * t + h][:])
 
-        def gather(values, c, lst, first, last):
-            nc.vector.tensor_copy(values, rows["e", c][:].indirect(entries(lst, first, last)))
+        ends = {}
 
-        folded = [placed([P, V], F32, "folded%d" % t, FOLD + 4 * V * t) for t in range(PACK)]
+        def fetch(c, d, on_vector, offset=None, first=0, last=V):
+            name = "end%d%d" % (c, d)
+            if first == 0:
+                ends[c, d] = (new_tile([P, V], F32, name) if offset is None else placed([P, V], F32, name, offset))[:]
+            window = rows["e", c][:].indirect(entries((pos1_t, pos2_t)[d], first, last))
+            if on_vector:
+                nc.vector.tensor_copy(ends[c, d][:, first:last], window)
+            else:
+                nc.scalar.activation(ends[c, d][:, first:last], window, COPY)
 
-        def larger(values, one, two, c, first, last):
-            nc.vector.tensor_tensor(values, one, two, MAX)
-            fold(values, c, first, last)
+        most = {}
+        low, high = slice(0, P // 2), slice(P // 2, P)
 
-        def fold(values, c, first, last):
-            for t in range(PACK):
-                nc.sync.dma_start(folded[t][QUAD * BLOCK[c] : QUAD * (BLOCK[c] + 1), first:last], values[t:P:PACK, :])
-
-        first_rounding = new_tile([P, PASSES * K_PASS], BF16, "first_rounding")[:]
-
-        def quantise_first(z, words):
-            part = slice(K_PASS * z, K_PASS * (z + 1))
-            cast_e(first_rounding[:, part], raw_e[0][:, part], "s")
-            codes["e", 0, z] = words
-            plane["e", 0, z] = quantise(words, first_rounding[:, part], "e0%d" % z)
-
-        quantise_first(0, new_tile([P, P], U32, "codes_e00")[:])
-        rows["e", 0] = new_tile([P, S], F32, "rows_e0")
-        pieces = list(zip((0, 1, 4), FIRST_CUTS, FIRST_CUTS[1:]))
-        for b, first, last in pieces:
-            multiply("e", 0, 0, b, first, last)
-        x_picked[1, 0] = new_tile([P, BANK], U32, "xg1_0")[:]
-        for b, first, last in pieces:
-            half = first // BANK * BANK
-            if first == BANK:
-                quantise_first(1, new_tile([P, P], U32, "codes_e01")[:])
-                x_picked[1, BANK] = placed([P, BANK], U32, "xg1_512", RAW + 4096)[:]
-            nc.vector.tensor_copy(
-                x_picked[1, half][:, first - half : last - half], x_window[1][:].indirect(entries(offs_t, first, last))
-            )
-        for b, first, last in pieces:
-            multiply("e", 0, 1, b, first, last)
-            nc.scalar.copy(rows["e", 0][:, first:last], banks[b][:, : last - first])
-
-        def round_e(c):
-            for z in range(PASSES):
-                part = slice(K_PASS * z, K_PASS * (z + 1))
-                cast_e(rounding[:, part], raw_e[c][:, part], "s" if (c, z) == (2, 0) else "g")
-
-        def dealt(dst):
-            return dst.rearrange("p (t m j) -> p m j t", t=PACK, j=PACK)
-
-        def by_line(src):
-            return src.rearrange("p (j m t) -> p m j t", j=PACK, t=PACK)
-
-        round_b = new_tile([P, 2 * K_PASS], BF16, "round_b")[:]
-        one, two = {}, {}
-        for c in range(3):
-            round_e(c + 1)
+        def larger(c, offset):
+            peak = placed([P, V], F32, "peak%d" % c, offset)[:]
+            nc.vector.tensor_tensor(peak, ends[c, 0], ends[c, 1], MAX)
             if c == 0:
-                for z in range(PASSES):
-                    codes["e", 1, z] = placed([P, P], U32, "codes_e1%d" % z, 4 * T + 4 * P * z)[:]
-                    held = placed([P, P], U8, "plane_e1%d" % z, ROUND + P * z)
-                    plane["e", 1, z] = quantise(codes["e", 1, z], rounding[:, K_PASS * z : K_PASS * (z + 1)], "", held)
+                most[0] = peak
+                most[1] = new_tile([P, V], F32, "most1")[:]
+                nc.sync.dma_start(most[1][low, :], peak[high, :])
+            elif c == 1:
+                nc.sync.dma_start(most[0][high, :], peak[low, :])
+                nc.sync.dma_start(most[1][high, :], peak[high, :])
             else:
-                quantise_e(c + 1, new_tile([P, PASSES * P], U32, "codes_e%d" % (c + 1))[:], rounding)
-            if c == 1:
-                difference = behind_rounding(c + 1, 2)
-                nc.vector.tensor_tensor(difference, rows["e", 0][:].indirect(pos2_t[:]), one[0], SUBTRACT)
-            if c == 2:
-                larger(behind_rounding(c + 1, 2), one[c - 1], two[c - 1], c - 1, 0, V)
-            if c == 2:
-                quantise_y(0, range(0, 4), round_a, None, placed([P, H], U8, "plane_y0", RAW + 7168 * 3 + 4096))
-                nc.scalar.copy(round_b.rearrange("p (t m j) -> p m j t", t=2, j=PACK), by_line(raw_last)[:, :, :, :2])
-            product("e", c + 1, (2, 3) if c % 2 == 0 else (0, 1))
-            if c == 1:
-                excess = placed([P, V], F32, "excess", ROWS + 4 * S)[:]
-                nc.scalar.activation(excess, difference, RELU, bias=zero[:, :1])
-            if c == 0:
-                round_a = placed([P, PACK * H], BF16, "round_a", ROUND)[:]
-                for half in (slice(0, P // 2), slice(P // 2, P)):
-                    nc.scalar.copy(dealt(round_a)[:, half], by_line(raw_first)[:, half])
-            one[c] = new_tile([P, V], F32, "one1")[:] if c == 1 else behind_rounding(c + 1, 0)
-            gather(one[c], c, pos1_t, 0, V)
-            if c > 0:
-                two[c] = behind_rounding(c + 1, 1)
-                gather(two[c], c, pos2_t, 0, V)
-        most_first = placed([P, V], F32, "most_first", ROUND + 1024)[:]
-        nc.gpsimd.tensor_tensor(most_first, one[0], excess, ADD)
-        fold(most_first, 0, 0, V)
+                most[c] = peak
 
-        round_c = placed([P, 2 * K_PASS], BF16, "round_c", ROUND + 3072)[:]
-        nc.scalar.copy(round_c.rearrange("p (t m j) -> p m j t", t=2, j=PACK), by_line(raw_last)[:, :, :, 2:])
+        x_first = new_tile([P, S], U32, "xg0")
+        nc.vector.tensor_copy(x_first[:], x_window[0][:].indirect(offs_t[:]))
+        for h in range(2):
+            x_picked[0, h] = x_first[:, BANK * h : BANK * (h + 1)]
+        whole = [new_tile([P, 2 * K_PASS], BF16, "rounded_whole%d" % z)[:] for z in range(PASSES)]
 
-        LAST = ROWS + 25 * S
-        quantise_y(1, range(0, 2), round_b)
-        product("y", 0, (4, 5))
-        product("y", 1, (6, 7))
+        def round_e(half, z):
+            paired = new_tile([P, K_PASS], BF16, "rounded_e%d%d" % (half, z))[:]
+            round_w(deal(paired, 2), raw_e[half, z][:, :, :, :2], half == 1)
+            round_w(deal(whole[z], 2)[:, (low, high)[half]], raw_e[half, z][:, :, :, 2:], half == 1)
+            quantise_w("e", z, (half,), paired)
 
-        def behind_last(n):
-            return placed([P, HALF], F32, "behind_last%d" % n, ROWS + 8 * S + 4 * HALF * n)[:]
+        round_e(0, 0)
+        for h in range(2):
+            multiply("e", 0, 0, h)
+            x_picked[1, h] = new_tile([P, BANK], U32, "xg1_%d" % h)[:]
+            nc.vector.tensor_copy(x_picked[1, h], x_window[1][:].indirect(entries(offs_t, BANK * h, BANK * (h + 1))))
+        round_e(0, 1)
+        for h in range(2):
+            multiply("e", 0, 1, h)
+        for z in range(PASSES):
+            round_e(1, z)
+            quantise_w("e", z, (2, 3), whole[z])
+        for c, z in ((1, 0), (2, 0), (1, 1), (3, 0), (2, 1), (3, 1)):
+            for h in range(2):
+                multiply("e", c, z, h)
+        empty("e", 0)
+        fetch(0, 0, False)
+        fetch(0, 1, False)
+        empty("e", 1)
+        fetch(1, 0, False)
+        fetch(1, 1, False)
+        empty("e", 3)
+        fetch(3, 0, False)
+        fetch(3, 1, False)
 
-        last_one = new_tile([P, HALF], F32, "last_one")[:]
-        last_two = new_tile([P, HALF], F32, "last_two")[:]
-        gather(last_one, 3, pos1_t, 0, HALF)
-        gather(last_two, 3, pos2_t, 0, HALF)
-        most = {2: behind_last(0), 3: behind_last(1)}
-        nc.vector.tensor_tensor(most[2], one[2][:, :HALF], two[2][:, :HALF], MAX)
-        nc.vector.tensor_tensor(most[3], last_one, last_two, MAX)
+        rounded = [new_tile([P, PACK * H], BF16, "rounded_y0")[:], placed([P, PACK * H], BF16, "rounded_y1", LAST)[:]]
+        round_w(deal(rounded[0], PACK), raw_y[0], True)
+        larger(0, RAW_Y[0])
+        quantise_w("y", 0, (0, 1, 2, 3), rounded[0])
+        empty("e", 2, True)
         for t in range(PACK):
-            for c in (2, 3):
-                nc.sync.dma_start(folded[t][QUAD * BLOCK[c] : QUAD * (BLOCK[c] + 1), :HALF], most[c][t:P:PACK, :])
-        quantise_y(1, range(2, 4), round_c)
-        end_one, end_two = behind_last(2), behind_last(3)
-        gather(end_one, 3, pos1_t, HALF, V)
-        gather(end_two, 3, pos2_t, HALF, V)
-        product("y", 2, (4, 5))
-        product("y", 3, (6, 7))
-        most = {2: behind_last(4), 3: placed([P, HALF], F32, "most31", LAST + 8192)[:]}
-        nc.vector.tensor_tensor(most[2], one[2][:, HALF:], two[2][:, HALF:], MAX)
-        nc.vector.tensor_tensor(most[3], end_one, end_two, MAX)
+            for h in range(2):
+                multiply("y", t, 0, h)
+        round_w(deal(rounded[1], PACK), raw_y[1], True)
+        larger(1, RAW_Y[1])
+        quantise_w("y", 1, (0,), rounded[1][:, :K_PASS])
+        quantise_w("y", 1, (1, 2, 3), rounded[1][:, K_PASS:])
         for t in range(PACK):
-            for c in (2, 3):
-                nc.sync.dma_start(folded[t][QUAD * BLOCK[c] : QUAD * (BLOCK[c] + 1), HALF:], most[c][t:P:PACK, :])
+            for h in range(2):
+                multiply("y", t, 1, h)
+        fetch(2, 0, True, RAW_Y[1] + 2048)
+        fetch(2, 1, True, RAW_Y[1] + 4096)
+        larger(3, LAST)
+        larger(2, RAW_Y[1] + 6144)
+        for t in range(PACK):
+            empty("y", t)
 
-        z_ready, sums = {}, {}
-
-        def relu_on_scalar(first, width, part):
-            nc.scalar.activation(
-                z_ready[first][:].rearrange("p (a b t) -> p a t b", b=4, t=PACK)[:, part],
-                sums[first][:].rearrange("p (t a b) -> p a t b", b=4, t=PACK)[:, part],
-                RELU,
-                bias=zero[:, :1],
-            )
-
-        for first, last in PIECES:
-            width = last - first
-            if last < V:
-                sums[first] = new_tile([P, PACK * width], F32, "sums%d" % first)
-            else:
-                sums[first] = placed([P, PACK * width], F32, "sums%d" % first, LAST + 8192 - 1536)
-            for t in range(PACK):
+        cuts = (0, QUARTER, V)
+        sums = [new_tile([P, PACK * (last - first)], F32, "sums%d" % first)[:] for first, last in zip(cuts, cuts[1:])]
+        for t in range(PACK):
+            for held, first, last in zip(sums, cuts, cuts[1:]):
+                centre = rows["y", t][:].indirect(entries(cen_t, first, last))
+                if t == PACK - 1:
+                    fetched = new_tile([P, last - first], F32, "centre%d" % first)[:]
+                    nc.scalar.activation(fetched, centre, COPY)
+                    centre = fetched
                 nc.vector.tensor_tensor(
-                    sums[first][:, width * t : width * (t + 1)],
-                    rows["y", t][:].indirect(entries(cen_t, first, last)),
-                    folded[t][:, first:last],
+                    held[:, (last - first) * t : (last - first) * (t + 1)],
+                    centre,
+                    most[t][:, first:last],
                     ADD,
                 )
-            z_ready[first] = new_tile([P, PACK * width], BF16, "z%d" % first)
-            relu_on_scalar(first, width, slice(0, width // 4 if last < V else width // 8))
-        for b, (first, last) in enumerate(PIECES):
-            width = last - first
-            if b == 1:
-                end = PIECES[-1][0]
+        pieces = ((0, QUARTER), (2 * QUARTER, 2 * QUARTER), (QUARTER, QUARTER))
+        z_ready = {first: new_tile([P, PACK * width], BF16, "z%d" % first)[:] for first, width in pieces}
+        for first, width in pieces:
+            held, start = (sums[0], 0) if first == 0 else (sums[1], first - QUARTER)
+            if first + width < V:
+                nc.scalar.activation(
+                    z_ready[first].rearrange("p (a b t) -> p a t b", b=4, t=PACK),
+                    held.rearrange("p (t a b) -> p a t b", b=4, t=PACK)[:, start // 4 : (start + width) // 4],
+                    RELU,
+                    bias=zero[:, :1],
+                )
+            else:
                 nc.vector.tensor_scalar(
-                    z_ready[end][:].rearrange("p (v t) -> p v t", t=PACK)[:, P // 2 :],
-                    sums[end][:].rearrange("p (t v) -> p v t", t=PACK)[:, P // 2 :],
+                    z_ready[first].rearrange("p (v t) -> p v t", t=PACK),
+                    held.rearrange("p (t v) -> p v t", t=PACK)[:, start : start + width],
                     0.0,
                     0.0,
                     MAX,
                     ADD,
                 )
+        for b, (first, width) in enumerate(pieces):
             z_codes = new_tile([P, width], U32, "zq%d" % first)[:]
-            held = placed([P, width], U8, "plane_z%d" % first, LAST + 8192 + 512 + first) if last < V else None
-            z_plane = quantise(z_codes, z_ready[first][:], "z%d" % first, held)
+            held = placed([P, width], U8, "plane_z0", LAST) if b == 0 else None
+            z_plane = quantise(z_codes, z_ready[first], "z%d" % first, held)
             nc.tensor.matmul_mx(
                 out=banks[b][:, :width],
                 lhsT=w3_codes[:].bitcast(FP4X4),
@@ -365,4 +297,4 @@ def tile_picked_edgecv_relu_p_kernel(
             )
             result = new_tile([P, width], F32, "result%d" % first)
             nc.scalar.copy(result[:], banks[b][:, :width])
-            nc.sync.dma_start(out[:, first:last], result[:])
+            nc.sync.dma_start(out[:, first : first + width], result[:])

@@ -27,8 +27,10 @@ PASSES = K // K_PASS
 BANK = 512
 PER_COLUMN = 16
 QUARTER = V // 4
-RAW_Y = (0, 8192)
-LAST = 16384
+RAW_E = 0
+ROUNDED = 8192
+RAW_Y = 20480
+ORDER = (2, 3, 0, 1)
 
 
 def tile_picked_edgecv_relu_p_kernel(
@@ -91,9 +93,9 @@ def tile_picked_edgecv_relu_p_kernel(
         raw_e[0, 1] = load_w(w2, 1, 0, H // 2, "raw_e01")
         raw_e[1, 0] = load_w(w2, 0, H // 2, H, "raw_e10")
         pos1_t = load_list(pos1, "pos1_t")
-        raw_e[1, 1] = load_w(w2, 1, H // 2, H, "raw_e11")
+        raw_e[1, 1] = load_w(w2, 1, H // 2, H, "raw_e11", RAW_E)
         pos2_t = load_list(pos2, "pos2_t")
-        raw_y = [load_w(w1, z, 0, H, "raw_y%d" % z, RAW_Y[z]) for z in range(PASSES)]
+        raw_y = [load_w(w1, z, 0, H, "raw_y%d" % z, (None, RAW_Y)[z]) for z in range(PASSES)]
         cen_t = load_list(cen, "cen_t")
         w3_codes = new_tile([P, 2 * N], U8, "w3w")
         nc.sync.dma_start(w3_codes[:], w3_words[0])
@@ -150,10 +152,7 @@ def tile_picked_edgecv_relu_p_kernel(
             )
 
         def empty(m, t, on_vector=False):
-            if on_vector:
-                rows[m, t] = placed([P, S], F32, "rows_%s%d" % (m, t), RAW_Y[0] + 2048)
-            else:
-                rows[m, t] = new_tile([P, S], F32, "rows_%s%d" % (m, t))
+            rows[m, t] = new_tile([P, S], F32, "rows_%s%d" % (m, t))
             for h in range(2):
                 dst = rows[m, t][:, BANK * h : BANK * (h + 1)]
                 if on_vector:
@@ -163,29 +162,26 @@ def tile_picked_edgecv_relu_p_kernel(
 
         ends = {}
 
-        def fetch(c, d, on_vector, offset=None, first=0, last=V):
-            name = "end%d%d" % (c, d)
-            if first == 0:
-                ends[c, d] = (new_tile([P, V], F32, name) if offset is None else placed([P, V], F32, name, offset))[:]
-            window = rows["e", c][:].indirect(entries((pos1_t, pos2_t)[d], first, last))
+        def fetch(c, d, on_vector, held=None):
+            ends[c, d] = new_tile([P, V], F32, "end%d%d" % (c, d))[:] if held is None else held
+            window = rows["e", c][:].indirect((pos1_t, pos2_t)[d][:])
             if on_vector:
-                nc.vector.tensor_copy(ends[c, d][:, first:last], window)
+                nc.vector.tensor_copy(ends[c, d], window)
             else:
-                nc.scalar.activation(ends[c, d][:, first:last], window, COPY)
+                nc.scalar.activation(ends[c, d], window, COPY)
 
         most = {}
         low, high = slice(0, P // 2), slice(P // 2, P)
 
+        for t in range(2):
+            most[t] = placed([P, V], F32, "most%d" % t, 16384 + 2048 * t)[:]
+
         def larger(c, offset):
             peak = placed([P, V], F32, "peak%d" % c, offset)[:]
             nc.vector.tensor_tensor(peak, ends[c, 0], ends[c, 1], MAX)
-            if c == 0:
-                most[0] = peak
-                most[1] = new_tile([P, V], F32, "most1")[:]
-                nc.sync.dma_start(most[1][low, :], peak[high, :])
-            elif c == 1:
-                nc.sync.dma_start(most[0][high, :], peak[low, :])
-                nc.sync.dma_start(most[1][high, :], peak[high, :])
+            if c < 2:
+                for t in range(2):
+                    nc.sync.dma_start(most[t][(low, high)[c], :], peak[(low, high)[t], :])
             else:
                 most[c] = peak
 
@@ -193,7 +189,7 @@ def tile_picked_edgecv_relu_p_kernel(
         nc.vector.tensor_copy(x_first[:], x_window[0][:].indirect(offs_t[:]))
         for h in range(2):
             x_picked[0, h] = x_first[:, BANK * h : BANK * (h + 1)]
-        whole = [new_tile([P, 2 * K_PASS], BF16, "rounded_whole%d" % z)[:] for z in range(PASSES)]
+        whole = [new_tile([P, 2 * K_PASS], BF16, "rounded_whole0")[:], placed([P, 2 * K_PASS], BF16, "rounded_whole1", ROUNDED + 1024)[:]]
 
         def round_e(half, z):
             paired = new_tile([P, K_PASS], BF16, "rounded_e%d%d" % (half, z))[:]
@@ -215,44 +211,52 @@ def tile_picked_edgecv_relu_p_kernel(
         for c, z in ((1, 0), (2, 0), (1, 1), (3, 0), (2, 1), (3, 1)):
             for h in range(2):
                 multiply("e", c, z, h)
+        def round_y(z):
+            held = placed([P, PACK * H], BF16, "rounded_y%d" % z, ROUNDED + 64 * z)[:]
+            nc.gpsimd.tensor_scalar(
+                held.rearrange("p (t m j) -> p m t j", t=PACK, j=PACK),
+                raw_y[z].rearrange("p m j t -> p m t j"),
+                1.0,
+                0.0,
+                MULT,
+                ADD,
+            )
+            return held
+
         empty("e", 0)
         fetch(0, 0, False)
-        fetch(0, 1, False)
+        fetch(0, 1, True, placed([P, V], F32, "end01", RAW_E)[:])
         empty("e", 1)
         fetch(1, 0, False)
         fetch(1, 1, False)
         empty("e", 3)
-        fetch(3, 0, False)
-        fetch(3, 1, False)
-
-        rounded = [new_tile([P, PACK * H], BF16, "rounded_y0")[:], placed([P, PACK * H], BF16, "rounded_y1", LAST)[:]]
-        round_w(deal(rounded[0], PACK), raw_y[0], True)
-        larger(0, RAW_Y[0])
-        quantise_w("y", 0, (0, 1, 2, 3), rounded[0])
         empty("e", 2, True)
-        for t in range(PACK):
+        quantise_w("y", 0, (0, 1, 2, 3), round_y(0))
+        for t in ORDER:
             for h in range(2):
                 multiply("y", t, 0, h)
-        round_w(deal(rounded[1], PACK), raw_y[1], True)
-        larger(1, RAW_Y[1])
-        quantise_w("y", 1, (0,), rounded[1][:, :K_PASS])
-        quantise_w("y", 1, (1, 2, 3), rounded[1][:, K_PASS:])
-        for t in range(PACK):
+        both = placed([P, 2 * V], F32, "ends2", ROUNDED + 64 - 8 * V)[:]
+        fetch(2, 0, True, both[:, :V])
+        fetch(2, 1, True, both[:, V:])
+        fetch(3, 0, False)
+        fetch(3, 1, False)
+        rounded = round_y(1)
+        quantise_w("y", 1, (2, 3), rounded[:, 2 * K_PASS :])
+        quantise_w("y", 1, (0, 1), rounded[:, : 2 * K_PASS])
+        for t in ORDER:
             for h in range(2):
                 multiply("y", t, 1, h)
-        fetch(2, 0, True, RAW_Y[1] + 2048)
-        fetch(2, 1, True, RAW_Y[1] + 4096)
-        larger(3, LAST)
-        larger(2, RAW_Y[1] + 6144)
-        for t in range(PACK):
+        for c in range(PACK):
+            larger(c, RAW_Y + 4 * V * c)
+        for t in ORDER:
             empty("y", t)
 
         cuts = (0, QUARTER, V)
         sums = [new_tile([P, PACK * (last - first)], F32, "sums%d" % first)[:] for first, last in zip(cuts, cuts[1:])]
-        for t in range(PACK):
+        for t in ORDER:
             for held, first, last in zip(sums, cuts, cuts[1:]):
                 centre = rows["y", t][:].indirect(entries(cen_t, first, last))
-                if t == PACK - 1:
+                if t == ORDER[-1] and first > 0:
                     fetched = new_tile([P, last - first], F32, "centre%d" % first)[:]
                     nc.scalar.activation(fetched, centre, COPY)
                     centre = fetched
@@ -284,7 +288,7 @@ def tile_picked_edgecv_relu_p_kernel(
                 )
         for b, (first, width) in enumerate(pieces):
             z_codes = new_tile([P, width], U32, "zq%d" % first)[:]
-            held = placed([P, width], U8, "plane_z0", LAST) if b == 0 else None
+            held = placed([P, width], U8, "plane_z0", 16384 + 2048) if b == 0 else None
             z_plane = quantise(z_codes, z_ready[first], "z%d" % first, held)
             nc.tensor.matmul_mx(
                 out=banks[b][:, :width],

@@ -29,7 +29,8 @@ PER_COLUMN = 16
 QUARTER = V // 4
 RAW_E = 0
 ROUNDED = 8192
-RAW_Y = 20480
+RAW_Y = 28672
+SCALAR_SHARE = 48
 ORDER = (2, 3, 0, 1)
 
 
@@ -213,9 +214,12 @@ def tile_picked_edgecv_relu_p_kernel(
                 multiply("e", c, z, h)
         def round_y(z):
             held = placed([P, PACK * H], BF16, "rounded_y%d" % z, ROUNDED + 64 * z)[:]
+            start = SCALAR_SHARE * z
+            if start:
+                round_w(deal(held, PACK)[:, :start], raw_y[z][:, :start], False)
             nc.gpsimd.tensor_scalar(
-                held.rearrange("p (t m j) -> p m t j", t=PACK, j=PACK),
-                raw_y[z].rearrange("p m j t -> p m t j"),
+                held.rearrange("p (t m j) -> p m t j", t=PACK, j=PACK)[:, start:],
+                raw_y[z].rearrange("p m j t -> p m t j")[:, start:],
                 1.0,
                 0.0,
                 MULT,
@@ -231,23 +235,29 @@ def tile_picked_edgecv_relu_p_kernel(
         fetch(1, 1, False)
         empty("e", 3)
         empty("e", 2, True)
+        fetch(2, 0, True)
         quantise_w("y", 0, (0, 1, 2, 3), round_y(0))
         for t in ORDER:
             for h in range(2):
                 multiply("y", t, 0, h)
-        both = placed([P, 2 * V], F32, "ends2", ROUNDED + 64 - 8 * V)[:]
-        fetch(2, 0, True, both[:, :V])
-        fetch(2, 1, True, both[:, V:])
-        fetch(3, 0, False)
-        fetch(3, 1, False)
+        mine = placed([P, V + V // 2], F32, "end21", ROUNDED + 64 - 6 * V)[:]
+        fetch(2, 1, True, mine[:, :V])
+        nc.vector.tensor_copy(mine[:, V:], rows["e", 3][:].indirect(entries(pos1_t, 0, V // 2)))
         rounded = round_y(1)
+        both = placed([P, V + V // 2], F32, "ends3", RAW_Y + 64 - 6 * V)[:]
+        fetch(3, 1, False, both[:, :V])
+        nc.scalar.activation(both[:, V:], rows["e", 3][:].indirect(entries(pos1_t, V // 2, V)), COPY)
         quantise_w("y", 1, (2, 3), rounded[:, 2 * K_PASS :])
         quantise_w("y", 1, (0, 1), rounded[:, : 2 * K_PASS])
         for t in ORDER:
             for h in range(2):
                 multiply("y", t, 1, h)
-        for c in range(PACK):
-            larger(c, RAW_Y + 4 * V * c)
+        for c in range(PACK - 1):
+            larger(c, RAW_Y + 64 + 4 * V * c)
+        most[3] = new_tile([P, V], F32, "most3")[:]
+        for n, first_end in enumerate((mine[:, V:], both[:, V:])):
+            part = slice(n * V // 2, (n + 1) * V // 2)
+            nc.vector.tensor_tensor(most[3][:, part], first_end, ends[3, 1][:, part], MAX)
         for t in ORDER:
             empty("y", t)
 

@@ -73,9 +73,8 @@ def tile_picked_edgecv_relu_p_kernel(
             return held.rearrange("p (j m t) -> p m j t", j=PACK, t=PACK)
 
         scale_window = new_tile([P, T], U8, "xs_win")
-        by_row = x_scales.rearrange("z (q r) c -> r q z c", r=4)
-        for r in range(4):
-            nc.sync.dma_start(scale_window[r:QUAD:4, :].bitcast(I32), by_row[r].bitcast(I32))
+        for z in range(PASSES):
+            nc.sync.dma_start(scale_window[z:QUAD:PASSES, :].bitcast(I32), x_scales[z].bitcast(I32))
         nc.vector.memset(scale_window[QUAD : 2 * QUAD, :].bitcast(I32), 0)
         nc.vector.memset(scale_window[2 * QUAD :, :].bitcast(I32), 0)
         offs_t = load_list(offs, "offs_t")
@@ -83,12 +82,12 @@ def tile_picked_edgecv_relu_p_kernel(
         raw_e = {(0, 0): load_w(w2, 0, 0, H // 2, "raw_e00")}
         x_window.append(load_x(1))
         scale_rows = new_tile([P, S], U8, "xsr")
-        scales_picked = new_tile([P, S], U8, "xsg")
+        scales_picked = new_tile([P, PASSES * S], U8, "xsg")
         nc.gpsimd.memset(scales_picked[:].bitcast(I32), 0)
         nc.vector.tensor_copy(scale_rows[:], scale_window[:].indirect(offs_t[:]))
         for q in range(4):
             nc.sync.dma_start(
-                scales_picked[QUAD * q : QUAD * q + 8, :].bitcast(I32),
+                scales_picked[QUAD * q : QUAD * q + 4, :].bitcast(I32).rearrange("r (z c) -> r z c", z=PASSES),
                 scale_rows[8 * q : 8 * q + 8, :].bitcast(I32),
             )
         raw_e[0, 1] = load_w(w2, 1, 0, H // 2, "raw_e01")
@@ -147,7 +146,7 @@ def tile_picked_edgecv_relu_p_kernel(
                 lhsT=codes[m, t, z].bitcast(FP8X4),
                 lhsT_scale=plane[m, t, z],
                 rhs=x_picked[z, h].bitcast(FP8X4),
-                rhs_scale=scales_picked[4 * z : P, BANK * h : BANK * (h + 1)],
+                rhs_scale=scales_picked[:, S * z + BANK * h : S * z + BANK * (h + 1)],
                 start=(z == 0),
                 stop=(z == PASSES - 1),
             )
@@ -261,7 +260,7 @@ def tile_picked_edgecv_relu_p_kernel(
         for t in ORDER:
             empty("y", t)
 
-        cuts = (0, QUARTER, V)
+        cuts = (0, V // 2, V)
         sums = [new_tile([P, PACK * (last - first)], F32, "sums%d" % first)[:] for first, last in zip(cuts, cuts[1:])]
         for t in ORDER:
             for held, first, last in zip(sums, cuts, cuts[1:]):
@@ -276,11 +275,11 @@ def tile_picked_edgecv_relu_p_kernel(
                     most[t][:, first:last],
                     ADD,
                 )
-        pieces = ((0, QUARTER), (2 * QUARTER, 2 * QUARTER), (QUARTER, QUARTER))
+        pieces = [(QUARTER * n, QUARTER) for n in (0, 2, 1, 3)]
         z_ready = {first: new_tile([P, PACK * width], BF16, "z%d" % first)[:] for first, width in pieces}
         for first, width in pieces:
-            held, start = (sums[0], 0) if first == 0 else (sums[1], first - QUARTER)
-            if first + width < V:
+            held, start = sums[first // (V // 2)], first % (V // 2)
+            if first < V // 2:
                 nc.scalar.activation(
                     z_ready[first].rearrange("p (a b t) -> p a t b", b=4, t=PACK),
                     held.rearrange("p (t a b) -> p a t b", b=4, t=PACK)[:, start // 4 : (start + width) // 4],
@@ -310,5 +309,8 @@ def tile_picked_edgecv_relu_p_kernel(
                 stop=True,
             )
             result = new_tile([P, width], F32, "result%d" % first)
-            nc.scalar.copy(result[:], banks[b][:, :width])
+            if b == 2:
+                nc.vector.tensor_copy(result[:], banks[b][:, :width])
+            else:
+                nc.scalar.copy(result[:], banks[b][:, :width])
             nc.sync.dma_start(out[:, first : first + width], result[:])

@@ -212,7 +212,7 @@ def tile_picked_edgecv_relu_p_kernel(
             for h in range(2):
                 multiply("e", c, z, h)
         def round_y(z):
-            held = placed([P, PACK * H], BF16, "rounded_y%d" % z, ROUNDED + 64 * z)[:]
+            held = placed([P, PACK * H + (64, 0)[z]], BF16, "rounded_y%d" % z, ROUNDED + 64 * z)[:, : PACK * H]
             start = SCALAR_SHARE * z
             if start:
                 round_w(deal(held, PACK)[:, :start], raw_y[z][:, :start], False)
@@ -230,9 +230,9 @@ def tile_picked_edgecv_relu_p_kernel(
         fetch(0, 0, False)
         fetch(0, 1, True, placed([P, V], F32, "end01", RAW_E)[:])
         empty("e", 1)
+        empty("e", 3)
         fetch(1, 0, False)
         fetch(1, 1, False)
-        empty("e", 3)
         empty("e", 2, True)
         fetch(2, 0, True)
         quantise_w("y", 0, (0, 1, 2, 3), round_y(0))
@@ -243,7 +243,7 @@ def tile_picked_edgecv_relu_p_kernel(
         fetch(2, 1, True, mine[:, :V])
         nc.vector.tensor_copy(mine[:, V:], rows["e", 3][:].indirect(entries(pos1_t, 0, V // 2)))
         rounded = round_y(1)
-        both = placed([P, V + V // 2], F32, "ends3", RAW_Y + 64 - 6 * V)[:]
+        both = placed([P, V + V // 2], F32, "ends3", ROUNDED + 64 + 2 * PACK * H)[:]
         fetch(3, 1, False, both[:, :V])
         nc.scalar.activation(both[:, V:], rows["e", 3][:].indirect(entries(pos1_t, V // 2, V)), COPY)
         quantise_w("y", 1, (2, 3), rounded[:, 2 * K_PASS :])

from contextlib import ExitStack

import concourse.mybir as mybir

K, T, S, V, H, N = 1024, 2048, 1024, 512, 512, 128
FLOPS = 2 * (2 * K * H * S + H * N * V)

F32 = mybir.dt.float32
BF16 = mybir.dt.bfloat16
I32 = mybir.dt.int32
U32 = mybir.dt.uint32
U16 = mybir.dt.uint16
U8 = mybir.dt.uint8
FP8X4 = mybir.dt.float8_e4m3fn_x4
FP4X4 = mybir.dt.float4_e2m1fn_x4
RELU = mybir.ActivationFunctionType.Relu
COPY = mybir.ActivationFunctionType.Copy
MAX = mybir.AluOpType.max
MULT = mybir.AluOpType.mult
ADD = mybir.AluOpType.add

P = 128
PACK = 4
QUAD = 32
K_PASS = P * PACK
PASSES = K // K_PASS
BANK = 512
PER_COLUMN = 16
QUARTER = V // 4
RAW_E = 0
ROUNDED = 8192
RAW_Y = 28672
SCALAR_SHARE = 48
ORDER = (2, 3, 0, 1)


def tile_picked_edgecv_relu_p_kernel(
    tc, x_words, x_scales, w1, w2, w3_words, w3_scales, offs, cen, pos1, pos2, out
):
    nc = tc.nc
    with ExitStack() as ctx:
        keep = ctx.enter_context(tc.tile_pool(name="keep", bufs=1))
        reused = ctx.enter_context(tc.tile_pool(name="reused", bufs=1))
        psum = ctx.enter_context(tc.psum_pool(name="psum", bufs=1))
        banks = [psum.tile([P, BANK], F32, name="bank%d" % b) for b in range(8)]

        def new_tile(shape, dtype, name):
            return keep.tile(shape, dtype, name=name, align_bytes=64)

        def placed(shape, dtype, name, offset):
            return reused.tile(shape, dtype, name=name, align_bytes=64, offset=offset)

        def load_list(src, name):
            held = keep.tile(list(src.shape), U16, name=name)
            nc.sync.dma_start(held[:], src)
            return held

        def entries(lst, first, last):
            return lst[:, first // PER_COLUMN : last // PER_COLUMN]

        def load_x(z):
            held = new_tile([P, T], U32, "x_window%d" % z)
            nc.sync.dma_start(held[:].bitcast(I32), x_words[z].rearrange("p c t -> p (c t)").bitcast(I32))
            return held

        def load_w(w, z, first, last, name, offset=None):
            if offset is None:
                held = new_tile([P, PACK * (last - first)], F32, name)[:]
            else:
                held = placed([P, PACK * (last - first)], F32, name, offset)[:]
            src = w[K_PASS * z : K_PASS * (z + 1), first:last].rearrange("(p j) i -> p j i", j=PACK)
            nc.sync.dma_start(held.rearrange("p (j i) -> p j i", j=PACK), src)
            return held.rearrange("p (j m t) -> p m j t", j=PACK, t=PACK)

        scale_window = new_tile([P, T], U8, "xs_win")
        for z in range(PASSES):
            nc.sync.dma_start(scale_window[z:QUAD:PASSES, :].bitcast(I32), x_scales[z].bitcast(I32))
        nc.vector.memset(scale_window[QUAD : 2 * QUAD, :].bitcast(I32), 0)
        nc.vector.memset(scale_window[2 * QUAD :, :].bitcast(I32), 0)
        offs_t = load_list(offs, "offs_t")
        x_window = [load_x(0)]
        raw_e = {(0, 0): load_w(w2, 0, 0, H // 2, "raw_e00")}
        x_window.append(load_x(1))
        scale_rows = new_tile([P, S], U8, "xsr")
        scales_picked = new_tile([P, PASSES * S], U8, "xsg")
        nc.gpsimd.memset(scales_picked[:].bitcast(I32), 0)
        nc.vector.tensor_copy(scale_rows[:], scale_window[:].indirect(offs_t[:]))
        for q in range(4):
            nc.sync.dma_start(
                scales_picked[QUAD * q : QUAD * q + 4, :].bitcast(I32).rearrange("r (z c) -> r z c", z=PASSES),
                scale_rows[8 * q : 8 * q + 8, :].bitcast(I32),
            )
        raw_e[0, 1] = load_w(w2, 1, 0, H // 2, "raw_e01")
        raw_e[1, 0] = load_w(w2, 0, H // 2, H, "raw_e10")
        pos1_t = load_list(pos1, "pos1_t")
        raw_e[1, 1] = load_w(w2, 1, H // 2, H, "raw_e11", RAW_E)
        pos2_t = load_list(pos2, "pos2_t")
        raw_y = [load_w(w1, z, 0, H, "raw_y%d" % z, (None, RAW_Y)[z]) for z in range(PASSES)]
        cen_t = load_list(cen, "cen_t")
        w3_codes = new_tile([P, 2 * N], U8, "w3w")
        nc.sync.dma_start(w3_codes[:], w3_words[0])
        w3_plane = new_tile([P, N], U8, "w3s")
        nc.gpsimd.memset(w3_plane[:].bitcast(I32), 0)
        for q in range(4):
            nc.sync.dma_start(
                w3_plane[QUAD * q : QUAD * q + 4, :].bitcast(I32), w3_scales[0, 4 * q : 4 * q + 4, :].bitcast(I32)
            )
        below = new_tile([P, 8], F32, "below")
        nc.gpsimd.memset(below[:], 0.0)
        zero = new_tile([P, 8], F32, "zero")
        nc.scalar.activation(zero[:], below[:], RELU)

        codes, plane, rows = {}, {}, {}

        def round_w(dealt, raw, on_vector):
            if on_vector:
                nc.vector.tensor_copy(dealt, raw)
            else:
                nc.scalar.copy(dealt, raw)

        def deal(held, slots):
            return held.rearrange("p (t m j) -> p m j t", t=slots, j=PACK)

        def quantise(words, src, name, scales=None):
            if scales is None:
                scales = new_tile([P, words.shape[1]], U8, "plane_" + name)
            nc.vector.quantize_mx(out=words.bitcast(FP8X4), scales=scales[:], in_=src)
            return scales[:]

        def quantise_w(m, z, tiles, src, offset=None):
            name = "%s%d%d" % (m, z, tiles[0])
            if offset is None:
                words = new_tile([P, P * len(tiles)], U32, "codes_" + name)[:]
            else:
                words = placed([P, P * len(tiles)], U32, "codes_" + name, offset)[:]
            scales = quantise(words, src, name)
            for n, t in enumerate(tiles):
                codes[m, t, z] = words[:, P * n : P * (n + 1)]
                plane[m, t, z] = scales[:, P * n : P * (n + 1)]

        x_picked = {}

        def multiply(m, t, z, h):
            nc.tensor.matmul_mx(
                out=banks[2 * t + h][:],
                lhsT=codes[m, t, z].bitcast(FP8X4),
                lhsT_scale=plane[m, t, z],
                rhs=x_picked[z, h].bitcast(FP8X4),
                rhs_scale=scales_picked[:, S * z + BANK * h : S * z + BANK * (h + 1)],
                start=(z == 0),
                stop=(z == PASSES - 1),
            )

        def empty(m, t, on_vector=False):
            rows[m, t] = new_tile([P, S], F32, "rows_%s%d" % (m, t))
            for h in range(2):
                dst = rows[m, t][:, BANK * h : BANK * (h + 1)]
                if on_vector:
                    nc.vector.tensor_copy(dst, banks[2 * t + h][:])
                else:
                    nc.scalar.copy(dst, banks[2 * t + h][:])

        ends = {}

        def fetch(c, d, on_vector, held=None):
            ends[c, d] = new_tile([P, V], F32, "end%d%d" % (c, d))[:] if held is None else held
            window = rows["e", c][:].indirect((pos1_t, pos2_t)[d][:])
            if on_vector:
                nc.vector.tensor_copy(ends[c, d], window)
            else:
                nc.scalar.activation(ends[c, d], window, COPY)

        most = {}
        low, high = slice(0, P // 2), slice(P // 2, P)

        for t in range(2):
            most[t] = placed([P, V], F32, "most%d" % t, 16384 + 2048 * t)[:]

        def larger(c, offset):
            peak = placed([P, V], F32, "peak%d" % c, offset)[:]
            nc.vector.tensor_tensor(peak, ends[c, 0], ends[c, 1], MAX)
            if c < 2:
                for t in range(2):
                    nc.sync.dma_start(most[t][(low, high)[c], :], peak[(low, high)[t], :])
            else:
                most[c] = peak

        x_first = new_tile([P, S], U32, "xg0")
        nc.vector.tensor_copy(x_first[:], x_window[0][:].indirect(offs_t[:]))
        for h in range(2):
            x_picked[0, h] = x_first[:, BANK * h : BANK * (h + 1)]
        whole = [new_tile([P, 2 * K_PASS], BF16, "rounded_whole0")[:], placed([P, 2 * K_PASS], BF16, "rounded_whole1", ROUNDED + 1024)[:]]

        def round_e(half, z):
            paired = new_tile([P, K_PASS], BF16, "rounded_e%d%d" % (half, z))[:]
            round_w(deal(paired, 2), raw_e[half, z][:, :, :, :2], half == 1)
            round_w(deal(whole[z], 2)[:, (low, high)[half]], raw_e[half, z][:, :, :, 2:], half == 1)
            quantise_w("e", z, (half,), paired)

        round_e(0, 0)
        for h in range(2):
            multiply("e", 0, 0, h)
            x_picked[1, h] = new_tile([P, BANK], U32, "xg1_%d" % h)[:]
            nc.vector.tensor_copy(x_picked[1, h], x_window[1][:].indirect(entries(offs_t, BANK * h, BANK * (h + 1))))
        round_e(0, 1)
        for h in range(2):
            multiply("e", 0, 1, h)
        for z in range(PASSES):
            round_e(1, z)
            quantise_w("e", z, (2, 3), whole[z])
        for c, z in ((1, 0), (2, 0), (1, 1), (3, 0), (2, 1), (3, 1)):
            for h in range(2):
                multiply("e", c, z, h)
        def round_y(z):
            held = placed([P, PACK * H + (64, 0)[z]], BF16, "rounded_y%d" % z, ROUNDED + 64 * z)[:, : PACK * H]
            start = SCALAR_SHARE * z
            if start:
                round_w(deal(held, PACK)[:, :start], raw_y[z][:, :start], False)
            nc.gpsimd.tensor_scalar(
                held.rearrange("p (t m j) -> p m t j", t=PACK, j=PACK)[:, start:],
                raw_y[z].rearrange("p m j t -> p m t j")[:, start:],
                1.0,
                0.0,
                MULT,
                ADD,
            )
            return held

        empty("e", 0)
        fetch(0, 0, False)
        fetch(0, 1, True, placed([P, V], F32, "end01", RAW_E)[:])
        empty("e", 1)
        empty("e", 3)
        fetch(1, 0, False)
        fetch(1, 1, False)
        empty("e", 2, True)
        fetch(2, 0, True)
        quantise_w("y", 0, (0, 1, 2, 3), round_y(0))
        for t in ORDER:
            for h in range(2):
                multiply("y", t, 0, h)
        mine = placed([P, V + V // 2], F32, "end21", ROUNDED + 64 - 6 * V)[:]
        fetch(2, 1, True, mine[:, :V])
        nc.vector.tensor_copy(mine[:, V:], rows["e", 3][:].indirect(entries(pos1_t, 0, V // 2)))
        rounded = round_y(1)
        both = placed([P, V + V // 2], F32, "ends3", ROUNDED + 64 + 2 * PACK * H)[:]
        fetch(3, 1, False, both[:, :V])
        nc.scalar.activation(both[:, V:], rows["e", 3][:].indirect(entries(pos1_t, V // 2, V)), COPY)
        quantise_w("y", 1, (2, 3), rounded[:, 2 * K_PASS :])
        quantise_w("y", 1, (0, 1), rounded[:, : 2 * K_PASS])
        for t in ORDER:
            for h in range(2):
                multiply("y", t, 1, h)
        for c in range(PACK - 1):
            larger(c, RAW_Y + 64 + 4 * V * c)
        most[3] = new_tile([P, V], F32, "most3")[:]
        for n, first_end in enumerate((mine[:, V:], both[:, V:])):
            part = slice(n * V // 2, (n + 1) * V // 2)
            nc.vector.tensor_tensor(most[3][:, part], first_end, ends[3, 1][:, part], MAX)
        for t in ORDER:
            empty("y", t)

        cuts = (0, V // 2, V)
        sums = [new_tile([P, PACK * (last - first)], F32, "sums%d" % first)[:] for first, last in zip(cuts, cuts[1:])]
        for t in ORDER:
            for held, first, last in zip(sums, cuts, cuts[1:]):
                centre = rows["y", t][:].indirect(entries(cen_t, first, last))
                if t == ORDER[-1] and first > 0:
                    fetched = new_tile([P, last - first], F32, "centre%d" % first)[:]
                    nc.scalar.activation(fetched, centre, COPY)
                    centre = fetched
                nc.vector.tensor_tensor(
                    held[:, (last - first) * t : (last - first) * (t + 1)],
                    centre,
                    most[t][:, first:last],
                    ADD,
                )
        pieces = [(QUARTER * n, QUARTER) for n in (0, 2, 1, 3)]
        z_ready = {first: new_tile([P, PACK * width], BF16, "z%d" % first)[:] for first, width in pieces}
        for first, width in pieces:
            held, start = sums[first // (V // 2)], first % (V // 2)
            if first < V // 2:
                nc.scalar.activation(
                    z_ready[first].rearrange("p (a b t) -> p a t b", b=4, t=PACK),
                    held.rearrange("p (t a b) -> p a t b", b=4, t=PACK)[:, start // 4 : (start + width) // 4],
                    RELU,
                    bias=zero[:, :1],
                )
            else:
                nc.vector.tensor_scalar(
                    z_ready[first].rearrange("p (v t) -> p v t", t=PACK),
                    held.rearrange("p (t v) -> p v t", t=PACK)[:, start : start + width],
                    0.0,
                    0.0,
                    MAX,
                    ADD,
                )
        for b, (first, width) in enumerate(pieces):
            z_codes = new_tile([P, width], U32, "zq%d" % first)[:]
            held = placed([P, width], U8, "plane_z0", 16384 + 2048) if b == 0 else None
            z_plane = quantise(z_codes, z_ready[first], "z%d" % first, held)
            nc.tensor.matmul_mx(
                out=banks[b][:, :width],
                lhsT=w3_codes[:].bitcast(FP4X4),
                lhsT_scale=w3_plane[:],
                rhs=z_codes.bitcast(FP8X4),
                rhs_scale=z_plane,
                start=True,
                stop=True,
            )
            result = new_tile([P, width], F32, "result%d" % first)
            if b == 2:
                nc.vector.tensor_copy(result[:], banks[b][:, :width])
            else:
                nc.scalar.copy(result[:], banks[b][:, :width])
            nc.sync.dma_start(out[:, first : first + width], result[:])
